import numpy as np, ml_dtypes
CORES = [8,136,40,168]
N = 4
BF = ml_dtypes.bfloat16
W, L, B, V, S = 4096, 128, 2, 5, 3
def parts(rng):
    x = rng.integers(0, 256, (N, 8, 16, W))
    pool = rng.integers(0, W, (N, 8, 1, B, L, 6)); q = np.take_along_axis(pool, rng.integers(0, 6, (N, 8, 16, B, L, 2)), 5)
    q[..., 1] = np.where(rng.random((N, 8, 16, B, L)) < 0.5, q[..., 1], rng.integers(0, W, (N, 8, 16, B, L)))
    h = rng.integers(0, W, (N, 8, 16, L)); g = rng.integers(0, W, (N, 8, 16, L)); z = rng.integers(0, 256, (N, 8, 16, L))
    t = rng.choice(np.array([750, 900, 1050, 1200]), (N, 8, 1, 1)) + rng.integers(0, 300, (N, 8, 16, 1))
    return x, q, h, g, z, t
def pack(x, q, h, g, z, t):
    c = lambda a, n: np.ascontiguousarray(np.reshape(a, (N, 128, n))).astype(np.int32)
    return {"xt": c(x, W).astype(np.float32).astype(BF), "qs": c(q, 2 * B * L), "hn": c(h, L), "gt": c(g, L), "zs": c(z, L), "th": c(t, 1)}
def setup_inputs(rng):
    return pack(*parts(rng))
def setup_inputs_spread(rng):
    x, q, h, g, z, t = parts(rng); lg = W.bit_length() - 1
    x = np.minimum((np.exp2(8 * rng.random((N, 8, 1, W))) * rng.random((N, 8, 16, W))).astype(np.int64), 255)
    uneven = lambda *s: np.minimum(np.exp2(lg * rng.random(s)).astype(np.int64), W) - 1
    m = rng.random(q.shape) < 0.6; q = np.where(m, uneven(*q.shape), q); h = uneven(*h.shape); g = np.where(rng.random(g.shape) < 0.5, uneven(*g.shape), g)
    z = np.minimum((np.exp2(8 * rng.random((N, 8, 1, L))) * rng.random((N, 8, 16, L))).astype(np.int64), 255)
    t = np.where(rng.random((N, 8, 16, 1)) < 0.5, rng.integers(0, 4081, (N, 8, 16, 1)), rng.integers(200, 1200, (N, 8, 16, 1)))
    return pack(x, q, h, g, z, t)
def setup_inputs_ends(rng):
    two = lambda *s: rng.integers(0, 2, s)
    kind = rng.integers(0, 3, (N, 8, 1, W)); x = 255 * np.where(kind == 2, two(N, 8, 16, W), kind)
    odd = (np.arange(8) & 1)[None, :, None]; x[..., 0] = 255 * odd; x[..., W - 1] = 255 - 255 * odd
    q = (W - 1) * two(N, 8, 16, B, L, 2); h = (W - 1) * two(N, 8, 16, L); g = (W - 1) * two(N, 8, 16, L)
    kind = rng.integers(0, 3, (N, 8, 1, L)); z = 255 * np.where(kind == 2, two(N, 8, 16, L), kind); z[..., 0] = 0; z[..., L - 1] = 255
    t = 4080 * two(N, 8, 16, 1); t[:, 0::2, 0] = 0; t[:, 1::2, 0] = 4080; t[:, :, 2] = 4080; t[:, :, 15] = 4080
    for l in (0, 5, L - 1):
        for k in (2, 15):
            h[:, :, k, l] = W - 1; g[:, :, k, l] = 0; q[:, :, k, :, l] = 0
    return pack(x, q, h, g, z, t)
def setup_inputs_corners(rng):
    x, q, h, g, z, t = parts(rng); off = int(rng.integers(0, 6))
    for r in range(N):
        for a in range(8):
            o = rng.permutation(16); p = (r + a + off) % 6; e = np.zeros(16, np.int64)
            if p == 0: e[:] = 4080
            if p == 2: e[o[1:]] = 4080
            if p == 3: e[o[0]] = 4080
            if p == 4: e[0] = 4080; e[15] = 4080
            if p == 5: e = rng.choice(np.array([0, 1000, 1365, 4080]), 16)
            t[r, a, :, 0] = e
    q[:, :, :, :, 0::4] = 0; h[..., 0::4] = 0; g[..., 0::4] = 0
    q[:, :, :, :, 1::4] = rng.integers(0, W, (N, 8, 1, 1, len(range(1, L, 4)), 1))
    h[..., 2::4] = q[:, :, :, 0, 2::4, 0]; g[..., 2::4] = q[:, :, :, 0, 2::4, 1]
    z[..., 0:2] = 0; z[..., L - 2:] = 255
    return pack(x, q, h, g, z, t)
def setup_inputs_ties(rng):
    x, q, h, g, z, t = parts(rng)
    x = rng.integers(0, 253, (N, 8, 16, 1)) + rng.integers(0, 4, (N, 8, 16, W)) * (rng.random((N, 8, 16, W)) < 0.25)
    t = rng.integers(0, 10, (N, 8, 16, 1))
    return pack(x, q, h, g, z, t)
def setup_inputs_high(rng):
    x, q, h, g, z, t = parts(rng); near = lambda *s: rng.integers(W - 32, W, s)
    gap = rng.choice(np.array([130, 180, 252]), (N, 8, 1, 1))
    x = gap * rng.integers(0, 2, (N, 8, 1, W)) + rng.integers(0, 4, (N, 8, 16, W)) * (rng.random((N, 8, 16, W)) < 0.25)
    t = np.where(rng.random((N, 8, 16, 1)) < 0.25, rng.integers(0, 40, (N, 8, 16, 1)), 16 * gap + rng.integers(-12, 13, (N, 8, 16, 1)))
    d = rng.choice(np.array([3, 5]), (N, 8, 1, L)); one = np.arange(16)[:, None] == rng.integers(0, 16, (N, 8, 1, L))
    z = np.where(rng.random((N, 8, 1, L)) < 0.75, 255 - d * one, rng.integers(250, 256, (N, 8, 16, L)))
    tail = np.where(d == 5, W - 3, W - 5)[:, :, :, None]; name = np.where(d == 5, W - 21, W - 19)[:, :, :, None]
    q[..., 1] = np.where(rng.random((N, 8, 16, B, L)) < 0.75, tail, near(N, 8, 16, B, L))
    q[..., 0] = np.where(rng.random((N, 8, 16, B, L)) < 0.5, name, near(N, 8, 16, B, L))
    ab = np.array([[W - 5, W - 19], [W - 3, W - 21], [W - 19, W - 5], [W - 21, W - 3]])[rng.integers(0, 4, (N, 8, 16, L))]
    m = rng.random((N, 8, 16, L)) < 0.5; h = np.where(m, ab[..., 0], near(N, 8, 16, L)); g = np.where(m, ab[..., 1], near(N, 8, 16, L))
    return pack(x, q, h, g, z, t)
def check_inputs(d):
    bad = []
    for k, lo, hi in (("xt", 0, 255), ("qs", 0, W - 1), ("hn", 0, W - 1), ("gt", 0, W - 1), ("zs", 0, 255), ("th", 0, 4080)):
        v = np.asarray(d[k]).astype(np.float32)
        if not (np.min(v) >= lo and np.max(v) <= hi): bad.append("range of " + k)
        elif np.any(v != np.floor(v)): bad.append("whole numbers in " + k)
    return bad
def rec(x, a, b):
    ix = ((a * b >> 5) + a + 37 * b) & (W - 1)
    return np.take_along_axis(x, ix.reshape(N, 8, 1, 16 * L), 3).reshape(N, 8, 16, 16, L)
def reference(xt, qs, hn, gt, zs, th):
    x0 = xt.astype(np.float32).astype(np.int32).reshape(N, 8, 16, W); q = qs.astype(np.int64).reshape(N, 8, 16, B, L, 2)
    h = hn.astype(np.int64).reshape(N, 8, 16, L); g = gt.astype(np.int64).reshape(N, 8, 16, L); z = zs.astype(np.int64).reshape(N, 8, 16, L)
    lim = th.astype(np.int64).reshape(N, 8, 16, 1); cnt = np.zeros((N, 8, 1, L), np.int64); row = np.arange(16); prev = None
    for v in range(V):
        u = np.add.reduce(z, axis=2)[:, :, None]
        cal = u & (B - 1); rf = np.take_along_axis(q, cal[:, :, :, None, :, None], 3)[:, :, :, 0]
        R = rf[..., 0]; F = rf[..., 1]; x = rec(x0, h, g)
        usek = np.zeros((N, 8, 16, L), bool); usej = np.zeros((N, 8, 16, L), bool); mate = np.zeros((N, 8, 16, L), np.int64); top = np.full((N, 8, 16, L), -1, np.int64)
        for s in range(S):
            j = (row + 5 * s + v) & 15
            y = rec(x0, R[:, :, j], F[:, :, j]); dist = np.add.reduce(np.abs(x - y), axis=2)
            m = (dist < lim + cnt) & ~usek & ~usej[:, :, j]
            top = np.maximum(top, np.max(np.where(m[:, :, None], y, -1), axis=3))
            usek = usek | m; usej[:, :, j] = usej[:, :, j] | m; mate = np.where(m, j[None, None, :, None], mate)
            hit = np.any(m, axis=2)[:, :, None]; low = np.argmax(m, axis=2)[:, :, None]
            old = np.take_along_axis(R[:, :, j], low, 2); new = np.take_along_axis(h, low, 2)
            R = np.where(hit & (R == old), new, R); F = np.where(hit & (F == old), new, F)
        fj = np.take_along_axis(F, mate, 2); g = np.where(usek, ((fj * u >> 5) + fj) & (W - 1), g)
        if v > 0:
            Rb = np.roll(R, -1, axis=0); Fb = np.roll(F, -1, axis=0); ub = np.roll(usej, -1, axis=0)
            for b in range(B):
                put = (prev == b) & ~ub
                q[:, :, :, b, :, 0] = np.where(put, Rb, q[:, :, :, b, :, 0]); q[:, :, :, b, :, 1] = np.where(put, Fb, q[:, :, :, b, :, 1])
        cnt = np.add.reduce(usek.astype(np.int64), axis=2)[:, :, None]; z = np.where(cnt > 0, (z + top) >> 1, z); prev = cal
        if v < V - 1:
            h = np.roll(h, 1, axis=0); g = np.roll(g, 1, axis=0); z = np.roll(z, 1, axis=0); cnt = np.roll(cnt, 1, axis=0)
    return {"yq": q.reshape(N, 128, 2 * B * L).astype(np.float32), "yg": g.reshape(N, 128, L).astype(np.float32), "yz": z.reshape(N, 128, L).astype(np.float32)}

@@ -1,0 +1,534 @@
+from concourse.bass import DstId, RemoteDMATransfer
+from concourse.mybir import AluOpType as A, ActivationFunctionType as AF
+
+NR, W, LN, NV, NS = 4, 4096, 128, 5, 3
+L = 64
+NCH = LN // L
+BIG = 8192.0
+MAGIC = 12582912.0
+HINTS = ("A70:-30 A72:5 A184:-10 A186:29 A190:18 A191:41 A223:49 B1:12 B7:-17 B8:-8 B42:7 B65:-21 B68:-17 B119:-20 "
+         "B171:-9 B172:34 B190:13 B220:26 B222:-16 C90:2 C121:-14 C140:-15 C169:13 C181:14 C182:-5 C223:42 C304:-19 "
+         "D1:-5 D61:14 D69:31 D168:11 D172:6 D175:7 D178:-11 D180:-36 D191:-7 D194:-15 E71:10 E121:4 E140:17 E178:-8 "
+         "E190:-4 E222:42 F7:-11 F121:12 F160:15")
+P = dict(
+    nd=(24, 24, 24),
+    vp=(24, 16),
+    xp=(("s", 16),) * 4,
+    fp=(("s", 16),) * 4,
+    xp0=(("v", 32), ("s", 32)),
+    zsep=True, bias=(3000, 0),
+    prio={("ABCDEF".index(h[0]), 1000 + int(h[1:].split(":")[0])): 100 * int(h.split(":")[1]) for h in HINTS.split()},
+    cyc=1.04, pe=0.52, gat=1.56, sca=3.8, lam=70.0, issue=900.0, fly=2200.0, dma=2200.0,
+)
+
+SIZE = {"bfloat16": 2, "float16": 2, "float32": 4, "int32": 4, "uint16": 2}
+ARENA = {"bfloat16": "ab", "float16": "ah", "float32": "af", "int32": "ai", "uint16": "au"}
+
+
+def build(P):
+    top = {k: 0 for k in ARENA}
+    ops, sems, cur = [], [], [0, 0]
+    cyc, pec = P["cyc"], P["pe"]
+
+    def new(dt, n):
+        al = 32 // SIZE[dt]
+        c = top[dt]
+        top[dt] = c + (n + al - 1) // al * al
+        return (ARENA[dt], c, c + n, 1)
+
+    def sub(v, a, b, st=1):
+        return (v[0], v[1] + a, v[1] + b, st)
+
+    def cnt(v):
+        if v[0] == "ind":
+            return 16 * cnt(v[2])
+        return (v[2] - v[1] + v[3] - 1) // v[3]
+
+    def ps(bank, a, b):
+        return ("ps%d" % bank, a, b, 1)
+
+    def ap(T, v):
+        if not isinstance(v, tuple):
+            return v
+        if v[0] == "ind":
+            return ap(T, v[1]).indirect(ap(T, v[2]))
+        if v[3] == 1:
+            return T[v[0]][:, v[1]:v[2]]
+        return T[v[0]][:, v[1]:v[2]:v[3]]
+
+    def add(eng, fn, rd, wr, cost, **kw):
+        r, w = [], []
+        for v in rd:
+            if isinstance(v, tuple):
+                r += [v[1], v[2]] if v[0] == "ind" else [v]
+        for v in wr:
+            if v[0] == "ind":
+                w.append(v[1]); r.append(v[2])
+            else:
+                w.append(v)
+        ops.append(dict(eng=eng, fn=fn, rd=r, wr=w, cost=cost, ch=cur[0] % 2, cls=cur[0], key=cur[1], **kw))
+        cur[1] += 1
+
+    def vcost(out, in0, k):
+        if in0 and in0[0] == "ind":
+            return 50 + cnt(in0) * P["gat"] * cyc
+        if out[0] == "ind":
+            return 50 + cnt(out) * P["sca"] * cyc
+        return max(64, cnt(out) * k) * cyc
+
+    def half(*vs):
+        return 0.5 if all(v[0] in ("ab", "ah", "au", "tb") for v in vs) else 1
+
+    def ts(out, in0, s1, op0, s2=None, op1=None):
+        def fn(g, T):
+            if op1 is None:
+                return g.vector.tensor_scalar(ap(T, out), ap(T, in0), ap(T, s1), None, op0)
+            return g.vector.tensor_scalar(ap(T, out), ap(T, in0), ap(T, s1), ap(T, s2), op0, op1)
+        add("v", fn, [in0, s1, s2], [out], vcost(out, in0, half(out, in0)))
+
+    def tt(out, in0, in1, op):
+        k = 1 if (in0[0].startswith("ps") or in1[0].startswith("ps")) else 2
+        add("v", lambda g, T: g.vector.tensor_tensor(ap(T, out), ap(T, in0), ap(T, in1), op),
+            [in0, in1], [out], vcost(out, in0, k))
+
+    def cp(out, in_):
+        add("v", lambda g, T: g.vector.tensor_copy(ap(T, out), ap(T, in_)), [in_], [out], vcost(out, in_, half(out, in_)))
+
+    def fill(out, val):
+        add("v", lambda g, T: g.vector.memset(ap(T, out), val), [], [out], vcost(out, None, half(out)))
+
+    def scan(out, d0, d1):
+        add("v", lambda g, T: g.vector.tensor_tensor_scan(ap(T, out), ap(T, d0), ap(T, d1), 0.0, A.min, A.max),
+            [d0, d1], [out], vcost(out, None, 0.5))
+
+    def act(out, in_, func, bias=0.0, scale=1.0):
+        c = 65 + cnt(in_) * P["gat"] * cyc if in_[0] == "ind" else max(64, cnt(out)) * cyc
+        add("s", lambda g, T: g.scalar.activation(ap(T, out), ap(T, in_), func, bias=ap(T, bias), scale=scale),
+            [in_, bias], [out], c)
+
+    def mm(groups, start=True, stop=True):
+        def fn(g, T):
+            last = None
+            for out, terms in groups:
+                for i, term in enumerate(terms):
+                    o = term[2] if len(term) > 2 else out
+                    last = g.tensor.matmul(ap(T, o), ap(T, term[0]), ap(T, term[1]),
+                                           start and i == 0, stop and i == len(terms) - 1)
+            return last
+        c, rd = 0, []
+        for out, terms in groups:
+            for term in terms:
+                c += max(64, cnt(term[1])) * (4 if term[1][0] == "af" else 1) * pec
+                rd += [term[0], term[1]]
+        add("pe", fn, rd, [o for o, _ in groups], c + 30)
+
+    def iota(out, pattern, base, cm):
+        def fn(g, T):
+            if out[0] == "ai":
+                return g.iota(ap(T, out), pattern, base, cm)
+            return g.iota(ap(T, out), pattern, base, cm, allow_small_or_imprecise_dtypes=True)
+        add("g", fn, [], [out], 130 + 2 * cnt(out) * cyc)
+
+    def dma(q, out, in_, rd, wr, lat):
+        sems.append("d%d" % len(sems))
+        eng = {"y": lambda g: g.sync, "s": lambda g: g.scalar}[q]
+        add(q, lambda g, T: eng(g).dma_start(out(T), in_(T)), rd, wr, 60, sem=sems[-1], lat=lat)
+
+    def load(q, dst, name, lat):
+        dma(q, lambda T: ap(T, dst), lambda T: T[name][:], [], [dst], lat)
+
+    def store(q, name, a, b, src):
+        dma(q, lambda T: T[name][:, a:b], lambda T: ap(T, src), [src], [], P["dma"])
+
+    def send(items):
+        sems.append("r%d" % len(sems))
+        add("g", None, [s for s, _, _ in items], [d for _, d, _ in items], P["issue"], sem=sems[-1], items=items,
+            lat=P["fly"] + cnt(items[0][0]) * (4 if items[0][0][0] == "af" else 2) * 128 / 40.0)
+
+    bf, fh, f32, i32, u16 = "bfloat16", "float16", "float32", "int32", "uint16"
+    table, win0 = ("tb", 0, W, 1), ("tb", 0, W + 16, 1)
+    hi, gi, zi, thi, qi = new(i32, LN), new(i32, LN), new(i32, LN), new(i32, 1), new(i32, 4 * LN)
+    load("s", table, "xt", P["dma"] + 3500)
+    load("y", hi, "hn", P["dma"]); load("y", gi, "gt", P["dma"]); load("y", zi, "zs", P["dma"])
+    load("y", qi, "qs", P["dma"] + 300); load("y", thi, "th", P["dma"])
+    row, rowg, rowh = new(bf, 144), new(bf, 128), new(bf, 144)
+    ci, cj, jt_i = new(i32, 16), new(i32, 2), new(i32, L // 8)
+    iota(ci, [[-1, 16]], 16, 1); iota(row, [[1, 144]], 0, 0); iota(cj, [[0, 2]], 0, 1)
+    iota(rowg, [[1, 8], [0, 16]], 0, 0); iota(rowh, [[1, 72], [0, 2]], 0, 0)
+    iota(jt_i, [[16, L // 8]], 0, 1)
+    SP = max(n for _, n in P["fp"])
+    reset = new(bf, 16 * SP)
+    iota(reset, [[0, SP], [256, 16]], 0, 0)
+    ci2, cj2, c16 = new(i32, 16), new(i32, 2), new(f32, 2)
+    ts(ci2, ci, 15, A.bitwise_and); ts(cj2, cj, 112, A.bitwise_and); cp(c16, cj2)
+    g16 = sub(c16, 0, 1)
+    col = new(f32, 16)
+    ts(col, ci2, g16, A.add)
+    cx = new(f32, 3)
+    ts(sub(cx, 0, 1), g16, 1.0 / 16, A.mult); ts(sub(cx, 1, 2), g16, 15.0, A.add)
+    ts(sub(cx, 2, 3), g16, 0.5, A.mult, 7.0, A.add)
+    jt = new(bf, L // 8)
+    ts(jt, jt_i, g16, A.subtract)
+    row128 = sub(row, 0, 128)
+
+    def cmp_mat(src, c, op, scale, dt=bf):
+        m = new(dt, cnt(src))
+        ts(m, src, c, op, scale, A.mult)
+        return m
+
+    def rot(r, scale, dt=bf):
+        return cmp_mat(row128, sub(col, r % 16, r % 16 + 1), A.is_equal, scale, dt)
+    I2080, I3232, I1 = rot(0, 2080.0), rot(0, 3232.0), rot(0, 1.0)
+    B2 = cmp_mat(rowh, sub(cx, 2, 3), A.is_equal, 2.0 * L)
+    ONE = cmp_mat(rowg, sub(cx, 0, 1), A.is_equal, 1.0)
+    Hc0, G0, z0, thc = new(fh, LN), new(fh, LN), new(bf, LN), new(fh, 1)
+    ts(Hc0, hi, 2048.0, A.subtract); ts(G0, gi, 2048.0, A.subtract); cp(z0, zi); ts(thc, thi, 2048.0, A.subtract)
+    qf = []
+    for c in range(NCH):
+        qf.append(new(f32, 4 * L))
+        for b in range(2):
+            cp(sub(qf[c], 2 * L * b, 2 * L * (b + 1)), sub(qi, 2 * (LN * b + L * c), 2 * (LN * b + L * c + L)))
+    Q = [I1] + [rot(-t, 1.0) for t in range(1, NV)]
+    NI, BI = rot(0, -1.0), rot(0, BIG)
+    B1 = cmp_mat(row, sub(cx, 1, 2), A.is_equal, 1.0)
+    LTa = cmp_mat(row128, sub(col, 0, 1), A.is_lt, -2 * BIG)
+    LTb = cmp_mat(row128, g16, A.is_lt, 2 * BIG)
+    NONE = cmp_mat(rowg, sub(cx, 0, 1), A.is_equal, -1.0)
+    R5, R6, R10 = rot(5, 1.0), rot(6, 1.0), rot(10, 1.0)
+    BR = [BI, rot(5, BIG), rot(10, BIG)]
+    NB = [rot(0, -BIG), rot(-5, -BIG), rot(-10, -BIG)]
+    IH, F2 = rot(0, 0.5), rot(0, 2.0, f32)
+    FT = [[Q[1], rot(-1, 2048.0), rot(-1, 32.0)], [rot(NV - 1, 1.0), rot(NV - 1, 2048.0), rot(NV - 1, 32.0)]]
+    k1, ka, kb, khalf = new(bf, L), new(bf, L), new(bf, L), new(bf, L)
+    fill(k1, 1.0); fill(ka, 6144 / BIG); fill(kb, (2048.0 * 6144 + 32 * 2048 - 2 ** 22) / BIG)
+    fill(khalf, -0.5); fill(("tb", W, W + 16, 1), 0.0)
+    bias = new(f32, 2)
+    bU, bX = sub(bias, 0, 1), sub(bias, 1, 2)
+    fill(bU, 32.0 - 2048); fill(bX, 2048.0)
+    Hr, Hl, thb = new(fh, 4 * LN), new(fh, 3 * LN), new(f32, NV)
+    mm([(ps(5, LN * i, LN * (i + 1)), [(Q[i + 1], Hc0)]) for i in range(4)])
+    cp(Hr, ps(5, 0, 4 * LN))
+    send([(sub(Hr, LN * i, LN * (i + 1)), sub(Hl, LN * i, LN * (i + 1)), i + 1) for i in range(3)])
+    H = [Hc0] + [sub(Hl, LN * i, LN * (i + 1)) for i in range(3)] + [sub(Hr, 3 * LN, 4 * LN)]
+    mm([(ps(5, t, t + 1), [(Q[t], thc)]) for t in range(NV)])
+    ts(thb, ps(5, 0, NV), 256.0, A.mult, 256.0 * 2048 - 128, A.add)
+    TR, wtmp = [None] * NV, new(bf, 128)
+
+    def make_tr(t, bank):
+        TR[t] = new(bf, 128)
+        r = ps(bank, 384, 512)
+        mm([(r, [(LTa, Q[t]), (LTb, Q[t]), (BI, Q[t])])])
+        act(wtmp if t else TR[t], r, AF.Copy)
+        if t:
+            mm([(r, [(Q[t], wtmp)])])
+            act(TR[t], r, AF.Copy)
+    make_tr(0, 7)
+
+    def pieces(sz):
+        out, a = [], 0
+        for n in sz:
+            out.append((a, a + n)); a += n
+        return out
+
+    def gather(eng, out, win, off):
+        if eng == "s":
+            act(out, ("ind", win, off), AF.Copy)
+        else:
+            cp(out, ("ind", win, off))
+
+    st = []
+    for c in range(NCH):
+        st.append(dict(
+            x=new(bf, 16 * L), d=[new(bf, 16 * L) for _ in range(NS)], a=[new(bf, 16 * L) for _ in range(NS)],
+            fin=new(bf, 16 * L), sc=new(bf, 16 * L), pr=new(f32, L), s=new(i32, L), px=new(f32, L), sx=new(i32, L),
+            ix=new(i32, L), ux=new(u16, L), idx=new(i32, 3 * L), uy=[new(u16, L) for _ in range(NS)],
+            c1=new(i32, L // 8), c2=new(i32, L // 8), off=[new(u16, L // 8) for _ in range(NV)],
+            rf=[new(fh, 2 * L) for _ in range(NS + 1)], m=new(bf, 3 * L), sel=new(fh, 2 * L), eq=new(bf, 2 * L),
+            t=new(f32, 2 * L), uc=new(f32, L), fp=new(f32, 3 * L), uf=new(u16, L), fs=new(fh, 4 * L), hi=new(bf, 2 * L),
+            p2=new(f32, L), s2=new(i32, L), g2=new(i32, L), zf=new(bf, L), tmp=new(f32, 2 * L),
+            G=sub(G0, L * c, L * c + L), z=sub(z0, L * c, L * c + L), cn=None, X=None))
+
+    def index(a, b, pl, pr, s, ix, ux):
+        mm([(pl, [(I2080, a), (I3232, b)])])
+        tt(pr, a, b, A.mult)
+        tt(s, pr, pl, A.add)
+        ts(ix, s, 5, A.arith_shift_right, W - 1, A.bitwise_and)
+        cp(ux, ix)
+
+    def merge(c, t):
+        S = st[c]
+        w = ("ind", qf[c], S["off"][t - 1])
+        act(S["hi"], S["X"], AF.Relu, scale=-1.0)
+        tt(S["tmp"], w, S["hi"], A.min)
+        tt(w, S["tmp"], S["X"], A.max)
+
+    def visit(c, t):
+        S = st[c]
+        bS, b1, b2, bD = 4 * c, 4 * c + 1, 4 * c + 2, 4 * c + 3
+        lay = dict(d=(bS, 0), u=(bS, 1), cn=(bS, 2), zf=(bS, 3), T=(bS, 4), D=(bD, 0), fid=(bD, 6), z=(bD, 7),
+                   sel=(b1, 0), delta=(b1, 2), rot=(b1, 4), X=(b1, 0), fb=(b1, 2),
+                   diff=(b2, 0), ly=(b2, 2), lx=(b2, 3), ch=(b2, 4), fm=(b2, 5), fa=(b2, 0))
+
+        def pr(name, a=0, b=1):
+            bank, o = lay[name]
+            return ps(bank, int((o + a) * L), int((o + b) * L))
+        Ht, G, z, x, m = sub(H[t], L * c, L * c + L), S["G"], S["z"], S["x"], S["m"]
+        last = t == NV - 1
+        index(Ht, G, pr("lx"), S["px"], S["sx"], S["ix"], S["ux"])
+        xp = P["xp" if t else "xp0"]
+        for (e, _), (a, b) in zip(xp, pieces([n for _, n in xp])):
+            gather(e, sub(x, 16 * a, 16 * b), table, sub(S["ux"], a, b))
+        cur[1] = 1020
+        if c == 0 and not last:
+            make_tr(t + 1, bD)
+        cur[1] = 1030
+        pc = pr("ch", 0, 0.125)
+        mm([(pc, [(I1, jt)] + [(sub(B2, 14 - 2 * a, 142 - 2 * a), sub(z, a, L, 8)) for a in range(8)])])
+        cp(S["c1"], pc); ts(S["c2"], S["c1"], 4 * L - 1, A.bitwise_and); cp(S["off"][t], S["c2"])
+        if t > 1:
+            merge(c, t - 1)
+        cur[1] = 1040
+        ts(S["rf"][0], ("ind", qf[c], S["off"][t]), 2048.0, A.subtract)
+        mm([(pr("u"), [(ONE, z)])])
+        act(S["uc"], pr("u"), AF.Identity, bias=bU)
+        ms = [sub(m, s * L, (s + 1) * L) for s in range(NS)]
+        fp = [sub(S["fp"], s * L, (s + 1) * L) for s in range(NS)]
+        for s in range(NS):
+            rf, idx = S["rf"][s], sub(S["idx"], s * L, (s + 1) * L)
+            cur[1] = 1060 + 50 * s
+            R, F = (sub(rf, 0, 2 * L, 2), sub(rf, 1, 2 * L, 2)) if s == 0 else (sub(rf, 0, L), sub(rf, L, 2 * L))
+            RT = R5 if s < NS - 1 else R6
+            index(R, F, pr("ly"), S["pr"], S["s"], idx, S["uy"][s])
+            d, a_, uy, nd = S["d"][s], S["a"][s], S["uy"][s], P["nd"][s]
+            nv = L - nd
+            ya, pD = sub(d, 16 * nv, 16 * L), pr("D", 0, 16.0 * nd / L)
+            act(ya, ("ind", table, sub(uy, nv, L)), AF.Copy)
+            mm([(pD, [(NI, sub(x, 16 * nv, 16 * L))])], stop=False)
+            mm([(pD, [(I1, ya)])], start=False)
+            act(sub(a_, 16 * nv, 16 * L), pD, AF.Abs)
+            vp = list(P["vp"]); vp[0] += nv - sum(vp)
+            for a, b in pieces(vp):
+                tt(sub(d, 16 * a, 16 * b), ("ind", table, sub(uy, a, b)), sub(x, 16 * a, 16 * b), A.subtract)
+                act(sub(a_, 16 * a, 16 * b), sub(d, 16 * a, 16 * b), AF.Abs)
+            pre = [(NI, S["cn"])] if t else []
+            pre += [(BI, ms[s0]) for s0 in range(s)] + [(BR[s - s0], ms[s0]) for s0 in range(s)]
+            if pre:
+                mm([(pr("d"), pre)], stop=False)
+            mm([(pr("d"), [(sub(B1, 15 - k, 143 - k), sub(a_, k, 16 * L, 16)) for k in range(16)])], start=not pre)
+            act(ms[s], pr("d"), AF.Sigmoid, bias=sub(thb, t, t + 1), scale=-256.0)
+            if s == 0:
+                mm([(pr("rot", 0, 1), [(RT, R)]), (pr("rot", 1, 2), [(RT, F)])])
+            else:
+                mm([(pr("rot", 0, 2), [(RT, rf)])])
+            if s == NS - 1:
+                mm([(pr("fid"), [(NB[0], ms[0]), (NB[0], ms[1]), (F2, fp[0]), (F2, fp[1])])], stop=False)
+                mm([(pr("fm"), [(I1, ms[s])])])
+                tt(fp[s], idx, pr("fm"), A.mult)
+                mm([(pr("fid"), [(NB[0], ms[2]), (F2, fp[2])])], start=False)
+                ts(S["uf"], pr("fid"), 0.5, A.mult, float(W), A.add)
+                for (e, _), (a, b) in zip(P["fp"], pieces([n for _, n in P["fp"]])):
+                    gather(e, sub(S["fin"], 16 * a, 16 * b), win0, sub(S["uf"], a, b))
+                    scan(sub(S["sc"], 16 * a, 16 * b), sub(reset, 0, 16 * (b - a)), sub(S["fin"], 16 * a, 16 * b))
+            cur[1] = 1090 + 50 * s
+            sR, sH = sub(S["sel"], 0, L), sub(S["sel"], L, 2 * L)
+            mm([(pr("sel"), [(I1, R), (TR[t], ms[s])])])
+            mm([(pr("T"), [(I1, Ht), (TR[t], ms[s])])])
+            ts(sR, pr("sel"), BIG, A.subtract, -2048.0, A.max)
+            ts(sH, pr("T"), BIG, A.subtract, -2048.0, A.max)
+            mm([(pr("diff", 0, 1), [(RT, R), (NONE, sR)]), (pr("diff", 1, 2), [(RT, F), (NONE, sR)])])
+            mm([(pr("delta", i, i + 1), [(ONE, sH), (NONE, sR)]) for i in range(2)])
+            ts(S["eq"], pr("diff", 0, 2), 15 * 2048.0, A.is_equal)
+            tt(S["t"], S["eq"], pr("delta", 0, 2), A.mult)
+            tt(S["rf"][s + 1], S["t"], pr("rot", 0, 2), A.add)
+            if s < NS - 1:
+                mm([(pr("fm"), [(I1, ms[s])])])
+                tt(fp[s], idx, pr("fm"), A.mult)
+        cur[1] = 1220
+        R, F = sub(S["rf"][NS], 0, L), sub(S["rf"][NS], L, 2 * L)
+        cn = new(bf, L)
+        mm([(pr("cn"), [(ONE, ms[i]) for i in range(NS)])])
+        act(cn, pr("cn"), AF.Copy)
+        mm([(pr("zf"), [(I1, z), (NB[0], cn)])])
+        act(S["zf"], pr("zf"), AF.Relu)
+        mm([(pr("z"), [(IH, khalf), (IH, z), (IH, S["zf"])])], stop=False)
+        mm([(pr("z"), [(IH, sub(S["sc"], 15, 16 * L, 16))])], start=False)
+        zn = new(f32 if last else bf, L)
+        ts(zn, pr("z"), MAGIC, A.add, MAGIC, A.subtract)
+        fs = S["fs"]
+        fq = [sub(fs, i * L, (i + 1) * L) for i in range(4)]
+        mm([(pr("T", 3, 4), [(I1, G), (BI, k1)] + [(NB[0], ms[i]) for i in range(NS)])])
+        mm([(pr("T", 0, 3), [(BI, m)])], stop=False)
+        mm([(pr("T", 0, 3), [([I1, R5, R10][i], F, pr("T", i, i + 1)) for i in range(NS)])], start=False)
+        ts(fs, pr("T", 0, 4), BIG, A.subtract, -2048.0, A.max)
+        f1, f2048, f32_ = FT[last]
+        mm([(pr("fa"), [(BI, ka)] + [(f1, f) for f in fq[:3]])])
+        cur[1] = 1300
+        if t:
+            xs, S["X"] = new(f32, 2 * L), new(f32, 2 * L)
+            mm([(pr("X", i, i + 1), [(NB[j], ms[j]) for j in range(NS)] + [(I1, (R, F)[i])]) for i in range(2)])
+            for i in range(2):
+                act(sub(xs, i, 2 * L, 2), pr("X", i, i + 1), AF.Identity, bias=bX)
+            send([(xs, S["X"], -1)])
+        cur[1] = 1304
+        mm([(pr("fb"), [(BI, kb)] + [(f2048, f) for f in fq[:3]] + [(f32_, fq[3])])])
+        tt(S["p2"], S["uc"], pr("fa"), A.mult)
+        tt(S["s2"], S["p2"], pr("fb"), A.add)
+        ts(S["g2"], S["s2"], 5, A.arith_shift_right, W - 1, A.bitwise_and)
+        gn = new(f32 if last else fh, L)
+        ts(gn, S["g2"], 0.0 if last else 2048.0, A.subtract)
+        cur[1] = 1312
+        if last:
+            cur[1] = 1320
+            store("y", "yg", L * c, L * c + L, gn); store("y", "yz", L * c, L * c + L, zn)
+            merge(c, t)
+            for b in range(2):
+                store("ys"[b], "yq", 2 * (LN * b + L * c), 2 * (LN * b + L * c + L), sub(qf[c], 2 * L * b, 2 * L * (b + 1)))
+        else:
+            S["G"], S["cn"], S["z"] = new(fh, L), new(bf, L), new(bf, L)
+            if P["zsep"]:
+                send([(gn, S["G"], 1), (cn, S["cn"], 1)]); send([(zn, S["z"], 1)])
+            else:
+                send([(gn, S["G"], 1), (cn, S["cn"], 1), (zn, S["z"], 1)])
+
+    for t in range(NV):
+        for c in range(NCH):
+            cur[0], cur[1] = c + 2 * (0 if 0 < t < NV - 1 else 1 if t == 0 else 2), 1000
+            visit(c, t)
+
+    hist = {}
+    for i, o in enumerate(ops):
+        dep = set()
+        for bank in {v[0] for v in o["rd"] + o["wr"] if v[0].startswith("ps")}:
+            runs = hist.setdefault(bank, [[], []])
+            if runs[1] and ops[runs[1][-1]]["eng"] != o["eng"]:
+                runs[0], runs[1] = runs[1], []
+            dep.update(runs[0])
+            if o["eng"] == "pe":
+                dep.update(runs[1][-1:])
+            runs[1].append(i)
+        acc = [(False, v) for v in o["rd"]] + [(True, v) for v in o["wr"]]
+        acc = [(isw, v) for isw, v in acc if not v[0].startswith("ps")]
+        for isw, v in acc:
+            for (j, w, a, b) in hist.get(v[0], ()):
+                if (w or isw) and a < v[2] and v[1] < b:
+                    dep.add(j)
+        for isw, v in acc:
+            h = hist.setdefault(v[0], [])
+            if isw and v[3] == 1:
+                h[:] = [e for e in h if not (v[1] <= e[2] and e[3] <= v[2])]
+            h.append((i, isw, v[1], v[2]))
+        dep.discard(i)
+        o["dep"] = sorted(dep)
+    return ops, sems, top, ap
+
+
+def schedule(ops, P):
+    n = len(ops)
+    succ = [[] for _ in range(n)]
+    for i, o in enumerate(ops):
+        for j in o["dep"]:
+            succ[j].append(i)
+    lam = P["lam"]
+    rank = [0.0] * n
+    for i in range(n - 1, -1, -1):
+        rank[i] = ops[i]["cost"] + ops[i].get("lat", 0) + lam + max([rank[j] for j in succ[i]], default=0)
+    pri = [rank[i] + P["bias"][o["ch"]] + P["prio"].get((o["cls"], o["key"]), 0) for i, o in enumerate(ops)]
+    left = [len(o["dep"]) for o in ops]
+    ready = [0.0] * n
+    pool = {e: [] for e in ("v", "s", "pe", "g", "y")}
+    for i in range(n):
+        if not left[i]:
+            pool[ops[i]["eng"]].append(i)
+    free = {e: 0.0 for e in pool}
+    order = {e: [] for e in pool}
+    seq = []
+    while len(seq) < n:
+        best = None
+        for e, q in pool.items():
+            if q:
+                t0 = max(free[e], min(ready[i] for i in q))
+                if best is None or t0 < best[0]:
+                    best = (t0, e)
+        t0, e = best
+        i = max((i for i in pool[e] if ready[i] <= t0), key=lambda i: pri[i])
+        pool[e].remove(i); order[e].append(i); seq.append(i)
+        free[e] = t0 + ops[i]["cost"]
+        fin = free[e] + ops[i].get("lat", 0) + lam
+        for j in succ[i]:
+            ready[j] = max(ready[j], fin); left[j] -= 1
+            if not left[j]:
+                pool[ops[j]["eng"]].append(j)
+    return order, seq
+
+
+OPS, DSEMS, TOP, AP = build(P)
+ORDER, SEQ = schedule(OPS, P)
+SCRATCH = {ARENA[k]: ("sbuf", [128, TOP[k]], k) for k in ARENA}
+SCRATCH["tb"] = ("sbuf", [128, W + 16], "bfloat16")
+for _b in range(8):
+    SCRATCH["ps%d" % _b] = ("psum", [128, 512], "float32")
+SEMAPHORES = ["cv", "cs", "cpe", "cg", "sent"] + DSEMS
+
+
+def rank_program(g, core, T, topo):
+    rank = T.rank_of(core)
+    if rank is None:
+        return
+    queue = {"v": g.vector, "s": g.scalar, "pe": g.tensor, "g": g, "y": g.sync}
+    peer = lambda step: T.cores[(rank + step) % NR]
+
+    def split(src, dst, k):
+        eng = topo.engines(src, dst)
+        per = 1
+        while 2 * per * k <= len(eng):
+            per *= 2
+        return [eng[i * per:(i + 1) * per] for i in range(k)]
+
+    mark, total = {}, {}
+    for e, lst in ORDER.items():
+        for i in lst:
+            o = OPS[i]
+            if "items" in o:
+                its = o["items"]
+                mark[i] = (o["sem"], sum(len(split(peer(-s), core, len(its))[k]) for k, (_, _, s) in enumerate(its)))
+            elif "sem" in o:
+                mark[i] = (o["sem"], 16)
+            else:
+                total["c" + e] = total.get("c" + e, 0) + 1
+                mark[i] = ("c" + e, total["c" + e])
+    pos = {i: n for n, i in enumerate(SEQ)}
+    waits, known, seen = {}, {}, {e: {} for e in ORDER}
+    for i in SEQ:
+        o, sn = OPS[i], seen[OPS[i]["eng"]]
+        waits[i] = []
+        for j in sorted(o["dep"], key=lambda j: -pos[j]):
+            s, v = mark[j]
+            if (o["eng"] == "pe" and OPS[j]["eng"] == "pe") or sn.get(s, 0) >= v:
+                continue
+            waits[i].append((s, v)); sn[s] = v
+            for s2, v2 in known[j].items():
+                sn[s2] = max(sn.get(s2, 0), v2)
+        known[i] = {} if "items" in o else dict(sn)
+    sent, waited = 0, set()
+    for e, lst in ORDER.items():
+        q = queue[e]
+        for i in lst:
+            o = OPS[i]
+            for s, v in waits[i]:
+                q.wait_ge(T.sem[s], v); waited.add((s, v))
+            if "items" in o:
+                its, tr = o["items"], []
+                for k, (src, dst, step) in enumerate(its):
+                    d = peer(step)
+                    rid, pid = topo.addr(d, core)
+                    eng = split(core, d, len(its))[k]
+                    tr.append(RemoteDMATransfer(dst_ids=[DstId(rid=rid, pnc=pid)], dma_engine_mask=sum(1 << x for x in eng),
+                                                remote_sem=T.sem[o["sem"]], src=AP(T, src), dst=AP(T, dst)))
+                    sent += len(eng)
+                g.remote_dma_fused(tr, local_sem=T.sem.sent)
+            else:
+                o["fn"](g, T).then_inc(T.sem[mark[i][0]], 16 if "sem" in o else 1)
+    g.wait_ge(T.sem.sent, sent)
+    for s, v in list(total.items()) + [m for i, m in mark.items() if "sem" in OPS[i]]:
+        if (s, v) not in waited:
+            g.wait_ge(T.sem[s], v)

@@ -6,19 +6,18 @@ L = 64
 NCH = LN // L
 BIG = 8192.0
 MAGIC = 12582912.0
-HINTS = ("A70:-30 A72:5 A184:-10 A186:29 A190:18 A191:41 A223:49 B1:12 B7:-17 B8:-8 B42:7 B65:-21 B68:-17 B119:-20 "
-         "B171:-9 B172:34 B190:13 B220:26 B222:-16 C90:2 C121:-14 C140:-15 C169:13 C181:14 C182:-5 C223:42 C304:-19 "
-         "D1:-5 D61:14 D69:31 D168:11 D172:6 D175:7 D178:-11 D180:-36 D191:-7 D194:-15 E71:10 E121:4 E140:17 E178:-8 "
-         "E190:-4 E222:42 F7:-11 F121:12 F160:15")
+HINTS = ("A177:-38 A178:-69 A182:-45 A190:-8 A191:-10 A229:45 B1:57 B2:36 B35:27 B69:-69 B119:-25 B123:-14 B176:-28 "
+         "B177:44 B184:-42 C3:-93 C119:-60 C182:18 C197:-10 C223:11 D61:40 E71:-12 E166:20 E178:-82 E231:-36 "
+         "F145:-48 F160:-5 F190:-15")
 P = dict(
     nd=(24, 24, 24),
     vp=(24, 16),
-    xp=(("s", 16),) * 4,
-    fp=(("s", 16),) * 4,
+    xp=(("s", 32),) * 2,
+    fp=(("s", 32), ("s", 16), ("v", 16)),
     xp0=(("v", 32), ("s", 32)),
-    zsep=True, bias=(3000, 0),
+    zsep=False, bias=(4000, 0),
     prio={("ABCDEF".index(h[0]), 1000 + int(h[1:].split(":")[0])): 100 * int(h.split(":")[1]) for h in HINTS.split()},
-    cyc=1.04, pe=0.52, gat=1.56, sca=3.8, lam=70.0, issue=900.0, fly=2200.0, dma=2200.0,
+    cyc=1.05, pe=.52, gat=1.6, sca=3.8, lam=190, issue=1300, fly=3000, dma=2500,
 )
 
 SIZE = {"bfloat16": 2, "float16": 2, "float32": 4, "int32": 4, "uint16": 2}
@@ -100,6 +99,10 @@ def build(P):
     def scan(out, d0, d1):
         add("v", lambda g, T: g.vector.tensor_tensor_scan(ap(T, out), ap(T, d0), ap(T, d1), 0.0, A.min, A.max),
             [d0, d1], [out], vcost(out, None, 0.5))
+
+    def fma(out, d0, d1):
+        add("v", lambda g, T: g.vector.tensor_tensor_scan(ap(T, out), ap(T, d0), ap(T, d1), 0.0, A.mult, A.add),
+            [d0, d1], [out], vcost(out, None, 1))
 
     def act(out, in_, func, bias=0.0, scale=1.0):
         c = 65 + cnt(in_) * P["gat"] * cyc if in_[0] == "ind" else max(64, cnt(out)) * cyc
@@ -243,10 +246,17 @@ def build(P):
             fin=new(bf, 16 * L), sc=new(bf, 16 * L), pr=new(f32, L), s=new(i32, L), px=new(f32, L), sx=new(i32, L),
             ix=new(i32, L), ux=new(u16, L), idx=new(i32, 3 * L), uy=[new(u16, L) for _ in range(NS)],
             c1=new(i32, L // 8), c2=new(i32, L // 8), off=[new(u16, L // 8) for _ in range(NV)],
-            rf=[new(fh, 2 * L) for _ in range(NS + 1)], m=new(bf, 3 * L), sel=new(fh, 2 * L), eq=new(bf, 2 * L),
-            t=new(f32, 2 * L), uc=new(f32, L), fp=new(f32, 3 * L), uf=new(u16, L), fs=new(fh, 4 * L), hi=new(bf, 2 * L),
-            p2=new(f32, L), s2=new(i32, L), g2=new(i32, L), zf=new(bf, L), tmp=new(f32, 2 * L),
+            rf=[new(fh, 4 * L) for _ in range(NS + 1)], m=new(bf, 3 * L), sel=new(fh, 2 * L), eq=new(bf, 4 * L),
+            uc=new(f32, 2 * L), fp=new(f32, 3 * L), uf=new(u16, L), fs=new(fh, 4 * L), hi=new(bf, 2 * L),
+            s2=new(i32, 2 * L), g2=new(i32, L), zf=new(bf, L), tmp=new(f32, 2 * L),
             G=sub(G0, L * c, L * c + L), z=sub(z0, L * c, L * c + L), cn=None, X=None))
+    for S in st:
+        fill(S["eq"], 0.0); fill(S["uc"], 0.0)
+
+    def names_tails(rf, s):
+        if s == 0:
+            return sub(rf, 0, 2 * L, 2), sub(rf, 1, 2 * L, 2)
+        return sub(rf, 1, 2 * L, 2), sub(rf, 2 * L + 1, 4 * L, 2)
 
     def index(a, b, pl, pr, s, ix, ux):
         mm([(pl, [(I2080, a), (I3232, b)])])
@@ -266,7 +276,7 @@ def build(P):
         S = st[c]
         bS, b1, b2, bD = 4 * c, 4 * c + 1, 4 * c + 2, 4 * c + 3
         lay = dict(d=(bS, 0), u=(bS, 1), cn=(bS, 2), zf=(bS, 3), T=(bS, 4), D=(bD, 0), fid=(bD, 6), z=(bD, 7),
-                   sel=(b1, 0), delta=(b1, 2), rot=(b1, 4), X=(b1, 0), fb=(b1, 2),
+                   sel=(b1, 0), delta=(b1, 2), X=(b1, 0),
                    diff=(b2, 0), ly=(b2, 2), lx=(b2, 3), ch=(b2, 4), fm=(b2, 5), fa=(b2, 0))
 
         def pr(name, a=0, b=1):
@@ -288,15 +298,15 @@ def build(P):
         if t > 1:
             merge(c, t - 1)
         cur[1] = 1040
-        ts(S["rf"][0], ("ind", qf[c], S["off"][t]), 2048.0, A.subtract)
+        ts(sub(S["rf"][0], 0, 2 * L), ("ind", qf[c], S["off"][t]), 2048.0, A.subtract)
         mm([(pr("u"), [(ONE, z)])])
-        act(S["uc"], pr("u"), AF.Identity, bias=bU)
+        act(sub(S["uc"], 1, 2 * L, 2), pr("u"), AF.Identity, bias=bU)
         ms = [sub(m, s * L, (s + 1) * L) for s in range(NS)]
         fp = [sub(S["fp"], s * L, (s + 1) * L) for s in range(NS)]
         for s in range(NS):
             rf, idx = S["rf"][s], sub(S["idx"], s * L, (s + 1) * L)
             cur[1] = 1060 + 50 * s
-            R, F = (sub(rf, 0, 2 * L, 2), sub(rf, 1, 2 * L, 2)) if s == 0 else (sub(rf, 0, L), sub(rf, L, 2 * L))
+            R, F = names_tails(rf, s)
             RT = R5 if s < NS - 1 else R6
             index(R, F, pr("ly"), S["pr"], S["s"], idx, S["uy"][s])
             d, a_, uy, nd = S["d"][s], S["a"][s], S["uy"][s], P["nd"][s]
@@ -316,10 +326,8 @@ def build(P):
                 mm([(pr("d"), pre)], stop=False)
             mm([(pr("d"), [(sub(B1, 15 - k, 143 - k), sub(a_, k, 16 * L, 16)) for k in range(16)])], start=not pre)
             act(ms[s], pr("d"), AF.Sigmoid, bias=sub(thb, t, t + 1), scale=-256.0)
-            if s == 0:
-                mm([(pr("rot", 0, 1), [(RT, R)]), (pr("rot", 1, 2), [(RT, F)])])
-            else:
-                mm([(pr("rot", 0, 2), [(RT, rf)])])
+            dr = pr("delta", 0, 4)
+            mm([(sub(dr, 2 * L * i + 1, 2 * L * (i + 1), 2), [(RT, (R, F)[i])]) for i in range(2)])
             if s == NS - 1:
                 mm([(pr("fid"), [(NB[0], ms[0]), (NB[0], ms[1]), (F2, fp[0]), (F2, fp[1])])], stop=False)
                 mm([(pr("fm"), [(I1, ms[s])])])
@@ -336,15 +344,15 @@ def build(P):
             ts(sR, pr("sel"), BIG, A.subtract, -2048.0, A.max)
             ts(sH, pr("T"), BIG, A.subtract, -2048.0, A.max)
             mm([(pr("diff", 0, 1), [(RT, R), (NONE, sR)]), (pr("diff", 1, 2), [(RT, F), (NONE, sR)])])
-            mm([(pr("delta", i, i + 1), [(ONE, sH), (NONE, sR)]) for i in range(2)])
-            ts(S["eq"], pr("diff", 0, 2), 15 * 2048.0, A.is_equal)
-            tt(S["t"], S["eq"], pr("delta", 0, 2), A.mult)
-            tt(S["rf"][s + 1], S["t"], pr("rot", 0, 2), A.add)
+            mm([(sub(dr, 2 * L * i, 2 * L * (i + 1), 2), [(ONE, sH), (NONE, sR)]) for i in range(2)])
+            ts(sub(S["eq"], 1, 4 * L, 2), pr("diff", 0, 2), 15 * 2048.0, A.is_equal)
+            fma(S["rf"][s + 1], S["eq"], dr)
+            cur[1] += 1
             if s < NS - 1:
                 mm([(pr("fm"), [(I1, ms[s])])])
                 tt(fp[s], idx, pr("fm"), A.mult)
         cur[1] = 1220
-        R, F = sub(S["rf"][NS], 0, L), sub(S["rf"][NS], L, 2 * L)
+        R, F = names_tails(S["rf"][NS], NS)
         cn = new(bf, L)
         mm([(pr("cn"), [(ONE, ms[i]) for i in range(NS)])])
         act(cn, pr("cn"), AF.Copy)
@@ -361,7 +369,8 @@ def build(P):
         mm([(pr("T", 0, 3), [([I1, R5, R10][i], F, pr("T", i, i + 1)) for i in range(NS)])], start=False)
         ts(fs, pr("T", 0, 4), BIG, A.subtract, -2048.0, A.max)
         f1, f2048, f32_ = FT[last]
-        mm([(pr("fa"), [(BI, ka)] + [(f1, f) for f in fq[:3]])])
+        fab = pr("fa", 0, 2)
+        mm([(sub(fab, 0, 2 * L, 2), [(BI, ka)] + [(f1, f) for f in fq[:3]])])
         cur[1] = 1300
         if t:
             xs, S["X"] = new(f32, 2 * L), new(f32, 2 * L)
@@ -370,10 +379,10 @@ def build(P):
                 act(sub(xs, i, 2 * L, 2), pr("X", i, i + 1), AF.Identity, bias=bX)
             send([(xs, S["X"], -1)])
         cur[1] = 1304
-        mm([(pr("fb"), [(BI, kb)] + [(f2048, f) for f in fq[:3]] + [(f32_, fq[3])])])
-        tt(S["p2"], S["uc"], pr("fa"), A.mult)
-        tt(S["s2"], S["p2"], pr("fb"), A.add)
-        ts(S["g2"], S["s2"], 5, A.arith_shift_right, W - 1, A.bitwise_and)
+        mm([(sub(fab, 1, 2 * L, 2), [(BI, kb)] + [(f2048, f) for f in fq[:3]] + [(f32_, fq[3])])])
+        fma(S["s2"], S["uc"], fab)
+        cur[1] += 1
+        ts(S["g2"], sub(S["s2"], 1, 2 * L, 2), 5, A.arith_shift_right, W - 1, A.bitwise_and)
         gn = new(f32 if last else fh, L)
         ts(gn, S["g2"], 0.0 if last else 2048.0, A.subtract)
         cur[1] = 1312

@@ -4,29 +4,38 @@ from concourse.mybir import AluOpType as A, ActivationFunctionType as AF
 NR, W, LN, NV, NS = 4, 4096, 128, 5, 3
 L = 64
 NCH = LN // L
+BLK = 128 // NR
 BIG = 8192.0
-MAGIC = 12582912.0
-HINTS = ("A177:-38 A178:-69 A182:-45 A190:-8 A191:-10 A229:45 B1:57 B2:36 B35:27 B69:-69 B119:-25 B123:-14 B176:-28 "
-         "B177:44 B184:-42 C3:-93 C119:-60 C182:18 C197:-10 C223:11 D61:40 E71:-12 E166:20 E178:-82 E231:-36 "
-         "F145:-48 F160:-5 F190:-15")
 P = dict(
     nd=(24, 24, 24),
-    vp=(24, 16),
+    vp=(16, 16, 8),
     xp=(("s", 32),) * 2,
-    fp=(("s", 32), ("s", 16), ("v", 16)),
+    fp=(("s", 24), ("v", 16), ("s", 24)),
     xp0=(("v", 32), ("s", 32)),
-    zsep=False, bias=(4000, 0),
-    prio={("ABCDEF".index(h[0]), 1000 + int(h[1:].split(":")[0])): 100 * int(h.split(":")[1]) for h in HINTS.split()},
-    cyc=1.05, pe=.52, gat=1.6, sca=3.8, lam=190, issue=1300, fly=3000, dma=2500,
+    bias=(2500, 0), tries=60, look=250, gam=3.0, fit=30,
+    cyc=0.9, pe=.45, gat=1.56, lam=190, issue=1300, fly=3000, dma=2500, rate=30.0,
 )
 
 SIZE = {"bfloat16": 2, "float16": 2, "float32": 4, "int32": 4, "uint16": 2}
 ARENA = {"bfloat16": "ab", "float16": "ah", "float32": "af", "int32": "ai", "uint16": "au"}
 
 
+def ap(T, v, r):
+    if not isinstance(v, tuple):
+        return v
+    if v[0] == "ind":
+        return ap(T, v[1], r).indirect(ap(T, v[2], r))
+    if len(v) == 5:
+        a = v[1] + v[4](r)
+        return T[v[0]][:, a:a + 128]
+    if v[3] == 1:
+        return T[v[0]][:, v[1]:v[2]]
+    return T[v[0]][:, v[1]:v[2]:v[3]]
+
+
 def build(P):
     top = {k: 0 for k in ARENA}
-    ops, sems, cur = [], [], [0, 0]
+    ops, sems, cur = [], [], [0]
     cyc, pec = P["cyc"], P["pe"]
 
     def new(dt, n):
@@ -46,186 +55,247 @@ def build(P):
     def ps(bank, a, b):
         return ("ps%d" % bank, a, b, 1)
 
-    def ap(T, v):
-        if not isinstance(v, tuple):
-            return v
-        if v[0] == "ind":
-            return ap(T, v[1]).indirect(ap(T, v[2]))
-        if v[3] == 1:
-            return T[v[0]][:, v[1]:v[2]]
-        return T[v[0]][:, v[1]:v[2]:v[3]]
+    def part(s):
+        return ("t2part%d" % s, 0, 1, 1)
 
     def add(eng, fn, rd, wr, cost, **kw):
-        r, w = [], []
+        r = []
         for v in rd:
             if isinstance(v, tuple):
                 r += [v[1], v[2]] if v[0] == "ind" else [v]
-        for v in wr:
-            if v[0] == "ind":
-                w.append(v[1]); r.append(v[2])
-            else:
-                w.append(v)
-        ops.append(dict(eng=eng, fn=fn, rd=r, wr=w, cost=cost, ch=cur[0] % 2, cls=cur[0], key=cur[1], **kw))
-        cur[1] += 1
+                if v[0] == "ind" and v[1][0] == "t2":
+                    r += [part(s) for s in range(NR)]
+        ops.append(dict(eng=eng, fn=fn, rd=r, wr=list(wr), cost=cost, ch=cur[0], **kw))
+        return len(ops) - 1
 
     def vcost(out, in0, k):
         if in0 and in0[0] == "ind":
             return 50 + cnt(in0) * P["gat"] * cyc
-        if out[0] == "ind":
-            return 50 + cnt(out) * P["sca"] * cyc
         return max(64, cnt(out) * k) * cyc
 
     def half(*vs):
-        return 0.5 if all(v[0] in ("ab", "ah", "au", "tb") for v in vs) else 1
+        return 0.5 if all(v[0] in ("ab", "ah", "au", "tb", "t2") for v in vs) else 1
 
     def ts(out, in0, s1, op0, s2=None, op1=None):
-        def fn(g, T):
+        def fn(g, T, r):
             if op1 is None:
-                return g.vector.tensor_scalar(ap(T, out), ap(T, in0), ap(T, s1), None, op0)
-            return g.vector.tensor_scalar(ap(T, out), ap(T, in0), ap(T, s1), ap(T, s2), op0, op1)
-        add("v", fn, [in0, s1, s2], [out], vcost(out, in0, half(out, in0)))
+                return g.vector.tensor_scalar(ap(T, out, r), ap(T, in0, r), ap(T, s1, r), None, op0)
+            return g.vector.tensor_scalar(ap(T, out, r), ap(T, in0, r), ap(T, s1, r), ap(T, s2, r), op0, op1)
+        return add("v", fn, [in0, s1, s2], [out], vcost(out, in0, half(out, in0)))
 
     def tt(out, in0, in1, op):
         k = 1 if (in0[0].startswith("ps") or in1[0].startswith("ps")) else 2
-        add("v", lambda g, T: g.vector.tensor_tensor(ap(T, out), ap(T, in0), ap(T, in1), op),
-            [in0, in1], [out], vcost(out, in0, k))
+        return add("v", lambda g, T, r: g.vector.tensor_tensor(ap(T, out, r), ap(T, in0, r), ap(T, in1, r), op),
+                   [in0, in1], [out], vcost(out, in0, k))
 
     def cp(out, in_):
-        add("v", lambda g, T: g.vector.tensor_copy(ap(T, out), ap(T, in_)), [in_], [out], vcost(out, in_, half(out, in_)))
+        return add("v", lambda g, T, r: g.vector.tensor_copy(ap(T, out, r), ap(T, in_, r)), [in_], [out],
+                   vcost(out, in_, half(out, in_)))
 
     def fill(out, val):
-        add("v", lambda g, T: g.vector.memset(ap(T, out), val), [], [out], vcost(out, None, half(out)))
+        return add("v", lambda g, T, r: g.vector.memset(ap(T, out, r), val), [], [out], vcost(out, None, half(out)))
 
-    def scan(out, d0, d1):
-        add("v", lambda g, T: g.vector.tensor_tensor_scan(ap(T, out), ap(T, d0), ap(T, d1), 0.0, A.min, A.max),
-            [d0, d1], [out], vcost(out, None, 0.5))
+    def scan(out, d0, d1, op0, op1):
+        return add("v", lambda g, T, r: g.vector.tensor_tensor_scan(ap(T, out, r), ap(T, d0, r), ap(T, d1, r), 0.0, op0, op1),
+                   [d0, d1], [out], vcost(out, None, half(out, d0, d1)))
 
     def fma(out, d0, d1):
-        add("v", lambda g, T: g.vector.tensor_tensor_scan(ap(T, out), ap(T, d0), ap(T, d1), 0.0, A.mult, A.add),
-            [d0, d1], [out], vcost(out, None, 1))
+        return scan(out, d0, d1, A.mult, A.add)
 
     def act(out, in_, func, bias=0.0, scale=1.0):
         c = 65 + cnt(in_) * P["gat"] * cyc if in_[0] == "ind" else max(64, cnt(out)) * cyc
-        add("s", lambda g, T: g.scalar.activation(ap(T, out), ap(T, in_), func, bias=ap(T, bias), scale=scale),
-            [in_, bias], [out], c)
+        return add("s", lambda g, T, r: g.scalar.activation(ap(T, out, r), ap(T, in_, r), func, bias=ap(T, bias, r), scale=scale),
+                   [in_, bias], [out], c)
 
-    def mm(groups, start=True, stop=True):
-        def fn(g, T):
+    def mm(terms, start=True, stop=True, after=()):
+        def fn(g, T, r):
             last = None
-            for out, terms in groups:
-                for i, term in enumerate(terms):
-                    o = term[2] if len(term) > 2 else out
-                    last = g.tensor.matmul(ap(T, o), ap(T, term[0]), ap(T, term[1]),
-                                           start and i == 0, stop and i == len(terms) - 1)
+            for i, (o, lhs, rhs) in enumerate(terms):
+                last = g.tensor.matmul(ap(T, o, r), ap(T, lhs, r), ap(T, rhs, r),
+                                       start and i == 0, stop and i == len(terms) - 1)
             return last
-        c, rd = 0, []
-        for out, terms in groups:
-            for term in terms:
-                c += max(64, cnt(term[1])) * (4 if term[1][0] == "af" else 1) * pec
-                rd += [term[0], term[1]]
-        add("pe", fn, rd, [o for o, _ in groups], c + 30)
+        c, rd = 30, []
+        for o, lhs, rhs in terms:
+            c += max(64, cnt(rhs)) * (4 if rhs[0] == "af" else 1) * pec
+            rd += [lhs, rhs]
+        tok = ("open" + terms[0][0][0], 0, 1, 1)
+        return add("pe", fn, rd + ([] if start else [tok]), [o for o, _, _ in terms] + ([] if stop else [tok]), c,
+                   start=start, stop=stop, bank=terms[0][0][0], after=after)
 
     def iota(out, pattern, base, cm):
-        def fn(g, T):
+        def fn(g, T, r):
             if out[0] == "ai":
-                return g.iota(ap(T, out), pattern, base, cm)
-            return g.iota(ap(T, out), pattern, base, cm, allow_small_or_imprecise_dtypes=True)
-        add("g", fn, [], [out], 130 + 2 * cnt(out) * cyc)
+                return g.iota(ap(T, out, r), pattern, base, cm)
+            return g.iota(ap(T, out, r), pattern, base, cm, allow_small_or_imprecise_dtypes=True)
+        return add("g", fn, [], [out], 130 + 2 * cnt(out) * cyc)
 
-    def dma(q, out, in_, rd, wr, lat):
+    def dma(q, out, in_, rd, wr, lat, after=()):
         sems.append("d%d" % len(sems))
         eng = {"y": lambda g: g.sync, "s": lambda g: g.scalar}[q]
-        add(q, lambda g, T: eng(g).dma_start(out(T), in_(T)), rd, wr, 60, sem=sems[-1], lat=lat)
+        return add(q, lambda g, T, r: eng(g).dma_start(out(T, r), in_(T, r)), rd, wr, 60, sem=sems[-1], lat=lat, after=after)
 
     def load(q, dst, name, lat):
-        dma(q, lambda T: ap(T, dst), lambda T: T[name][:], [], [dst], lat)
+        return dma(q, lambda T, r: ap(T, dst, r), lambda T, r: T[name][:], [], [dst], lat)
 
     def store(q, name, a, b, src):
-        dma(q, lambda T: T[name][:, a:b], lambda T: ap(T, src), [src], [], P["dma"])
+        return dma(q, lambda T, r: T[name][:, a:b], lambda T, r: ap(T, src, r), [src], [], P["dma"])
 
-    def send(items):
+    def send(items, rd, wr, nbytes):
         sems.append("r%d" % len(sems))
-        add("g", None, [s for s, _, _ in items], [d for _, d, _ in items], P["issue"], sem=sems[-1], items=items,
-            lat=P["fly"] + cnt(items[0][0]) * (4 if items[0][0][0] == "af" else 2) * 128 / 40.0)
+        return add("g", None, rd, wr, P["issue"], sem=sems[-1], items=items, lat=P["fly"] + nbytes / P["rate"])
 
     bf, fh, f32, i32, u16 = "bfloat16", "float16", "float32", "int32", "uint16"
-    table, win0 = ("tb", 0, W, 1), ("tb", 0, W + 16, 1)
+    tabs = [(n, 16, 16 + W, 1) for n in ("tb", "t2")]
+    wins = [(n, 0, 16 + W, 1) for n in ("tb", "t2")]
     hi, gi, zi, thi, qi = new(i32, LN), new(i32, LN), new(i32, LN), new(i32, 1), new(i32, 4 * LN)
-    load("s", table, "xt", P["dma"] + 3500)
+    first = load("s", tabs[0], "xt", P["dma"] + 3500)
     load("y", hi, "hn", P["dma"]); load("y", gi, "gt", P["dma"]); load("y", zi, "zs", P["dma"])
     load("y", qi, "qs", P["dma"] + 300); load("y", thi, "th", P["dma"])
-    row, rowg, rowh = new(bf, 144), new(bf, 128), new(bf, 144)
-    ci, cj, jt_i = new(i32, 16), new(i32, 2), new(i32, L // 8)
-    iota(ci, [[-1, 16]], 16, 1); iota(row, [[1, 144]], 0, 0); iota(cj, [[0, 2]], 0, 1)
-    iota(rowg, [[1, 8], [0, 16]], 0, 0); iota(rowh, [[1, 72], [0, 2]], 0, 0)
-    iota(jt_i, [[16, L // 8]], 0, 1)
+    cur[0] = 2
+    for k in range(1, NR):
+        sx, lx, slot = ("sx", k, k + 1, 1), ("lx", k, k + 1, 1), NR - k
+        dma("y", lambda T, r, k=k: T.sx[k - 1], lambda T, r, k=k: T.xt[BLK * ((r + k) % NR):BLK * ((r + k) % NR + 1), :],
+            [], [sx], P["dma"] + 1000 * k, after=[first])
+        send([(lambda T, k=k: T.sx[k - 1], lambda T, k=k: T.lx[k - 1], k)], [sx], [lx], BLK * W * k // 2)
+        dma("y", lambda T, r, s=slot: T.t2[BLK * s:BLK * (s + 1), 16:16 + W], lambda T, r, k=k: T.lx[k - 1],
+            [lx], [part(slot)], P["dma"] + 1500)
+    dma("y", lambda T, r: T.t2[0:BLK, 16:16 + W], lambda T, r: T.xt[BLK * r:BLK * (r + 1), :], [], [part(0)],
+        P["dma"] + 4000, after=[first])
+    cur[0] = 0
+    row, rowg = new(bf, 144), new(bf, 128)
+    ci, cj = new(i32, 16), new(i32, 3)
+    iota(ci, [[-1, 16]], 16, 1); iota(row, [[1, 144]], 0, 0); iota(cj, [[BLK, 3]], 128 - BLK, 1)
+    iota(rowg, [[16, 8], [0, 16]], 0, 0)
     SP = max(n for _, n in P["fp"])
     reset = new(bf, 16 * SP)
     iota(reset, [[0, SP], [256, 16]], 0, 0)
-    ci2, cj2, c16 = new(i32, 16), new(i32, 2), new(f32, 2)
+    wpi, WP = new(bf, 640), new(bf, 640)
+    iota(wpi, [[-BLK, 5], [-1024, 4], [-1, BLK]], BLK, 1)
+    ci2, cj2, c16 = new(i32, 16), new(i32, 3), new(f32, 3)
     ts(ci2, ci, 15, A.bitwise_and); ts(cj2, cj, 112, A.bitwise_and); cp(c16, cj2)
-    g16 = sub(c16, 0, 1)
-    col = new(f32, 16)
-    ts(col, ci2, g16, A.add)
-    cx = new(f32, 3)
-    ts(sub(cx, 0, 1), g16, 1.0 / 16, A.mult); ts(sub(cx, 1, 2), g16, 15.0, A.add)
-    ts(sub(cx, 2, 3), g16, 0.5, A.mult, 7.0, A.add)
-    jt = new(bf, L // 8)
-    ts(jt, jt_i, g16, A.subtract)
+    g16 = {sh: sub(c16, sh + 1, sh + 2) for sh in (-1, 0, 1)}
+    col = {sh: new(f32, 16) for sh in g16}
+    c15 = new(f32, 1)
+    ts(col[0], ci2, g16[0], A.add); ts(c15, g16[0], 15.0, A.add)
     row128 = sub(row, 0, 128)
+    made = {}
 
     def cmp_mat(src, c, op, scale, dt=bf):
         m = new(dt, cnt(src))
         ts(m, src, c, op, scale, A.mult)
         return m
 
-    def rot(r, scale, dt=bf):
-        return cmp_mat(row128, sub(col, r % 16, r % 16 + 1), A.is_equal, scale, dt)
-    I2080, I3232, I1 = rot(0, 2080.0), rot(0, 3232.0), rot(0, 1.0)
-    B2 = cmp_mat(rowh, sub(cx, 2, 3), A.is_equal, 2.0 * L)
-    ONE = cmp_mat(rowg, sub(cx, 0, 1), A.is_equal, 1.0)
-    Hc0, G0, z0, thc = new(fh, LN), new(fh, LN), new(bf, LN), new(fh, 1)
-    ts(Hc0, hi, 2048.0, A.subtract); ts(G0, gi, 2048.0, A.subtract); cp(z0, zi); ts(thc, thi, 2048.0, A.subtract)
-    qf = []
+    def rot(r, scale=1.0, sh=0, dt=bf):
+        key = ("rot", r % 16, scale, sh, dt)
+        if key not in made:
+            made[key] = cmp_mat(row128, sub(col[sh], r % 16, r % 16 + 1), A.is_equal, scale, dt)
+        return made[key]
+
+    def grp(scale, sh=0):
+        key = ("grp", scale, sh)
+        if key not in made:
+            made[key] = cmp_mat(rowg, g16[sh], A.is_equal, scale)
+        return made[key]
+
+    I1, I2080, I3232 = rot(0), rot(0, 2080.0), rot(0, 3232.0)
+    k1, khalf, k3072 = new(bf, L), new(bf, L), new(bf, L)
+    fill(k1, 1.0)
+    IW = 168
+    IB, SB = new(fh, 4 * IW), new(fh, 4 * IW)
+    fill(sub(IB, 5 * LN, 4 * IW), 0.0)
+    names = [sub(b, 4 * LN, 5 * LN) for b in (IB, SB)]
+    thc = [sub(b, 5 * LN, 5 * LN + 1) for b in (IB, SB)]
+    st = []
     for c in range(NCH):
-        qf.append(new(f32, 4 * L))
+        st.append(dict(
+            x=new(bf, 16 * L), d=[new(bf, 16 * L) for _ in range(NS)], a=[new(bf, 16 * L) for _ in range(NS)],
+            fin=new(bf, 16 * L), sc=new(bf, 16 * L), pr=new(f32, L), s=new(i32, L), sx=new(i32, 2 * L),
+            ix=new(i32, L), ux=new(u16, L), idx=new(i32, 3 * L), uy=[new(u16, L) for _ in range(NS)],
+            rf=[new(fh, 4 * L) for _ in range(NS + 1)], m=new(bf, 3 * L), sel=new(fh, 2 * L), eq=new(bf, 4 * L),
+            e3=new(f32, 3 * L), s3=new(i32, 3 * L), g2=new(i32, L), fp=new(f32, 3 * L), uf=new(u16, L), fs=new(fh, 4 * L),
+            hi=new(bf, 2 * L), tmp=new(fh, 4 * L), pb=[new(bf, 2 * L) for _ in range(2)], zf=new(bf, L), gb=new(fh, 2 * L),
+            q=sub(IB, 4 * L * c, 4 * L * (c + 1)), z=new(bf, L), cn=None, par=None))
+    ts(names[0], hi, 2048.0, A.subtract)
+    for c, S in enumerate(st):
+        fill(S["gb"], 0.0)
+        ts(sub(S["gb"], 1, 2 * L, 2), sub(gi, L * c, L * c + L), 2048.0, A.subtract)
+        cp(S["z"], sub(zi, L * c, L * c + L))
         for b in range(2):
-            cp(sub(qf[c], 2 * L * b, 2 * L * (b + 1)), sub(qi, 2 * (LN * b + L * c), 2 * (LN * b + L * c + L)))
-    Q = [I1] + [rot(-t, 1.0) for t in range(1, NV)]
-    NI, BI = rot(0, -1.0), rot(0, BIG)
-    B1 = cmp_mat(row, sub(cx, 1, 2), A.is_equal, 1.0)
-    LTa = cmp_mat(row128, sub(col, 0, 1), A.is_lt, -2 * BIG)
-    LTb = cmp_mat(row128, g16, A.is_lt, 2 * BIG)
-    NONE = cmp_mat(rowg, sub(cx, 0, 1), A.is_equal, -1.0)
-    R5, R6, R10 = rot(5, 1.0), rot(6, 1.0), rot(10, 1.0)
-    BR = [BI, rot(5, BIG), rot(10, BIG)]
-    NB = [rot(0, -BIG), rot(-5, -BIG), rot(-10, -BIG)]
-    IH, F2 = rot(0, 0.5), rot(0, 2.0, f32)
-    FT = [[Q[1], rot(-1, 2048.0), rot(-1, 32.0)], [rot(NV - 1, 1.0), rot(NV - 1, 2048.0), rot(NV - 1, 32.0)]]
-    k1, ka, kb, khalf = new(bf, L), new(bf, L), new(bf, L), new(bf, L)
-    fill(k1, 1.0); fill(ka, 6144 / BIG); fill(kb, (2048.0 * 6144 + 32 * 2048 - 2 ** 22) / BIG)
-    fill(khalf, -0.5); fill(("tb", W, W + 16, 1), 0.0)
-    bias = new(f32, 2)
-    bU, bX = sub(bias, 0, 1), sub(bias, 1, 2)
-    fill(bU, 32.0 - 2048); fill(bX, 2048.0)
-    Hr, Hl, thb = new(fh, 4 * LN), new(fh, 3 * LN), new(f32, NV)
-    mm([(ps(5, LN * i, LN * (i + 1)), [(Q[i + 1], Hc0)]) for i in range(4)])
-    cp(Hr, ps(5, 0, 4 * LN))
-    send([(sub(Hr, LN * i, LN * (i + 1)), sub(Hl, LN * i, LN * (i + 1)), i + 1) for i in range(3)])
-    H = [Hc0] + [sub(Hl, LN * i, LN * (i + 1)) for i in range(3)] + [sub(Hr, 3 * LN, 4 * LN)]
-    mm([(ps(5, t, t + 1), [(Q[t], thc)]) for t in range(NV)])
-    ts(thb, ps(5, 0, NV), 256.0, A.mult, 256.0 * 2048 - 128, A.add)
-    TR, wtmp = [None] * NV, new(bf, 128)
+            ts(sub(S["q"], 2 * L * b, 2 * L * (b + 1)), sub(qi, 2 * (LN * b + L * c), 2 * (LN * b + L * c + L)),
+               2048.0, A.subtract)
+    ts(thc[0], thi, 2048.0, A.subtract)
+    NI, BI, NB, ONE, NONE = rot(0, -1.0), rot(0, BIG), rot(0, -BIG), grp(1.0), grp(-1.0)
+    fill(khalf, -0.5); fill(k3072, 3072.0)
+    for S in st:
+        fill(S["pb"][0], 0.0); fill(S["pb"][1], 0.0)
+    B1 = cmp_mat(row, c15, A.is_equal, 1.0)
+    LTa = cmp_mat(row128, sub(col[0], 0, 1), A.is_lt, -2 * BIG)
+    LTb = cmp_mat(row128, g16[0], A.is_lt, 2 * BIG)
+    for n in ("tb", "t2"):
+        fill((n, 0, 16, 1), 0.0)
+    for S in st:
+        fill(S["eq"], 0.0); fill(S["e3"], 0.0)
+    k1536, k1024, kq = new(bf, L), new(bf, L), new(bf, 4 * L)
+    fill(k1536, 1536.0); fill(k1024, 1024.0); fill(kq, 0.25)
+    bias = new(f32, 3)
+    b32, bX, bN = sub(bias, 0, 1), sub(bias, 1, 2), sub(bias, 2, 3)
+    fill(b32, 32.0); fill(bX, 2048.0); fill(bN, -2048.0)
+    ts(col[1], ci2, g16[1], A.add); ts(col[-1], ci2, g16[-1], A.add)
+    ts(WP, wpi, 0.0, A.is_equal)
+    IF = rot(0, 1.0, 0, f32)
+    Q = [rot(-t) for t in range(NV)]
+    thb = new(f32, NV)
+    H, TR, wtmp = [names[0]] + [None] * (NV - 1), [None] * NV, new(bf, 128)
+
+    def move(src, dst):
+        return (WP[0], WP[1], WP[2], 1, lambda r: 128 + 128 * src(r) - BLK * dst(r))
+
+    def thresholds(bank, ts_):
+        r = ps(bank, 504 + ts_[0], 505 + ts_[-1])
+        mm([(ps(bank, 504 + t, 505 + t), Q[t], thc[t > 0]) for t in ts_])
+        ts(sub(thb, ts_[0], ts_[-1] + 1), r, 256.0, A.mult, 256.0 * 2048 - 128, A.add)
 
     def make_tr(t, bank):
         TR[t] = new(bf, 128)
         r = ps(bank, 384, 512)
-        mm([(r, [(LTa, Q[t]), (LTb, Q[t]), (BI, Q[t])])])
+        mm([(r, LTa, Q[t]), (r, LTb, Q[t]), (r, BI, Q[t])])
         act(wtmp if t else TR[t], r, AF.Copy)
         if t:
-            mm([(r, [(Q[t], wtmp)])])
+            mm([(r, Q[t], wtmp)])
             act(TR[t], r, AF.Copy)
+
+    def make_names(t, bank):
+        H[t] = new(fh, LN)
+        r = ps(bank, 384, 512)
+        mm([(r, rot(-1, 1.0, 1), names[1] if t == 1 else H[t - 1])])
+        act(H[t], r, AF.Copy)
+
+    def ship(src, w, pack, from_blk, to_blk, copy):
+        out, land = new(fh, 3 * w), new(fh, 3 * w)
+        for k in range(1, NR):
+            o = sub(pack, (k - 1) * w, k * w)
+            mm([(o, move(lambda r, k=k: from_blk(r, k), lambda r, a=a: a), sub(src, a * w, (a + 1) * w)) for a in range(4)])
+        copy(out, sub(pack, 0, 3 * w))
+        send([(lambda T, k=k: ap(T, sub(out, (k - 1) * w, k * w), 0), lambda T, k=k: ap(T, sub(land, (k - 1) * w, k * w), 0), k)
+              for k in range(1, NR)], [out], [land], 128 * w * 2 * 2)
+
+        def unpack(reg, quarters):
+            terms = []
+            for n, a in enumerate(quarters):
+                o = sub(reg, n * w, (n + 1) * w)
+                terms.append((o, move(lambda r: from_blk(r, 0), lambda r, a=a: to_blk(r, 0, a)), sub(src, a * w, (a + 1) * w)))
+                terms += [(o, move(lambda r, a=a: a, lambda r, a=a, k=k: to_blk(r, k, a)), sub(land, (k - 1) * w, k * w))
+                          for k in range(1, NR)]
+            mm(terms)
+        return unpack
+
+    def scopy(out, in_):
+        act(out, in_, AF.Copy)
+
+    thresholds(7, [0])
     make_tr(0, 7)
+    cur[0] = 2
+    dealt = ship(IB, IW, ps(4, 0, 3 * IW), lambda r, k: (r + k) % NR, lambda r, k, a: -k % NR, scopy)
 
     def pieces(sz):
         out, a = [], 0
@@ -239,184 +309,197 @@ def build(P):
         else:
             cp(out, ("ind", win, off))
 
-    st = []
-    for c in range(NCH):
-        st.append(dict(
-            x=new(bf, 16 * L), d=[new(bf, 16 * L) for _ in range(NS)], a=[new(bf, 16 * L) for _ in range(NS)],
-            fin=new(bf, 16 * L), sc=new(bf, 16 * L), pr=new(f32, L), s=new(i32, L), px=new(f32, L), sx=new(i32, L),
-            ix=new(i32, L), ux=new(u16, L), idx=new(i32, 3 * L), uy=[new(u16, L) for _ in range(NS)],
-            c1=new(i32, L // 8), c2=new(i32, L // 8), off=[new(u16, L // 8) for _ in range(NV)],
-            rf=[new(fh, 4 * L) for _ in range(NS + 1)], m=new(bf, 3 * L), sel=new(fh, 2 * L), eq=new(bf, 4 * L),
-            uc=new(f32, 2 * L), fp=new(f32, 3 * L), uf=new(u16, L), fs=new(fh, 4 * L), hi=new(bf, 2 * L),
-            s2=new(i32, 2 * L), g2=new(i32, L), zf=new(bf, L), tmp=new(f32, 2 * L),
-            G=sub(G0, L * c, L * c + L), z=sub(z0, L * c, L * c + L), cn=None, X=None))
-    for S in st:
-        fill(S["eq"], 0.0); fill(S["uc"], 0.0)
-
-    def names_tails(rf, s):
-        if s == 0:
-            return sub(rf, 0, 2 * L, 2), sub(rf, 1, 2 * L, 2)
+    def names_tails(rf):
         return sub(rf, 1, 2 * L, 2), sub(rf, 2 * L + 1, 4 * L, 2)
-
-    def index(a, b, pl, pr, s, ix, ux):
-        mm([(pl, [(I2080, a), (I3232, b)])])
-        tt(pr, a, b, A.mult)
-        tt(s, pr, pl, A.add)
-        ts(ix, s, 5, A.arith_shift_right, W - 1, A.bitwise_and)
-        cp(ux, ix)
-
-    def merge(c, t):
-        S = st[c]
-        w = ("ind", qf[c], S["off"][t - 1])
-        act(S["hi"], S["X"], AF.Relu, scale=-1.0)
-        tt(S["tmp"], w, S["hi"], A.min)
-        tt(w, S["tmp"], S["X"], A.max)
 
     def visit(c, t):
         S = st[c]
-        bS, b1, b2, bD = 4 * c, 4 * c + 1, 4 * c + 2, 4 * c + 3
-        lay = dict(d=(bS, 0), u=(bS, 1), cn=(bS, 2), zf=(bS, 3), T=(bS, 4), D=(bD, 0), fid=(bD, 6), z=(bD, 7),
-                   sel=(b1, 0), delta=(b1, 2), X=(b1, 0),
-                   diff=(b2, 0), ly=(b2, 2), lx=(b2, 3), ch=(b2, 4), fm=(b2, 5), fa=(b2, 0))
+        b0, b1, b2, b3 = 4 * c, 4 * c + 1, 4 * c + 2, 4 * c + 3
+        lay = dict(d=(b0, 0), cn=(b0, 1), zf=(b0, 2), z=(b0, 3), hi=(b0, 4), T01=(b0, 4), fm=(b0, 1), w=(b0, 6),
+                   sel=(b1, 0), T23=(b1, 2), lx=(b1, 2), dg=(b1, 4), ly=(b1, 5), diff=(b1, 6),
+                   dr=(b2, 0), par=(b2, 0), g3=(b2, 4),
+                   D=(b3, 0), fid=(b3, 6), hd=(b3, 0), A=(b3, 4), qd=(b3, 0))
 
-        def pr(name, a=0, b=1):
-            bank, o = lay[name]
-            return ps(bank, int((o + a) * L), int((o + b) * L))
-        Ht, G, z, x, m = sub(H[t], L * c, L * c + L), S["G"], S["z"], S["x"], S["m"]
+        def pr(name, a=0, b=1, o=0, st=1):
+            bank, u = lay[name]
+            return ("ps%d" % bank, int((u + a) * L) + o, int((u + b) * L), st)
         last = t == NV - 1
-        index(Ht, G, pr("lx"), S["px"], S["sx"], S["ix"], S["ux"])
+        table, win0 = tabs[t > 0], wins[t > 0]
+        nr, ns = (NV - 1, 0) if last else (-1, int(t > 0))
+        if c == 0 and not last:
+            make_tr(t + 1, b3)
+        if c == 1 and 0 < t < NV - 1:
+            make_names(t + 1, b3)
+        Ht, G, z, x, m, q = sub(H[t], L * c, L * c + L), sub(S["gb"], 1, 2 * L, 2), S["z"], S["x"], S["m"], S["q"]
+        mm([(pr("lx", 0, 2, 0, 2), I1, Ht), (pr("lx", 0, 2, 0, 2), I3232, k1), (pr("lx", 0, 2, 1, 2), I2080, Ht)])
+        fma(S["sx"], S["gb"], pr("lx", 0, 2))
+        ts(S["ix"], sub(S["sx"], 1, 2 * L, 2), 5, A.arith_shift_right, W - 1, A.bitwise_and)
+        cp(S["ux"], S["ix"])
         xp = P["xp" if t else "xp0"]
         for (e, _), (a, b) in zip(xp, pieces([n for _, n in xp])):
             gather(e, sub(x, 16 * a, 16 * b), table, sub(S["ux"], a, b))
-        cur[1] = 1020
-        if c == 0 and not last:
-            make_tr(t + 1, bD)
-        cur[1] = 1030
-        pc = pr("ch", 0, 0.125)
-        mm([(pc, [(I1, jt)] + [(sub(B2, 14 - 2 * a, 142 - 2 * a), sub(z, a, L, 8)) for a in range(8)])])
-        cp(S["c1"], pc); ts(S["c2"], S["c1"], 4 * L - 1, A.bitwise_and); cp(S["off"][t], S["c2"])
-        if t > 1:
-            merge(c, t - 1)
-        cur[1] = 1040
-        ts(sub(S["rf"][0], 0, 2 * L), ("ind", qf[c], S["off"][t]), 2048.0, A.subtract)
-        mm([(pr("u"), [(ONE, z)])])
-        act(sub(S["uc"], 1, 2 * L, 2), pr("u"), AF.Identity, bias=bU)
+        qv = [[sub(q, 2 * L * b + i, 2 * L * (b + 1), 2) for b in range(2)] for i in range(2)]
+        mm([x_ for i in range(2) for x_ in ((pr("qd", 2 * i, 2 * i + 2, 0, 2), I1, qv[i][0]),
+                                            (pr("qd", 2 * i, 2 * i + 2, 0, 2), NI, qv[i][1]),
+                                            (pr("qd", 2 * i, 2 * i + 2, 1, 2), I1, qv[i][0]))])
+        po, pb = pr("par"), S["pb"][t % 2]
+        mm([(po, I1, khalf)], stop=False)
+        mm([(po, ONE, z), (po, BI, k3072), (po, NB, k3072), (po, NONE, z)], start=False)
+        par_before, S["par"] = S["par"], sub(pb, 1, 2 * L, 2)
+        scopy(S["par"], po)
+        for i in range(2):
+            fma(sub(S["rf"][0], 2 * L * i, 2 * L * (i + 1)), pb, pr("qd", 2 * i, 2 * i + 2))
+        msg = new(fh, 6 * L if last else 4 * L) if t == 0 or last else None
+        if t == 0:
+            scopy(sub(msg, 3 * L, 4 * L), po)
+        mm([(pr("w"), grp(1.0, ns), z)])
+        act(sub(S["e3"], 2, 3 * L, 3), pr("w"), AF.Identity, bias=b32)
         ms = [sub(m, s * L, (s + 1) * L) for s in range(NS)]
-        fp = [sub(S["fp"], s * L, (s + 1) * L) for s in range(NS)]
+        fs = S["fs"]
+        fq = [sub(fs, i * L, (i + 1) * L) for i in range(4)]
         for s in range(NS):
             rf, idx = S["rf"][s], sub(S["idx"], s * L, (s + 1) * L)
-            cur[1] = 1060 + 50 * s
-            R, F = names_tails(rf, s)
-            RT = R5 if s < NS - 1 else R6
-            index(R, F, pr("ly"), S["pr"], S["s"], idx, S["uy"][s])
+            end = s == NS - 1
+            R, F = names_tails(rf)
+            mm([(pr("ly"), I2080, R), (pr("ly"), I3232, F)])
+            tt(S["pr"], R, F, A.mult)
+            tt(S["s"], S["pr"], pr("ly"), A.add)
+            ts(idx, S["s"], 5, A.arith_shift_right, W - 1, A.bitwise_and)
+            cp(S["uy"][s], idx)
+            early = []
+            if end:
+                early.append(mm([(pr("T01", i, i + 1), lhs, rhs) for i in range(2)
+                                 for lhs, rhs in ((rot(5 * i - 10), F), (BI, ms[i]))]))
+                ts(sub(fs, 0, 2 * L), pr("T01", 0, 2), BIG, A.subtract, -2048.0, A.max)
+                early.append(mm([(pr("fm", 0, 1), I1, ms[0]), (pr("fm", 1, 2), I1, ms[1]), (pr("fm", 2, 3), I1, k1),
+                                 (pr("fm", 2, 3), NI, ms[0]), (pr("fm", 2, 3), NI, ms[1])]))
+                tt(S["fp"], S["idx"], pr("fm", 0, 3), A.mult)
             d, a_, uy, nd = S["d"][s], S["a"][s], S["uy"][s], P["nd"][s]
             nv = L - nd
             ya, pD = sub(d, 16 * nv, 16 * L), pr("D", 0, 16.0 * nd / L)
             act(ya, ("ind", table, sub(uy, nv, L)), AF.Copy)
-            mm([(pD, [(NI, sub(x, 16 * nv, 16 * L))])], stop=False)
-            mm([(pD, [(I1, ya)])], start=False)
+            mm([(pD, NI, sub(x, 16 * nv, 16 * L))], stop=False)
+            mm([(pD, I1, ya)], start=False)
             act(sub(a_, 16 * nv, 16 * L), pD, AF.Abs)
             vp = list(P["vp"]); vp[0] += nv - sum(vp)
             for a, b in pieces(vp):
                 tt(sub(d, 16 * a, 16 * b), ("ind", table, sub(uy, a, b)), sub(x, 16 * a, 16 * b), A.subtract)
                 act(sub(a_, 16 * a, 16 * b), sub(d, 16 * a, 16 * b), AF.Abs)
             pre = [(NI, S["cn"])] if t else []
-            pre += [(BI, ms[s0]) for s0 in range(s)] + [(BR[s - s0], ms[s0]) for s0 in range(s)]
+            pre += [(BI, ms[s0]) for s0 in range(s)] + [(rot(5 * (s - s0), BIG), ms[s0]) for s0 in range(s)]
             if pre:
-                mm([(pr("d"), pre)], stop=False)
-            mm([(pr("d"), [(sub(B1, 15 - k, 143 - k), sub(a_, k, 16 * L, 16)) for k in range(16)])], start=not pre)
+                mm([(pr("d"), lhs, rhs) for lhs, rhs in pre], stop=False, after=early)
+            mm([(pr("d"), sub(B1, 15 - k, 143 - k), sub(a_, k, 16 * L, 16)) for k in range(16)], start=not pre)
             act(ms[s], pr("d"), AF.Sigmoid, bias=sub(thb, t, t + 1), scale=-256.0)
-            dr = pr("delta", 0, 4)
-            mm([(sub(dr, 2 * L * i + 1, 2 * L * (i + 1), 2), [(RT, (R, F)[i])]) for i in range(2)])
-            if s == NS - 1:
-                mm([(pr("fid"), [(NB[0], ms[0]), (NB[0], ms[1]), (F2, fp[0]), (F2, fp[1])])], stop=False)
-                mm([(pr("fm"), [(I1, ms[s])])])
-                tt(fp[s], idx, pr("fm"), A.mult)
-                mm([(pr("fid"), [(NB[0], ms[2]), (F2, fp[2])])], start=False)
-                ts(S["uf"], pr("fid"), 0.5, A.mult, float(W), A.add)
+            rename = not end or t > 0
+            xs = -1 if end else 0
+            RT = rot(6, 1.0, -1) if end and rename else rot(5)
+            if end:
+                mm([(pr("fid"), IF, sub(S["fp"], i * L, (i + 1) * L)) for i in range(NS)]
+                   + [(pr("fid"), BI, ms[0]), (pr("fid"), BI, ms[1])], stop=False)
+                mm([(pr("fid"), BI, ms[2])], start=False)
+                ts(S["uf"], pr("fid"), 16.0 - BIG, A.add)
                 for (e, _), (a, b) in zip(P["fp"], pieces([n for _, n in P["fp"]])):
                     gather(e, sub(S["fin"], 16 * a, 16 * b), win0, sub(S["uf"], a, b))
-                    scan(sub(S["sc"], 16 * a, 16 * b), sub(reset, 0, 16 * (b - a)), sub(S["fin"], 16 * a, 16 * b))
-            cur[1] = 1090 + 50 * s
+                    scan(sub(S["sc"], 16 * a, 16 * b), sub(reset, 0, 16 * (b - a)), sub(S["fin"], 16 * a, 16 * b), A.min, A.max)
             sR, sH = sub(S["sel"], 0, L), sub(S["sel"], L, 2 * L)
-            mm([(pr("sel"), [(I1, R), (TR[t], ms[s])])])
-            mm([(pr("T"), [(I1, Ht), (TR[t], ms[s])])])
-            ts(sR, pr("sel"), BIG, A.subtract, -2048.0, A.max)
-            ts(sH, pr("T"), BIG, A.subtract, -2048.0, A.max)
-            mm([(pr("diff", 0, 1), [(RT, R), (NONE, sR)]), (pr("diff", 1, 2), [(RT, F), (NONE, sR)])])
-            mm([(sub(dr, 2 * L * i, 2 * L * (i + 1), 2), [(ONE, sH), (NONE, sR)]) for i in range(2)])
-            ts(sub(S["eq"], 1, 4 * L, 2), pr("diff", 0, 2), 15 * 2048.0, A.is_equal)
-            fma(S["rf"][s + 1], S["eq"], dr)
-            cur[1] += 1
-            if s < NS - 1:
-                mm([(pr("fm"), [(I1, ms[s])])])
-                tt(fp[s], idx, pr("fm"), A.mult)
-        cur[1] = 1220
-        R, F = names_tails(S["rf"][NS], NS)
-        cn = new(bf, L)
-        mm([(pr("cn"), [(ONE, ms[i]) for i in range(NS)])])
-        act(cn, pr("cn"), AF.Copy)
-        mm([(pr("zf"), [(I1, z), (NB[0], cn)])])
+            T2, T3 = pr("T23", 0, 1), pr("T23", 1, 2)
+            mm([(pr("sel", 0, 1), I1, R), (pr("sel", 1, 2), I1, Ht)]
+               + ([(T2, I1, F), (T3, I1, G), (T3, BI, k1), (T3, NB, ms[0]), (T3, NB, ms[1])] if end else []), stop=False)
+            mm([(pr("sel", 0, 1), TR[t], ms[s]), (pr("sel", 1, 2), TR[t], ms[s])]
+               + ([(T2, BI, ms[s]), (T3, NB, ms[s])] if end else []), start=False)
+            ts(S["sel"], pr("sel", 0, 2), BIG, A.subtract, -2048.0, A.max)
+            if end:
+                ts(sub(fs, 2 * L, 4 * L), pr("T23", 0, 2), BIG, A.subtract, -2048.0, A.max)
+            g3 = [pr("g3", 0, 3, i, 3) for i in range(3)]
+            f1 = rot(nr, 1.0, ns) if end else None
+            pre, post = [], []
+            if rename:
+                pre += [(pr("dr", 2 * i, 2 * i + 2, 1, 2), RT, (R, F)[i]) for i in range(2)]
+                post += [(pr("dr", 2 * i, 2 * i + 2, 0, 2), lhs, rhs) for i in range(2)
+                         for lhs, rhs in ((grp(1.0, xs), sH), (grp(-1.0, xs), sR))]
+            if end:
+                pre += [(g3[1], NB, khalf), (g3[1], f1, fq[0]), (g3[1], f1, fq[1]),
+                        (g3[2], grp(2048.0, ns), z), (g3[2], NB, k1024)]
+            mm(pre, stop=False)
+            if rename:
+                mm([(pr("diff", i, i + 1), lhs, rhs) for i in range(2)
+                    for lhs, rhs in ((RT, (R, F)[i]), (grp(-1.0, xs), sR))])
+            if end:
+                mm([(pr("dg"), rot(nr, -BIG, ns), ms[i]) for i in range(NS)] + [(pr("dg"), f1, fq[i]) for i in range(NS)]
+                   + [(pr("dg"), grp(-1.0, ns), sR)])
+                post += [(g3[0], grp(1.0, ns), sH), (g3[0], grp(-1.0, ns), sR), (g3[1], f1, fq[2]),
+                         (g3[2], rot(nr, 32.0, ns), fq[3])]
+            mm(post, start=False)
+            if end:
+                ts(sub(S["e3"], 1, 3 * L, 3), pr("dg"), 13 * 2048.0 - BIG, A.is_equal)
+                fma(S["s3"], S["e3"], pr("g3", 0, 3))
+                ts(S["g2"], sub(S["s3"], 2, 3 * L, 3), 5, A.arith_shift_right, W - 1, A.bitwise_and)
+                ts(sub(msg, 4 * L, 5 * L) if last else sub(msg, 0, L) if t == 0 else G, S["g2"], 2048.0, A.subtract)
+            if rename:
+                ts(sub(S["eq"], 1, 4 * L, 2), pr("diff", 0, 2), 15 * 2048.0, A.is_equal)
+                fma(S["rf"][s + 1], S["eq"], pr("dr", 0, 4))
+        mm([(pr("zf"), I1, z)] + [(pr("zf"), grp(-BIG), ms[i]) for i in range(NS)])
         act(S["zf"], pr("zf"), AF.Relu)
-        mm([(pr("z"), [(IH, khalf), (IH, z), (IH, S["zf"])])], stop=False)
-        mm([(pr("z"), [(IH, sub(S["sc"], 15, 16 * L, 16))])], start=False)
-        zn = new(f32 if last else bf, L)
-        ts(zn, pr("z"), MAGIC, A.add, MAGIC, A.subtract)
-        fs = S["fs"]
-        fq = [sub(fs, i * L, (i + 1) * L) for i in range(4)]
-        mm([(pr("T", 3, 4), [(I1, G), (BI, k1)] + [(NB[0], ms[i]) for i in range(NS)])])
-        mm([(pr("T", 0, 3), [(BI, m)])], stop=False)
-        mm([(pr("T", 0, 3), [([I1, R5, R10][i], F, pr("T", i, i + 1)) for i in range(NS)])], start=False)
-        ts(fs, pr("T", 0, 4), BIG, A.subtract, -2048.0, A.max)
-        f1, f2048, f32_ = FT[last]
-        fab = pr("fa", 0, 2)
-        mm([(sub(fab, 0, 2 * L, 2), [(BI, ka)] + [(f1, f) for f in fq[:3]])])
-        cur[1] = 1300
+        early = []
+        if not last:
+            S["cn"] = sub(msg, 2 * L, 3 * L) if t == 0 else new(bf, L)
+            early.append(mm([(pr("cn"), grp(1.0, ns), ms[i]) for i in range(NS)]))
+            scopy(S["cn"], pr("cn"))
         if t:
-            xs, S["X"] = new(f32, 2 * L), new(f32, 2 * L)
-            mm([(pr("X", i, i + 1), [(NB[j], ms[j]) for j in range(NS)] + [(I1, (R, F)[i])]) for i in range(2)])
-            for i in range(2):
-                act(sub(xs, i, 2 * L, 2), pr("X", i, i + 1), AF.Identity, bias=bX)
-            send([(xs, S["X"], -1)])
-        cur[1] = 1304
-        mm([(sub(fab, 1, 2 * L, 2), [(BI, kb)] + [(f2048, f) for f in fq[:3]] + [(f32_, fq[3])])])
-        fma(S["s2"], S["uc"], fab)
-        cur[1] += 1
-        ts(S["g2"], sub(S["s2"], 1, 2 * L, 2), 5, A.arith_shift_right, W - 1, A.bitwise_and)
-        gn = new(f32 if last else fh, L)
-        ts(gn, S["g2"], 0.0 if last else 2048.0, A.subtract)
-        cur[1] = 1312
+            early.append(mm([(pr("hi", b, b + 1), rot(-5 * i, BIG, -1), ms[i]) for b in range(2) for i in range(NS)]
+                            + [(pr("hi", 0, 1), NB, par_before), (pr("hi", 1, 2), BI, par_before), (pr("hi", 1, 2), BI, k1)]))
+            scopy(S["hi"], pr("hi", 0, 2))
+        IH = rot(0, 0.5, ns)
+        mm([(pr("z"), IH, khalf), (pr("z"), IH, z), (pr("z"), IH, S["zf"])], stop=False, after=early)
+        mm([(pr("z"), IH, sub(S["sc"], 15, 16 * L, 16)), (pr("z"), BI, k1536), (pr("z"), NB, k1536)], start=False)
         if last:
-            cur[1] = 1320
-            store("y", "yg", L * c, L * c + L, gn); store("y", "yz", L * c, L * c + L, zn)
-            merge(c, t)
-            for b in range(2):
-                store("ys"[b], "yq", 2 * (LN * b + L * c), 2 * (LN * b + L * c + L), sub(qf[c], 2 * L * b, 2 * L * (b + 1)))
+            act(sub(msg, 5 * L, 6 * L), pr("z"), AF.Identity, bias=bN)
         else:
-            S["G"], S["cn"], S["z"] = new(fh, L), new(bf, L), new(bf, L)
-            if P["zsep"]:
-                send([(gn, S["G"], 1), (cn, S["cn"], 1)]); send([(zn, S["z"], 1)])
-            else:
-                send([(gn, S["G"], 1), (cn, S["cn"], 1), (zn, S["z"], 1)])
+            S["z"] = sub(msg, L, 2 * L) if t == 0 else new(bf, L)
+            scopy(S["z"], pr("z"))
+        if t:
+            R, F = names_tails(S["rf"][NS])
+            mm([(pr("hd", 0, 4), NB, kq)] + [(pr("hd", 0, 4, i, 2), I1, S["hi"]) for i in range(2)])
+            tt(S["tmp"], q, pr("hd", 0, 4), A.min)
+            mm([(pr("A", 0, 4, i, 2), NI, S["hi"]) for i in range(2)]
+               + [(pr("A", 2 * b, 2 * b + 2, i, 2), I1, (R, F)[i]) for b in range(2) for i in range(2)])
+            S["q"] = sub(msg, 0, 4 * L) if last else new(fh, 4 * L)
+            tt(S["q"], S["tmp"], pr("A", 0, 4), A.max)
+        if t == 0:
+            un = ps(b3, 4 * L, 8 * L)
+            if c == 0:
+                for i, b in enumerate((b1, b2)):
+                    dealt(ps(b, 0, 2 * IW), (2 * i, 2 * i + 1))
+                    scopy(sub(SB, 2 * IW * i, 2 * IW * (i + 1)), ps(b, 0, 2 * IW))
+                make_names(1, b2)
+                thresholds(b1, [1, 2, 3, 4])
+            ship(msg, L, ps(b3, 0, 3 * L), lambda r, k: (r + k) % NR,
+                 lambda r, k, a: (int(a < 3) - k) % NR, cp)(un, (0, 1, 2, 3))
+            rest = new(bf, 3 * L)
+            scopy(rest, sub(un, L, 4 * L)); cp(G, sub(un, 0, L))
+            S["z"], S["cn"], S["par"] = [sub(rest, i * L, (i + 1) * L) for i in range(3)]
+            S["q"] = sub(SB, 4 * L * c, 4 * L * (c + 1))
+        if last:
+            w = 6 * L // 4
+            unpack = ship(msg, w, ps(b3, 0, 3 * w), lambda r, k: k, lambda r, k, a: (r - k) % NR, cp)
+            unpack(ps(b1, 0, 2 * w), (0, 1)); unpack(ps(b2, 0, 2 * w), (2, 3))
+            o = new(f32, 6 * L)
+            act(sub(o, 0, 2 * w), ps(b1, 0, 2 * w), AF.Identity, bias=bX)
+            ts(sub(o, 2 * w, 4 * w), ps(b2, 0, 2 * w), 2048.0, A.add)
+            for b in range(2):
+                store("ys"[b], "yq", 2 * (LN * b + L * c), 2 * (LN * b + L * c + L), sub(o, 2 * L * b, 2 * L * (b + 1)))
+            store("y", "yg", L * c, L * c + L, sub(o, 4 * L, 5 * L)); store("s", "yz", L * c, L * c + L, sub(o, 5 * L, 6 * L))
 
     for t in range(NV):
         for c in range(NCH):
-            cur[0], cur[1] = c + 2 * (0 if 0 < t < NV - 1 else 1 if t == 0 else 2), 1000
+            cur[0] = c
             visit(c, t)
 
     hist = {}
     for i, o in enumerate(ops):
-        dep = set()
-        for bank in {v[0] for v in o["rd"] + o["wr"] if v[0].startswith("ps")}:
-            runs = hist.setdefault(bank, [[], []])
-            if runs[1] and ops[runs[1][-1]]["eng"] != o["eng"]:
-                runs[0], runs[1] = runs[1], []
-            dep.update(runs[0])
-            if o["eng"] == "pe":
-                dep.update(runs[1][-1:])
-            runs[1].append(i)
+        dep = set(o.get("after", ()))
         acc = [(False, v) for v in o["rd"]] + [(True, v) for v in o["wr"]]
-        acc = [(isw, v) for isw, v in acc if not v[0].startswith("ps")]
         for isw, v in acc:
             for (j, w, a, b) in hist.get(v[0], ()):
                 if (w or isw) and a < v[2] and v[1] < b:
@@ -427,53 +510,113 @@ def build(P):
                 h[:] = [e for e in h if not (v[1] <= e[2] and e[3] <= v[2])]
             h.append((i, isw, v[1], v[2]))
         dep.discard(i)
-        o["dep"] = sorted(dep)
-    return ops, sems, top, ap
+        o["dep"] = dep
+        o["banks"] = sorted({v[0] for v in o["rd"] + o["wr"] if v[0].startswith("ps")})
+    anc, opened = [], {}
+    for i, o in enumerate(ops):
+        anc.append(set(o["dep"]).union(*[anc[j] for j in o["dep"]]) if o["dep"] else set())
+        if o["eng"] == "pe" and not o["stop"]:
+            opened[o["bank"]] = i
+        elif o["eng"] == "pe" and not o["start"]:
+            k = opened.pop(o["bank"])
+            ops[k]["dep"] |= {j for j in anc[i] if j != k and ops[j].get("bank") == o["bank"] and ops[j]["start"]
+                              and j not in anc[k]}
+    for o in ops:
+        o["dep"] = sorted(o["dep"])
+    return ops, sems, top
 
 
-def schedule(ops, P):
+def schedule(ops, P, seed):
     n = len(ops)
     succ = [[] for _ in range(n)]
     for i, o in enumerate(ops):
         for j in o["dep"]:
             succ[j].append(i)
     lam = P["lam"]
-    rank = [0.0] * n
-    for i in range(n - 1, -1, -1):
-        rank[i] = ops[i]["cost"] + ops[i].get("lat", 0) + lam + max([rank[j] for j in succ[i]], default=0)
-    pri = [rank[i] + P["bias"][o["ch"]] + P["prio"].get((o["cls"], o["key"]), 0) for i, o in enumerate(ops)]
     left = [len(o["dep"]) for o in ops]
-    ready = [0.0] * n
+    topo_order = [i for i in range(n) if not left[i]]
+    cnt = list(left)
+    for i in topo_order:
+        for j in succ[i]:
+            cnt[j] -= 1
+            if not cnt[j]:
+                topo_order.append(j)
+    rank = [0.0] * n
+    for i in reversed(topo_order):
+        rank[i] = ops[i]["cost"] + ops[i].get("lat", 0) + lam + max([rank[j] for j in succ[i]], default=0)
+    pri = []
+    for i, o in enumerate(ops):
+        seed = (seed * 1103515245 + 12345) % 2 ** 31
+        pri.append(rank[i] + (P["bias"] + (0,))[o["ch"]] + P.get("jit", 0) * seed / 2 ** 31)
+    ready, fin = [0.0] * n, [0.0] * n
     pool = {e: [] for e in ("v", "s", "pe", "g", "y")}
     for i in range(n):
         if not left[i]:
             pool[ops[i]["eng"]].append(i)
     free = {e: 0.0 for e in pool}
     order = {e: [] for e in pool}
-    seq = []
+    seq, deps, touch, shut = [], [None] * n, {}, set()
+
+    def when(i):
+        o = ops[i]
+        if o.get("start") and o["bank"] in shut:
+            return None
+        t = ready[i]
+        for b in o["banks"]:
+            for e, j in touch.get(b, {}).items():
+                if e != o["eng"] and fin[j] + lam > t:
+                    t = fin[j] + lam
+        return t
     while len(seq) < n:
         best = None
         for e, q in pool.items():
-            if q:
-                t0 = max(free[e], min(ready[i] for i in q))
+            cand = [(t, i) for t, i in ((when(i), i) for i in q) if t is not None]
+            if cand:
+                t0 = max(free[e], min(cand)[0])
                 if best is None or t0 < best[0]:
-                    best = (t0, e)
-        t0, e = best
-        i = max((i for i in pool[e] if ready[i] <= t0), key=lambda i: pri[i])
+                    best = (t0, e, cand)
+        t0, e, cand = best
+        t1, i = max(((t, i) for t, i in cand if t <= t0 + P["look"]), key=lambda x: pri[x[1]] - P["gam"] * max(0, x[0] - t0))
+        if t1 > t0:
+            fit = [j for t, j in cand if t <= t0 and ops[j]["cost"] <= t1 - t0 + P["fit"]]
+            if fit:
+                i = max(fit, key=lambda j: pri[j])
+            else:
+                t0 = t1
+        o = ops[i]
+        deps[i] = set(o["dep"])
+        for b in o["banks"]:
+            deps[i] |= {j for e2, j in touch.get(b, {}).items() if e2 != e}
+            touch.setdefault(b, {})[e] = i
+        if e == "pe":
+            if not o["stop"]:
+                shut.add(o["bank"])
+            elif not o["start"]:
+                shut.discard(o["bank"])
         pool[e].remove(i); order[e].append(i); seq.append(i)
-        free[e] = t0 + ops[i]["cost"]
-        fin = free[e] + ops[i].get("lat", 0) + lam
+        free[e] = t0 + o["cost"]
+        fin[i] = free[e] + o.get("lat", 0)
         for j in succ[i]:
-            ready[j] = max(ready[j], fin); left[j] -= 1
+            ready[j] = max(ready[j], fin[i] + (0 if e == "pe" and ops[j]["eng"] == "pe" else lam)); left[j] -= 1
             if not left[j]:
                 pool[ops[j]["eng"]].append(j)
-    return order, seq
+    return max(fin), order, seq, deps
 
 
-OPS, DSEMS, TOP, AP = build(P)
-ORDER, SEQ = schedule(OPS, P)
+def plan(P):
+    ops, sems, top = build(P)
+    best = schedule(ops, P, 1)
+    for seed in range(2, 2 + P["tries"]):
+        best = min(best, schedule(ops, dict(P, jit=400), seed), key=lambda x: x[0])
+    return (ops, sems, top) + best
+
+
+OPS, DSEMS, TOP, SPAN, ORDER, SEQ, DEPS = plan(P)
 SCRATCH = {ARENA[k]: ("sbuf", [128, TOP[k]], k) for k in ARENA}
 SCRATCH["tb"] = ("sbuf", [128, W + 16], "bfloat16")
+SCRATCH["t2"] = ("sbuf", [128, W + 16], "bfloat16")
+SCRATCH["sx"] = ("dram", [NR - 1, 128, W // NR], "bfloat16")
+SCRATCH["lx"] = ("dram", [NR - 1, 128, W // NR], "bfloat16")
 for _b in range(8):
     SCRATCH["ps%d" % _b] = ("psum", [128, 512], "float32")
 SEMAPHORES = ["cv", "cs", "cpe", "cg", "sent"] + DSEMS
@@ -510,7 +653,7 @@ def rank_program(g, core, T, topo):
     for i in SEQ:
         o, sn = OPS[i], seen[OPS[i]["eng"]]
         waits[i] = []
-        for j in sorted(o["dep"], key=lambda j: -pos[j]):
+        for j in sorted(DEPS[i], key=lambda j: -pos[j]):
             s, v = mark[j]
             if (o["eng"] == "pe" and OPS[j]["eng"] == "pe") or sn.get(s, 0) >= v:
                 continue
@@ -532,11 +675,11 @@ def rank_program(g, core, T, topo):
                     rid, pid = topo.addr(d, core)
                     eng = split(core, d, len(its))[k]
                     tr.append(RemoteDMATransfer(dst_ids=[DstId(rid=rid, pnc=pid)], dma_engine_mask=sum(1 << x for x in eng),
-                                                remote_sem=T.sem[o["sem"]], src=AP(T, src), dst=AP(T, dst)))
+                                                remote_sem=T.sem[o["sem"]], src=src(T), dst=dst(T)))
                     sent += len(eng)
                 g.remote_dma_fused(tr, local_sem=T.sem.sent)
             else:
-                o["fn"](g, T).then_inc(T.sem[mark[i][0]], 16 if "sem" in o else 1)
+                o["fn"](g, T, rank).then_inc(T.sem[mark[i][0]], 16 if "sem" in o else 1)
     g.wait_ge(T.sem.sent, sent)
     for s, v in list(total.items()) + [m for i, m in mark.items() if "sem" in OPS[i]]:
         if (s, v) not in waited:

@@ -7,13 +7,15 @@ NCH = LN // L
 BLK = 128 // NR
 BIG = 8192.0
 P = dict(
-    nd=(24, 24, 24),
-    vp=(16, 16, 8),
-    xp=(("s", 32),) * 2,
+    nd=(24, 32, 24),
+    vp={32: (16, 16), 40: (20, 12, 8), 48: (16, 16, 16), 56: (24, 16, 16), 64: (24, 24, 16)},
+    xp=(("s", 16), ("s", 24), ("s", 24)),
     fp=(("s", 24), ("v", 16), ("s", 24)),
     xp0=(("v", 32), ("s", 32)),
-    bias=(2500, 0), tries=60, look=250, gam=3.0, fit=30,
-    cyc=0.9, pe=.45, gat=1.56, lam=190, issue=1300, fly=3000, dma=2500, rate=30.0,
+    on=dict(ux="s", uy="v", uf="v", g="v", par="v", z="s", hi="v", w="s", m="v"),
+    bias=(2500, 0), tries=300, again=20, jit_=100, look=250, gam=6.0, fit=80,
+    seed=0, dpre=False, also=(dict(cyc=1.1, pe=.55, gat=1.7, lam=200), dict(cyc=.83, pe=.5, gat=1.3, lam=230)),
+    cyc=0.87, pe=.46, gat=1.56, lam=190, issue=1300, fly=3000, dma=2500, rate=30.0,
 )
 
 SIZE = {"bfloat16": 2, "float16": 2, "float32": 4, "int32": 4, "uint16": 2}
@@ -25,6 +27,8 @@ def ap(T, v, r):
         return v
     if v[0] == "ind":
         return ap(T, v[1], r).indirect(ap(T, v[2], r))
+    if len(v) == 6:
+        return T[v[0]][v[4]:v[5], v[1]:v[2]]
     if len(v) == 5:
         a = v[1] + v[4](r)
         return T[v[0]][:, a:a + 128]
@@ -35,7 +39,7 @@ def ap(T, v, r):
 
 def build(P):
     top = {k: 0 for k in ARENA}
-    ops, sems, cur = [], [], [0]
+    ops, sems, cur = [], [], [0, -1, 0]
     cyc, pec = P["cyc"], P["pe"]
 
     def new(dt, n):
@@ -65,7 +69,8 @@ def build(P):
                 r += [v[1], v[2]] if v[0] == "ind" else [v]
                 if v[0] == "ind" and v[1][0] == "t2":
                     r += [part(s) for s in range(NR)]
-        ops.append(dict(eng=eng, fn=fn, rd=r, wr=list(wr), cost=cost, ch=cur[0], **kw))
+        ops.append(dict(eng=eng, fn=fn, rd=r, wr=list(wr), cost=cost, ch=cur[0], key=(cur[1], cur[2]), **kw))
+        cur[2] += 1
         return len(ops) - 1
 
     def vcost(out, in0, k):
@@ -112,11 +117,11 @@ def build(P):
             last = None
             for i, (o, lhs, rhs) in enumerate(terms):
                 last = g.tensor.matmul(ap(T, o, r), ap(T, lhs, r), ap(T, rhs, r),
-                                       start and i == 0, stop and i == len(terms) - 1)
+                                       start and i == 0, stop and o[4:] not in [x[0][4:] for x in terms[i + 1:]])
             return last
         c, rd = 30, []
         for o, lhs, rhs in terms:
-            c += max(64, cnt(rhs)) * (4 if rhs[0] == "af" else 1) * pec
+            c += max(min(64, cnt(lhs)), cnt(rhs)) * (4 if rhs[0] == "af" else 1) * pec
             rd += [lhs, rhs]
         tok = ("open" + terms[0][0][0], 0, 1, 1)
         return add("pe", fn, rd + ([] if start else [tok]), [o for o, _, _ in terms] + ([] if stop else [tok]), c,
@@ -162,10 +167,11 @@ def build(P):
     dma("y", lambda T, r: T.t2[0:BLK, 16:16 + W], lambda T, r: T.xt[BLK * r:BLK * (r + 1), :], [], [part(0)],
         P["dma"] + 4000, after=[first])
     cur[0] = 0
-    row, rowg = new(bf, 144), new(bf, 128)
-    ci, cj = new(i32, 16), new(i32, 3)
-    iota(ci, [[-1, 16]], 16, 1); iota(row, [[1, 144]], 0, 0); iota(cj, [[BLK, 3]], 128 - BLK, 1)
-    iota(rowg, [[16, 8], [0, 16]], 0, 0)
+    row128, rowg, rowp = new(bf, 128), new(bf, 128), new(bf, 128)
+    ci, cj, cip, cjp = new(i32, 16), new(i32, 3), new(i32, 16), new(i32, 3)
+    iota(ci, [[-1, 16]], 16, 1); iota(row128, [[1, 128]], 0, 0); iota(cj, [[BLK, 3]], 128 - BLK, 1)
+    iota(rowg, [[16, 8], [0, 16]], 0, 0); iota(rowp, [[1, 16], [16, 8]], 0, 0)
+    iota(cip, [[-8, 16]], 128, 1); iota(cjp, [[BLK, 3]], 128 - BLK, 16)
     SP = max(n for _, n in P["fp"])
     reset = new(bf, 16 * SP)
     iota(reset, [[0, SP], [256, 16]], 0, 0)
@@ -173,33 +179,39 @@ def build(P):
     iota(wpi, [[-BLK, 5], [-1024, 4], [-1, BLK]], BLK, 1)
     ci2, cj2, c16 = new(i32, 16), new(i32, 3), new(f32, 3)
     ts(ci2, ci, 15, A.bitwise_and); ts(cj2, cj, 112, A.bitwise_and); cp(c16, cj2)
-    g16 = {sh: sub(c16, sh + 1, sh + 2) for sh in (-1, 0, 1)}
-    col = {sh: new(f32, 16) for sh in g16}
-    c15 = new(f32, 1)
-    ts(col[0], ci2, g16[0], A.add); ts(c15, g16[0], 15.0, A.add)
-    row128 = sub(row, 0, 128)
+    cip2, cjp2, c16p = new(i32, 16), new(i32, 3), new(f32, 3)
+    ts(cip2, cip, 3, A.arith_shift_right, 15, A.bitwise_and); ts(cjp2, cjp, 112, A.bitwise_and); cp(c16p, cjp2)
+    g16 = {(sh, p): sub((c16, c16p)[p], sh + 1, sh + 2) for sh in (-1, 0, 1) for p in (0, 1)}
+    col = {key: new(f32, 16) for key in g16}
+    c24 = new(f32, 1)
+    ts(col[0, 0], ci2, g16[0, 0], A.add); ts(c24, g16[0, 0], 1.0 / 16, A.mult, 24.0, A.add)
     made = {}
 
     def cmp_mat(src, c, op, scale, dt=bf):
-        m = new(dt, cnt(src))
+        m, keep = new(dt, cnt(src)), cur[1:]
+        cur[1:] = [-2, len(ops)]
         ts(m, src, c, op, scale, A.mult)
+        cur[1:] = keep
         return m
 
-    def rot(r, scale=1.0, sh=0, dt=bf):
-        key = ("rot", r % 16, scale, sh, dt)
+    def rot(r, scale=1.0, sh=0, dt=bf, pin=0, pout=0):
+        key = ("rot", r % 16, scale, sh, dt, pin, pout)
         if key not in made:
-            made[key] = cmp_mat(row128, sub(col[sh], r % 16, r % 16 + 1), A.is_equal, scale, dt)
+            made[key] = cmp_mat(rowp if pout else row128, sub(col[sh, pin], r % 16, r % 16 + 1), A.is_equal, scale, dt)
         return made[key]
 
-    def grp(scale, sh=0):
-        key = ("grp", scale, sh)
+    def grp(scale, sh=0, pin=0):
+        key = ("grp", scale, sh, pin)
         if key not in made:
-            made[key] = cmp_mat(rowg, g16[sh], A.is_equal, scale)
+            made[key] = cmp_mat(rowg, g16[sh, pin], A.is_equal, scale)
         return made[key]
+
+    def mrot(r, scale, sh=0, pout=0):
+        return rot(r, scale, sh, bf, 1, pout)
 
     I1, I2080, I3232 = rot(0), rot(0, 2080.0), rot(0, 3232.0)
-    k1, khalf, k3072 = new(bf, L), new(bf, L), new(bf, L)
-    fill(k1, 1.0)
+    k0, k1, khalf, k3072 = new(bf, L), new(bf, L), new(bf, L), new(bf, L)
+    fill(k1, 1.0); fill(k0, 0.0)
     IW = 168
     IB, SB = new(fh, 4 * IW), new(fh, 4 * IW)
     fill(sub(IB, 5 * LN, 4 * IW), 0.0)
@@ -209,12 +221,14 @@ def build(P):
     for c in range(NCH):
         st.append(dict(
             x=new(bf, 16 * L), d=[new(bf, 16 * L) for _ in range(NS)], a=[new(bf, 16 * L) for _ in range(NS)],
-            fin=new(bf, 16 * L), sc=new(bf, 16 * L), pr=new(f32, L), s=new(i32, L), sx=new(i32, 2 * L),
+            fin=new(bf, 16 * L), sc=new(bf, 16 * L), s=new(i32, 3 * L), sx=new(i32, 2 * L),
             ix=new(i32, L), ux=new(u16, L), idx=new(i32, 3 * L), uy=[new(u16, L) for _ in range(NS)],
-            rf=[new(fh, 4 * L) for _ in range(NS + 1)], m=new(bf, 3 * L), sel=new(fh, 2 * L), eq=new(bf, 4 * L),
+            rf=new(fh, 4 * L), m=new(bf, 3 * L), sel=new(fh, 2 * L), eq=new(bf, 4 * L), ef=new(bf, 3 * L),
+            pb=[new(bf, 6 * L) for _ in range(2)], rb=[new(fh, 6 * L) for _ in range(NS)], fb=new(f32, 3 * L),
+            F=[new(fh, L) for _ in range(NS)],
             e3=new(f32, 3 * L), s3=new(i32, 3 * L), g2=new(i32, L), fp=new(f32, 3 * L), uf=new(u16, L), fs=new(fh, 4 * L),
-            hi=new(bf, 2 * L), tmp=new(fh, 4 * L), pb=[new(bf, 2 * L) for _ in range(2)], zf=new(bf, L), gb=new(fh, 2 * L),
-            q=sub(IB, 4 * L * c, 4 * L * (c + 1)), z=new(bf, L), cn=None, par=None))
+            hi=new(bf, 2 * L), tmp=new(fh, 4 * L), zf=new(bf, L), gb=new(fh, 2 * L),
+            q=sub(IB, 4 * L * c, 4 * L * (c + 1)), z=new(bf, L), cn=k0, par=None, shut=[]))
     ts(names[0], hi, 2048.0, A.subtract)
     for c, S in enumerate(st):
         fill(S["gb"], 0.0)
@@ -226,43 +240,57 @@ def build(P):
     ts(thc[0], thi, 2048.0, A.subtract)
     NI, BI, NB, ONE, NONE = rot(0, -1.0), rot(0, BIG), rot(0, -BIG), grp(1.0), grp(-1.0)
     fill(khalf, -0.5); fill(k3072, 3072.0)
+    kn = new(bf, L)
+    fill(kn, -2080.0)
     for S in st:
-        fill(S["pb"][0], 0.0); fill(S["pb"][1], 0.0)
-    B1 = cmp_mat(row, c15, A.is_equal, 1.0)
-    LTa = cmp_mat(row128, sub(col[0], 0, 1), A.is_lt, -2 * BIG)
-    LTb = cmp_mat(row128, g16[0], A.is_lt, 2 * BIG)
+        for b in S["pb"]:
+            fill(b, 0.0); fill(sub(b, 5, 6 * L, 6), 3232.0)
+        for b in S["rb"]:
+            fill(b, 0.0)
+        fill(S["ef"], 0.0); fill(sub(S["ef"], 2, 3 * L, 3), 3232.0)
+    B1 = cmp_mat(sub(row128, 0, 56), c24, A.is_equal, 1.0)
+    LTa = cmp_mat(row128, sub(col[0, 0], 0, 1), A.is_lt, -2 * BIG)
+    LTb = cmp_mat(row128, g16[0, 0], A.is_lt, 2 * BIG)
+    ts(col[0, 1], cip2, g16[0, 1], A.add)
     for n in ("tb", "t2"):
         fill((n, 0, 16, 1), 0.0)
     for S in st:
         fill(S["eq"], 0.0); fill(S["e3"], 0.0)
-    k1536, k1024, kq = new(bf, L), new(bf, L), new(bf, 4 * L)
-    fill(k1536, 1536.0); fill(k1024, 1024.0); fill(kq, 0.25)
-    bias = new(f32, 3)
-    b32, bX, bN = sub(bias, 0, 1), sub(bias, 1, 2), sub(bias, 2, 3)
-    fill(b32, 32.0); fill(bX, 2048.0); fill(bN, -2048.0)
-    ts(col[1], ci2, g16[1], A.add); ts(col[-1], ci2, g16[-1], A.add)
+    k1536, k1024, kq, k3q = new(bf, L), new(bf, L), new(bf, L), new(bf, L)
+    fill(k1536, 1536.0); fill(k1024, 1024.0); fill(kq, 0.25); fill(k3q, 0.75)
+    bias = new(f32, 5)
+    BIAS = {v: sub(bias, i, i + 1) for i, v in enumerate((32.0, 2048.0, -2048.0, -2080.0, 16.0 - 2 * BIG))}
+    for v in BIAS:
+        fill(BIAS[v], v)
+    for key in col:
+        if key[0]:
+            ts(col[key], (ci2, cip2)[key[1]], g16[key], A.add)
+    MB, MN, MN2 = mrot(0, BIG), mrot(0, -BIG), mrot(0, -2 * BIG)
     ts(WP, wpi, 0.0, A.is_equal)
-    IF = rot(0, 1.0, 0, f32)
+    IF, NB2 = rot(0, 1.0, 0, f32), rot(0, -2 * BIG)
     Q = [rot(-t) for t in range(NV)]
-    thb = new(f32, NV)
-    H, TR, wtmp = [names[0]] + [None] * (NV - 1), [None] * NV, new(bf, 128)
+    QP = [rot(-t, pout=1) for t in range(NV)]
+    thb = thv = new(f32, NV)
+    H, TR = [names[0]] + [None] * (NV - 1), [None] * NV
 
     def move(src, dst):
         return (WP[0], WP[1], WP[2], 1, lambda r: 128 + 128 * src(r) - BLK * dst(r))
 
     def thresholds(bank, ts_):
         r = ps(bank, 504 + ts_[0], 505 + ts_[-1])
-        mm([(ps(bank, 504 + t, 505 + t), Q[t], thc[t > 0]) for t in ts_])
-        ts(sub(thb, ts_[0], ts_[-1] + 1), r, 256.0, A.mult, 256.0 * 2048 - 128, A.add)
+        mm([(ps(bank, 504 + t, 505 + t), QP[t], thc[t > 0]) for t in ts_])
+        if P["on"].get("m", "s") == "v":
+            ts(sub(thv, ts_[0], ts_[-1] + 1), r, 2048.0, A.add)
+        else:
+            ts(sub(thb, ts_[0], ts_[-1] + 1), r, 256.0, A.mult, 256.0 * 2048 - 128, A.add)
 
     def make_tr(t, bank):
         TR[t] = new(bf, 128)
-        r = ps(bank, 384, 512)
+        r, wtmp = ps(bank, 384, 512), new(bf, 128)
         mm([(r, LTa, Q[t]), (r, LTb, Q[t]), (r, BI, Q[t])])
-        act(wtmp if t else TR[t], r, AF.Copy)
-        if t:
-            mm([(r, Q[t], wtmp)])
-            act(TR[t], r, AF.Copy)
+        act(wtmp, r, AF.Copy)
+        mm([(r, QP[t], wtmp)])
+        act(TR[t], r, AF.Copy)
 
     def make_names(t, bank):
         H[t] = new(fh, LN)
@@ -279,21 +307,30 @@ def build(P):
         send([(lambda T, k=k: ap(T, sub(out, (k - 1) * w, k * w), 0), lambda T, k=k: ap(T, sub(land, (k - 1) * w, k * w), 0), k)
               for k in range(1, NR)], [out], [land], 128 * w * 2 * 2)
 
-        def unpack(reg, quarters):
-            terms = []
+        def unpack(reg, quarters, ahead=True):
+            own, came = [], []
             for n, a in enumerate(quarters):
                 o = sub(reg, n * w, (n + 1) * w)
-                terms.append((o, move(lambda r: from_blk(r, 0), lambda r, a=a: to_blk(r, 0, a)), sub(src, a * w, (a + 1) * w)))
-                terms += [(o, move(lambda r, a=a: a, lambda r, a=a, k=k: to_blk(r, k, a)), sub(land, (k - 1) * w, k * w))
-                          for k in range(1, NR)]
-            mm(terms)
+                own.append((o, move(lambda r: from_blk(r, 0), lambda r, a=a: to_blk(r, 0, a)), sub(src, a * w, (a + 1) * w)))
+                came += [(o, move(lambda r, a=a: a, lambda r, a=a, k=k: to_blk(r, k, a)), sub(land, (k - 1) * w, k * w))
+                         for k in range(1, NR)]
+            if ahead:
+                mm(own, stop=False); mm(came, start=False)
+            else:
+                mm(own + came)
         return unpack
 
     def scopy(out, in_):
         act(out, in_, AF.Copy)
 
+    def shift(name, out, in_, add_=0.0):
+        if P["on"].get(name, "s") == "v":
+            return ts(out, in_, add_, A.add)
+        return act(out, in_, AF.Identity, bias=BIAS[add_]) if add_ else act(out, in_, AF.Copy)
+
     thresholds(7, [0])
-    make_tr(0, 7)
+    for t in range(NV):
+        make_tr(t, 3 + 4 * (t % 2))
     cur[0] = 2
     dealt = ship(IB, IW, ps(4, 0, 3 * IW), lambda r, k: (r + k) % NR, lambda r, k, a: -k % NR, scopy)
 
@@ -315,10 +352,10 @@ def build(P):
     def visit(c, t):
         S = st[c]
         b0, b1, b2, b3 = 4 * c, 4 * c + 1, 4 * c + 2, 4 * c + 3
-        lay = dict(d=(b0, 0), cn=(b0, 1), zf=(b0, 2), z=(b0, 3), hi=(b0, 4), T01=(b0, 4), fm=(b0, 1), w=(b0, 6),
-                   sel=(b1, 0), T23=(b1, 2), lx=(b1, 2), dg=(b1, 4), ly=(b1, 5), diff=(b1, 6),
-                   dr=(b2, 0), par=(b2, 0), g3=(b2, 4),
-                   D=(b3, 0), fid=(b3, 6), hd=(b3, 0), A=(b3, 4), qd=(b3, 0))
+        lay = dict(d=(b0, 0), cn=(b0, 1), zf=(b0, 2), z=(b0, 3), hi=(b3, 4), T01=(b0, 4), fm=(b0, 1), w=(b0, 5), diff=(b0, 6),
+                   sel=(b1, 0), T23=(b1, 2), lx=(b1, 2), dg=(b1, 4), ly=(b1, 5), dif1=(b1, 6),
+                   dr=(b2, 0), par=(b2, 0), g3=(b2, 5),
+                   D=(b3, 0), fid=(b3, 7), A=(b3, 0), qd=(b3, 0))
 
         def pr(name, a=0, b=1, o=0, st=1):
             bank, u = lay[name]
@@ -326,88 +363,102 @@ def build(P):
         last = t == NV - 1
         table, win0 = tabs[t > 0], wins[t > 0]
         nr, ns = (NV - 1, 0) if last else (-1, int(t > 0))
-        if c == 0 and not last:
-            make_tr(t + 1, b3)
         if c == 1 and 0 < t < NV - 1:
             make_names(t + 1, b3)
         Ht, G, z, x, m, q = sub(H[t], L * c, L * c + L), sub(S["gb"], 1, 2 * L, 2), S["z"], S["x"], S["m"], S["q"]
         mm([(pr("lx", 0, 2, 0, 2), I1, Ht), (pr("lx", 0, 2, 0, 2), I3232, k1), (pr("lx", 0, 2, 1, 2), I2080, Ht)])
         fma(S["sx"], S["gb"], pr("lx", 0, 2))
         ts(S["ix"], sub(S["sx"], 1, 2 * L, 2), 5, A.arith_shift_right, W - 1, A.bitwise_and)
-        cp(S["ux"], S["ix"])
+        shift("ux", S["ux"], S["ix"])
         xp = P["xp" if t else "xp0"]
         for (e, _), (a, b) in zip(xp, pieces([n for _, n in xp])):
             gather(e, sub(x, 16 * a, 16 * b), table, sub(S["ux"], a, b))
         qv = [[sub(q, 2 * L * b + i, 2 * L * (b + 1), 2) for b in range(2)] for i in range(2)]
-        mm([x_ for i in range(2) for x_ in ((pr("qd", 2 * i, 2 * i + 2, 0, 2), I1, qv[i][0]),
-                                            (pr("qd", 2 * i, 2 * i + 2, 0, 2), NI, qv[i][1]),
-                                            (pr("qd", 2 * i, 2 * i + 2, 1, 2), I1, qv[i][0]))])
+
+        def two(name, i):
+            return pr(name, 0, 2, i, 2)
+
+        def three(name, i):
+            return pr(name, 2, 5, i, 3)
+
+        def consts(name):
+            return [(three(name, 1), I2080, k1), (three(name, 2), I3232, kn)]
+
+        def renamed(s, name, er, ef):
+            fma(S["fb"], ef, pr(name, 2, 5))
+            fma(sub(S["rb"][s], 1, 6 * L, 3), er, pr(name, 0, 2))
+            fma(S["s"], sub(S["rb"][s], 0, 6 * L, 2), S["fb"])
+            shift("F", S["F"][s], sub(S["fb"], 1, 3 * L, 3), -2080.0)
+        mm(consts("qd") + [x_ for f, v in zip((two, three), qv)
+                           for x_ in ((f("qd", 0), I1, v[0]), (f("qd", 0), NI, v[1]), (f("qd", 1), I1, v[0]))])
         po, pb = pr("par"), S["pb"][t % 2]
         mm([(po, I1, khalf)], stop=False)
         mm([(po, ONE, z), (po, BI, k3072), (po, NB, k3072), (po, NONE, z)], start=False)
-        par_before, S["par"] = S["par"], sub(pb, 1, 2 * L, 2)
-        scopy(S["par"], po)
-        for i in range(2):
-            fma(sub(S["rf"][0], 2 * L * i, 2 * L * (i + 1)), pb, pr("qd", 2 * i, 2 * i + 2))
+        par_before, S["par"] = S["par"], sub(pb, 3, 6 * L, 6)
+        shift("par", S["par"], po)
+        renamed(0, "qd", sub(pb, 0, 6 * L, 3), sub(pb, 1, 6 * L, 2))
         msg = new(fh, 6 * L if last else 4 * L) if t == 0 or last else None
         if t == 0:
             scopy(sub(msg, 3 * L, 4 * L), po)
         mm([(pr("w"), grp(1.0, ns), z)])
-        act(sub(S["e3"], 2, 3 * L, 3), pr("w"), AF.Identity, bias=b32)
+        shift("w", sub(S["e3"], 2, 3 * L, 3), pr("w"), 32.0)
         ms = [sub(m, s * L, (s + 1) * L) for s in range(NS)]
         fs = S["fs"]
         fq = [sub(fs, i * L, (i + 1) * L) for i in range(4)]
         for s in range(NS):
-            rf, idx = S["rf"][s], sub(S["idx"], s * L, (s + 1) * L)
+            idx = sub(S["idx"], NS - 1 - s, NS * L, NS)
             end = s == NS - 1
-            R, F = names_tails(rf)
-            mm([(pr("ly"), I2080, R), (pr("ly"), I3232, F)])
-            tt(S["pr"], R, F, A.mult)
-            tt(S["s"], S["pr"], pr("ly"), A.add)
-            ts(idx, S["s"], 5, A.arith_shift_right, W - 1, A.bitwise_and)
-            cp(S["uy"][s], idx)
+            R, F = sub(S["rb"][s], 4, 6 * L, 6), S["F"][s]
+            ts(idx, sub(S["s"], 2, 3 * L, 3), 5, A.arith_shift_right, W - 1, A.bitwise_and)
+            shift("uy", S["uy"][s], idx)
             early = []
             if end:
                 early.append(mm([(pr("T01", i, i + 1), lhs, rhs) for i in range(2)
-                                 for lhs, rhs in ((rot(5 * i - 10), F), (BI, ms[i]))]))
+                                 for lhs, rhs in ((rot(5 * i - 10), F), (MB, ms[i]))]))
                 ts(sub(fs, 0, 2 * L), pr("T01", 0, 2), BIG, A.subtract, -2048.0, A.max)
-                early.append(mm([(pr("fm", 0, 1), I1, ms[0]), (pr("fm", 1, 2), I1, ms[1]), (pr("fm", 2, 3), I1, k1),
-                                 (pr("fm", 2, 3), NI, ms[0]), (pr("fm", 2, 3), NI, ms[1])]))
-                tt(S["fp"], S["idx"], pr("fm", 0, 3), A.mult)
+                fm = [pr("fm", 0, 3, i, 3) for i in range(3)]
+                early.append(mm([(fm[0], NB2, k1), (fm[1], BI, k1), (fm[1], MN2, ms[1]), (fm[2], MB, ms[1]), (fm[2], MN2, ms[0])]))
+                scan(S["fp"], pr("fm", 0, 3), S["idx"], A.add, A.max)
             d, a_, uy, nd = S["d"][s], S["a"][s], S["uy"][s], P["nd"][s]
             nv = L - nd
             ya, pD = sub(d, 16 * nv, 16 * L), pr("D", 0, 16.0 * nd / L)
-            act(ya, ("ind", table, sub(uy, nv, L)), AF.Copy)
-            mm([(pD, NI, sub(x, 16 * nv, 16 * L))], stop=False)
-            mm([(pD, I1, ya)], start=False)
-            act(sub(a_, 16 * nv, 16 * L), pD, AF.Abs)
-            vp = list(P["vp"]); vp[0] += nv - sum(vp)
-            for a, b in pieces(vp):
+            if nd:
+                act(ya, ("ind", table, sub(uy, nv, L)), AF.Copy)
+                mm([(pD, NI, sub(x, 16 * nv, 16 * L))], stop=False)
+                mm([(pD, I1, ya)], start=False)
+                act(sub(a_, 16 * nv, 16 * L), pD, AF.Abs)
+            for a, b in pieces(P["vp"][nv]):
                 tt(sub(d, 16 * a, 16 * b), ("ind", table, sub(uy, a, b)), sub(x, 16 * a, 16 * b), A.subtract)
                 act(sub(a_, 16 * a, 16 * b), sub(d, 16 * a, 16 * b), AF.Abs)
-            pre = [(NI, S["cn"])] if t else []
-            pre += [(BI, ms[s0]) for s0 in range(s)] + [(rot(5 * (s - s0), BIG), ms[s0]) for s0 in range(s)]
+            pre = [(rot(0, -1.0, pout=1), S["cn"])]
+            pre += [(mrot(r, BIG, 0, 1), ms[s0]) for s0 in range(s) for r in (0, 5 * (s - s0))]
             if pre:
-                mm([(pr("d"), lhs, rhs) for lhs, rhs in pre], stop=False, after=early)
-            mm([(pr("d"), sub(B1, 15 - k, 143 - k), sub(a_, k, 16 * L, 16)) for k in range(16)], start=not pre)
-            act(ms[s], pr("d"), AF.Sigmoid, bias=sub(thb, t, t + 1), scale=-256.0)
+                mm([(pr("d"), lhs, rhs) for lhs, rhs in pre], stop=False, after=early + S["shut"])
+            for h in range(2):
+                mm([(pr("d", h / 2, (h + 1) / 2) + (32 * (k // 4), 32 * (k // 4 + 1)), sub(B1, 24 - 8 * (k % 4), 56 - 8 * (k % 4)),
+                     sub(a_, 8 * L * h + k, 8 * L * (h + 1), 16)) for k in range(16)], start=not pre and not h, stop=h == 1)
+            if P["on"].get("m", "s") == "v":
+                matched = ts(ms[s], pr("d"), sub(thv, t, t + 1), A.is_lt)
+            else:
+                matched = act(ms[s], pr("d"), AF.Sigmoid, bias=sub(thb, t, t + 1), scale=-256.0)
             rename = not end or t > 0
             xs = -1 if end else 0
             RT = rot(6, 1.0, -1) if end and rename else rot(5)
             if end:
-                mm([(pr("fid"), IF, sub(S["fp"], i * L, (i + 1) * L)) for i in range(NS)]
-                   + [(pr("fid"), BI, ms[0]), (pr("fid"), BI, ms[1])], stop=False)
-                mm([(pr("fid"), BI, ms[2])], start=False)
-                ts(S["uf"], pr("fid"), 16.0 - BIG, A.add)
+                mm([(pr("fid"), IF, sub(S["fp"], 2, 3 * L, 3)), (pr("fid"), mrot(0, 2 * BIG), ms[0]), (pr("fid"), MB, ms[1])],
+                   stop=False)
+                mm([(pr("fid"), MB, ms[2])], start=False)
+                shift("uf", S["uf"], pr("fid"), 16.0 - 2 * BIG)
                 for (e, _), (a, b) in zip(P["fp"], pieces([n for _, n in P["fp"]])):
                     gather(e, sub(S["fin"], 16 * a, 16 * b), win0, sub(S["uf"], a, b))
                     scan(sub(S["sc"], 16 * a, 16 * b), sub(reset, 0, 16 * (b - a)), sub(S["fin"], 16 * a, 16 * b), A.min, A.max)
             sR, sH = sub(S["sel"], 0, L), sub(S["sel"], L, 2 * L)
             T2, T3 = pr("T23", 0, 1), pr("T23", 1, 2)
             mm([(pr("sel", 0, 1), I1, R), (pr("sel", 1, 2), I1, Ht)]
-               + ([(T2, I1, F), (T3, I1, G), (T3, BI, k1), (T3, NB, ms[0]), (T3, NB, ms[1])] if end else []), stop=False)
+               + ([(T2, I1, F), (T3, I1, G), (T3, BI, k1), (T3, MN, ms[0]), (T3, MN, ms[1])] if end else []),
+               stop=False)
             mm([(pr("sel", 0, 1), TR[t], ms[s]), (pr("sel", 1, 2), TR[t], ms[s])]
-               + ([(T2, BI, ms[s]), (T3, NB, ms[s])] if end else []), start=False)
+               + ([(T2, MB, ms[s]), (T3, MN, ms[s])] if end else []), start=False)
             ts(S["sel"], pr("sel", 0, 2), BIG, A.subtract, -2048.0, A.max)
             if end:
                 ts(sub(fs, 2 * L, 4 * L), pr("T23", 0, 2), BIG, A.subtract, -2048.0, A.max)
@@ -415,18 +466,22 @@ def build(P):
             f1 = rot(nr, 1.0, ns) if end else None
             pre, post = [], []
             if rename:
-                pre += [(pr("dr", 2 * i, 2 * i + 2, 1, 2), RT, (R, F)[i]) for i in range(2)]
-                post += [(pr("dr", 2 * i, 2 * i + 2, 0, 2), lhs, rhs) for i in range(2)
+                dr = [[two("dr", i), pr("dr", 2, 4, i, 2) if end else three("dr", i)] for i in range(2)]
+                pre += [(dr[1][i], RT, (R, F)[i]) for i in range(2)] + ([] if end else consts("dr"))
+                post += [(dr[0][i], lhs, rhs) for i in range(2)
                          for lhs, rhs in ((grp(1.0, xs), sH), (grp(-1.0, xs), sR))]
             if end:
                 pre += [(g3[1], NB, khalf), (g3[1], f1, fq[0]), (g3[1], f1, fq[1]),
                         (g3[2], grp(2048.0, ns), z), (g3[2], NB, k1024)]
             mm(pre, stop=False)
-            if rename:
-                mm([(pr("diff", i, i + 1), lhs, rhs) for i in range(2)
+            if rename and not P["dpre"]:
+                mm([(pr("dif1", i, i + 1), lhs, rhs) for i in range(2)
                     for lhs, rhs in ((RT, (R, F)[i]), (grp(-1.0, xs), sR))])
+            elif rename:
+                mm([(pr("diff", i, i + 1), RT, (R, F)[i]) for i in range(2)], stop=False, after=[matched])
+                S["shut"] = [mm([(pr("diff", i, i + 1), grp(-1.0, xs), sR) for i in range(2)], start=False)]
             if end:
-                mm([(pr("dg"), rot(nr, -BIG, ns), ms[i]) for i in range(NS)] + [(pr("dg"), f1, fq[i]) for i in range(NS)]
+                mm([(pr("dg"), mrot(nr, -BIG, ns), ms[i]) for i in range(NS)] + [(pr("dg"), f1, fq[i]) for i in range(NS)]
                    + [(pr("dg"), grp(-1.0, ns), sR)])
                 post += [(g3[0], grp(1.0, ns), sH), (g3[0], grp(-1.0, ns), sR), (g3[1], f1, fq[2]),
                          (g3[2], rot(nr, 32.0, ns), fq[3])]
@@ -435,33 +490,42 @@ def build(P):
                 ts(sub(S["e3"], 1, 3 * L, 3), pr("dg"), 13 * 2048.0 - BIG, A.is_equal)
                 fma(S["s3"], S["e3"], pr("g3", 0, 3))
                 ts(S["g2"], sub(S["s3"], 2, 3 * L, 3), 5, A.arith_shift_right, W - 1, A.bitwise_and)
-                ts(sub(msg, 4 * L, 5 * L) if last else sub(msg, 0, L) if t == 0 else G, S["g2"], 2048.0, A.subtract)
-            if rename:
-                ts(sub(S["eq"], 1, 4 * L, 2), pr("diff", 0, 2), 15 * 2048.0, A.is_equal)
-                fma(S["rf"][s + 1], S["eq"], pr("dr", 0, 4))
-        mm([(pr("zf"), I1, z)] + [(pr("zf"), grp(-BIG), ms[i]) for i in range(NS)])
-        act(S["zf"], pr("zf"), AF.Relu)
+                shift("g", sub(msg, 4 * L, 5 * L) if last else sub(msg, 0, L) if t == 0 else G, S["g2"], -2048.0)
+            df = "diff" if P["dpre"] else "dif1"
+            if not end:
+                ts(sub(S["ef"], 1, 3 * L, 3), pr(df, 1, 2), 15 * 2048.0, A.is_equal)
+                ts(sub(S["eq"], 1, 2 * L, 2), pr(df, 0, 1), 15 * 2048.0, A.is_equal)
+                renamed(s + 1, "dr", sub(S["eq"], 0, 2 * L), S["ef"])
+            elif rename:
+                ts(sub(S["eq"], 1, 4 * L, 2), pr(df, 0, 2), 15 * 2048.0, A.is_equal)
+                fma(S["rf"], S["eq"], pr("dr", 0, 4))
+        mm([(pr("zf"), I1, z)] + [(pr("zf"), grp(-BIG, 0, 1), ms[i]) for i in range(NS)])
+        if P["on"].get("zf", "s") == "v":
+            ts(S["zf"], pr("zf"), 0.0, A.max)
+        else:
+            act(S["zf"], pr("zf"), AF.Relu)
         early = []
         if not last:
             S["cn"] = sub(msg, 2 * L, 3 * L) if t == 0 else new(bf, L)
-            early.append(mm([(pr("cn"), grp(1.0, ns), ms[i]) for i in range(NS)]))
-            scopy(S["cn"], pr("cn"))
+            early.append(mm([(pr("cn"), grp(1.0, ns, 1), ms[i]) for i in range(NS)]))
+            shift("cn", S["cn"], pr("cn"))
         if t:
-            early.append(mm([(pr("hi", b, b + 1), rot(-5 * i, BIG, -1), ms[i]) for b in range(2) for i in range(NS)]
-                            + [(pr("hi", 0, 1), NB, par_before), (pr("hi", 1, 2), BI, par_before), (pr("hi", 1, 2), BI, k1)]))
-            scopy(S["hi"], pr("hi", 0, 2))
+            early.append(mm([(pr("hi", b, b + 1), mrot(-5 * i, BIG, -1), ms[i]) for b in range(2) for i in range(NS)]
+                            + [(pr("hi", 0, 1), NB, par_before), (pr("hi", 1, 2), BI, par_before),
+                               (pr("hi", 0, 1), NB, kq), (pr("hi", 1, 2), BI, k3q)]))
+            shift("hi", S["hi"], pr("hi", 0, 2), 2048.0)
+            for i in range(2):
+                tt(sub(S["tmp"], i, 4 * L, 2), sub(q, i, 4 * L, 2), pr("hi", 0, 2), A.min)
         IH = rot(0, 0.5, ns)
-        mm([(pr("z"), IH, khalf), (pr("z"), IH, z), (pr("z"), IH, S["zf"])], stop=False, after=early)
+        mm([(pr("z"), IH, khalf), (pr("z"), IH, z), (pr("z"), IH, S["zf"])], stop=False, after=early + S["shut"])
         mm([(pr("z"), IH, sub(S["sc"], 15, 16 * L, 16)), (pr("z"), BI, k1536), (pr("z"), NB, k1536)], start=False)
         if last:
-            act(sub(msg, 5 * L, 6 * L), pr("z"), AF.Identity, bias=bN)
+            shift("z", sub(msg, 5 * L, 6 * L), pr("z"), -2048.0)
         else:
             S["z"] = sub(msg, L, 2 * L) if t == 0 else new(bf, L)
-            scopy(S["z"], pr("z"))
+            shift("z", S["z"], pr("z"))
         if t:
-            R, F = names_tails(S["rf"][NS])
-            mm([(pr("hd", 0, 4), NB, kq)] + [(pr("hd", 0, 4, i, 2), I1, S["hi"]) for i in range(2)])
-            tt(S["tmp"], q, pr("hd", 0, 4), A.min)
+            R, F = names_tails(S["rf"])
             mm([(pr("A", 0, 4, i, 2), NI, S["hi"]) for i in range(2)]
                + [(pr("A", 2 * b, 2 * b + 2, i, 2), I1, (R, F)[i]) for b in range(2) for i in range(2)])
             S["q"] = sub(msg, 0, 4 * L) if last else new(fh, 4 * L)
@@ -470,7 +534,7 @@ def build(P):
             un = ps(b3, 4 * L, 8 * L)
             if c == 0:
                 for i, b in enumerate((b1, b2)):
-                    dealt(ps(b, 0, 2 * IW), (2 * i, 2 * i + 1))
+                    dealt(ps(b, 0, 2 * IW), (2 * i, 2 * i + 1), False)
                     scopy(sub(SB, 2 * IW * i, 2 * IW * (i + 1)), ps(b, 0, 2 * IW))
                 make_names(1, b2)
                 thresholds(b1, [1, 2, 3, 4])
@@ -485,7 +549,7 @@ def build(P):
             unpack = ship(msg, w, ps(b3, 0, 3 * w), lambda r, k: k, lambda r, k, a: (r - k) % NR, cp)
             unpack(ps(b1, 0, 2 * w), (0, 1)); unpack(ps(b2, 0, 2 * w), (2, 3))
             o = new(f32, 6 * L)
-            act(sub(o, 0, 2 * w), ps(b1, 0, 2 * w), AF.Identity, bias=bX)
+            shift("out", sub(o, 0, 2 * w), ps(b1, 0, 2 * w), 2048.0)
             ts(sub(o, 2 * w, 4 * w), ps(b2, 0, 2 * w), 2048.0, A.add)
             for b in range(2):
                 store("ys"[b], "yq", 2 * (LN * b + L * c), 2 * (LN * b + L * c + L), sub(o, 2 * L * b, 2 * L * (b + 1)))
@@ -493,9 +557,13 @@ def build(P):
 
     for t in range(NV):
         for c in range(NCH):
-            cur[0] = c
+            cur[:] = [c, c + NCH * (0 if t == 0 else 2 if t == NV - 1 else 1), 0]
             visit(c, t)
 
+    return ops, sems, top
+
+
+def link(ops):
     hist = {}
     for i, o in enumerate(ops):
         dep = set(o.get("after", ()))
@@ -512,21 +580,24 @@ def build(P):
         dep.discard(i)
         o["dep"] = dep
         o["banks"] = sorted({v[0] for v in o["rd"] + o["wr"] if v[0].startswith("ps")})
-    anc, opened = [], {}
+    anc, opened, starts = [], {}, {}
     for i, o in enumerate(ops):
-        anc.append(set(o["dep"]).union(*[anc[j] for j in o["dep"]]) if o["dep"] else set())
-        if o["eng"] == "pe" and not o["stop"]:
+        a = 0
+        for j in o["dep"]:
+            a |= anc[j] | 1 << j
+        anc.append(a)
+        if o["eng"] == "pe" and o["start"]:
+            starts.setdefault(o["bank"], []).append(i)
+        if o["eng"] == "pe" and o["start"] and not o["stop"]:
             opened[o["bank"]] = i
-        elif o["eng"] == "pe" and not o["start"]:
+        elif o["eng"] == "pe" and o["stop"] and not o["start"]:
             k = opened.pop(o["bank"])
-            ops[k]["dep"] |= {j for j in anc[i] if j != k and ops[j].get("bank") == o["bank"] and ops[j]["start"]
-                              and j not in anc[k]}
+            ops[k]["dep"] |= {j for j in starts[o["bank"]] if j != k and a >> j & 1 and not anc[k] >> j & 1}
     for o in ops:
         o["dep"] = sorted(o["dep"])
-    return ops, sems, top
 
 
-def schedule(ops, P, seed):
+def schedule(ops, P, seed, given=None):
     n = len(ops)
     succ = [[] for _ in range(n)]
     for i, o in enumerate(ops):
@@ -547,8 +618,10 @@ def schedule(ops, P, seed):
     pri = []
     for i, o in enumerate(ops):
         seed = (seed * 1103515245 + 12345) % 2 ** 31
-        pri.append(rank[i] + (P["bias"] + (0,))[o["ch"]] + P.get("jit", 0) * seed / 2 ** 31)
-    ready, fin = [0.0] * n, [0.0] * n
+        pri.append(rank[i] + (P["bias"] + (0,))[o["ch"]] + P.get("jit", 0) * seed / 2 ** 31 + P.get("prio", {}).get(o["key"], 0))
+    if given:
+        pri = [p - r + x for p, r, x in zip(pri, rank, given)]
+    ready, fin = [o.get("pre", 0.0) for o in ops], [0.0] * n
     pool = {e: [] for e in ("v", "s", "pe", "g", "y")}
     for i in range(n):
         if not left[i]:
@@ -597,21 +670,52 @@ def schedule(ops, P, seed):
         free[e] = t0 + o["cost"]
         fin[i] = free[e] + o.get("lat", 0)
         for j in succ[i]:
-            ready[j] = max(ready[j], fin[i] + (0 if e == "pe" and ops[j]["eng"] == "pe" else lam)); left[j] -= 1
+            ready[j] = max(ready[j], fin[i] + ops[j].get("pre", 0) + (0 if e == "pe" and ops[j]["eng"] == "pe" else lam))
+            left[j] -= 1
             if not left[j]:
                 pool[ops[j]["eng"]].append(j)
-    return max(fin), order, seq, deps
+    return max(fin), order, seq, deps, fin
+
+
+def replay(ops, lam, seq, deps):
+    fin, free = {}, {}
+    for i in seq:
+        o = ops[i]
+        t = max([free.get(o["eng"], 0)] + [fin[j] + (0 if o["eng"] == ops[j]["eng"] == "pe" else lam) for j in deps[i]])
+        free[o["eng"]] = t + o["cost"]
+        fin[i] = t + o["cost"] + o.get("lat", 0)
+    return max(fin.values())
+
+
+def mirror(ops, deps):
+    back = [dict(o, dep=[], lat=0, pre=o.get("lat", 0), start=o.get("stop"), stop=o.get("start")) for o in ops]
+    for i in range(len(ops)):
+        for j in deps[i]:
+            back[j]["dep"].append(i)
+    return back
 
 
 def plan(P):
     ops, sems, top = build(P)
-    best = schedule(ops, P, 1)
-    for seed in range(2, 2 + P["tries"]):
-        best = min(best, schedule(ops, dict(P, jit=400), seed), key=lambda x: x[0])
+    link(ops)
+    back = mirror(ops, [o["dep"] for o in ops])
+    others = [(build(dict(P, **m))[0], m["lam"]) for m in P["also"]]
+
+    def worth(x):
+        return x[0] + sum(replay(o, lam, x[2], x[3]) for o, lam in others)
+    best = last = schedule(ops, P, 1)
+    mark = worth(best)
+    Q = dict(P, bias=(0, 0), jit=P["jit_"])
+    for seed in range(P["tries"]):
+        if seed % P["again"] == 0:
+            last = best
+        last = schedule(ops, Q, seed + P["seed"], schedule(back, Q, seed + P["seed"], last[4])[4])
+        if last[0] < best[0] * 1.01 and worth(last) < mark:
+            best, mark = last, worth(last)
     return (ops, sems, top) + best
 
 
-OPS, DSEMS, TOP, SPAN, ORDER, SEQ, DEPS = plan(P)
+OPS, DSEMS, TOP, SPAN, ORDER, SEQ, DEPS, FIN = plan(P)
 SCRATCH = {ARENA[k]: ("sbuf", [128, TOP[k]], k) for k in ARENA}
 SCRATCH["tb"] = ("sbuf", [128, W + 16], "bfloat16")
 SCRATCH["t2"] = ("sbuf", [128, W + 16], "bfloat16")

from concourse.bass import DstId, RemoteDMATransfer
from concourse.mybir import AluOpType as A, ActivationFunctionType as AF

NR, W, LN, NV, NS = 4, 4096, 128, 5, 3
L = 64
NCH = LN // L
BLK = 128 // NR
BIG = 8192.0
P = dict(
    nd=(24, 32, 24),
    vp={32: (16, 16), 40: (20, 12, 8), 48: (16, 16, 16), 56: (24, 16, 16), 64: (24, 24, 16)},
    xp=(("s", 16), ("s", 24), ("s", 24)),
    fp=(("s", 24), ("v", 16), ("s", 24)),
    xp0=(("v", 32), ("s", 32)),
    on=dict(ux="s", uy="v", uf="v", g="v", par="v", z="s", hi="v", w="s", m="v"),
    bias=(2500, 0), tries=300, again=20, jit_=100, look=250, gam=6.0, fit=80,
    seed=0, dpre=False, also=(dict(cyc=1.1, pe=.55, gat=1.7, lam=200), dict(cyc=.83, pe=.5, gat=1.3, lam=230)),
    cyc=0.87, pe=.46, gat=1.56, lam=190, issue=1300, fly=3000, dma=2500, rate=30.0,
)

SIZE = {"bfloat16": 2, "float16": 2, "float32": 4, "int32": 4, "uint16": 2}
ARENA = {"bfloat16": "ab", "float16": "ah", "float32": "af", "int32": "ai", "uint16": "au"}


def ap(T, v, r):
    if not isinstance(v, tuple):
        return v
    if v[0] == "ind":
        return ap(T, v[1], r).indirect(ap(T, v[2], r))
    if len(v) == 6:
        return T[v[0]][v[4]:v[5], v[1]:v[2]]
    if len(v) == 5:
        a = v[1] + v[4](r)
        return T[v[0]][:, a:a + 128]
    if v[3] == 1:
        return T[v[0]][:, v[1]:v[2]]
    return T[v[0]][:, v[1]:v[2]:v[3]]


def build(P):
    top = {k: 0 for k in ARENA}
    ops, sems, cur = [], [], [0, -1, 0]
    cyc, pec = P["cyc"], P["pe"]

    def new(dt, n):
        al = 32 // SIZE[dt]
        c = top[dt]
        top[dt] = c + (n + al - 1) // al * al
        return (ARENA[dt], c, c + n, 1)

    def sub(v, a, b, st=1):
        return (v[0], v[1] + a, v[1] + b, st)

    def cnt(v):
        if v[0] == "ind":
            return 16 * cnt(v[2])
        return (v[2] - v[1] + v[3] - 1) // v[3]

    def ps(bank, a, b):
        return ("ps%d" % bank, a, b, 1)

    def part(s):
        return ("t2part%d" % s, 0, 1, 1)

    def add(eng, fn, rd, wr, cost, **kw):
        r = []
        for v in rd:
            if isinstance(v, tuple):
                r += [v[1], v[2]] if v[0] == "ind" else [v]
                if v[0] == "ind" and v[1][0] == "t2":
                    r += [part(s) for s in range(NR)]
        ops.append(dict(eng=eng, fn=fn, rd=r, wr=list(wr), cost=cost, ch=cur[0], key=(cur[1], cur[2]), **kw))
        cur[2] += 1
        return len(ops) - 1

    def vcost(out, in0, k):
        if in0 and in0[0] == "ind":
            return 50 + cnt(in0) * P["gat"] * cyc
        return max(64, cnt(out) * k) * cyc

    def half(*vs):
        return 0.5 if all(v[0] in ("ab", "ah", "au", "tb", "t2") for v in vs) else 1

    def ts(out, in0, s1, op0, s2=None, op1=None):
        def fn(g, T, r):
            if op1 is None:
                return g.vector.tensor_scalar(ap(T, out, r), ap(T, in0, r), ap(T, s1, r), None, op0)
            return g.vector.tensor_scalar(ap(T, out, r), ap(T, in0, r), ap(T, s1, r), ap(T, s2, r), op0, op1)
        return add("v", fn, [in0, s1, s2], [out], vcost(out, in0, half(out, in0)))

    def tt(out, in0, in1, op):
        k = 1 if (in0[0].startswith("ps") or in1[0].startswith("ps")) else 2
        return add("v", lambda g, T, r: g.vector.tensor_tensor(ap(T, out, r), ap(T, in0, r), ap(T, in1, r), op),
                   [in0, in1], [out], vcost(out, in0, k))

    def cp(out, in_):
        return add("v", lambda g, T, r: g.vector.tensor_copy(ap(T, out, r), ap(T, in_, r)), [in_], [out],
                   vcost(out, in_, half(out, in_)))

    def fill(out, val):
        return add("v", lambda g, T, r: g.vector.memset(ap(T, out, r), val), [], [out], vcost(out, None, half(out)))

    def scan(out, d0, d1, op0, op1):
        return add("v", lambda g, T, r: g.vector.tensor_tensor_scan(ap(T, out, r), ap(T, d0, r), ap(T, d1, r), 0.0, op0, op1),
                   [d0, d1], [out], vcost(out, None, half(out, d0, d1)))

    def fma(out, d0, d1):
        return scan(out, d0, d1, A.mult, A.add)

    def act(out, in_, func, bias=0.0, scale=1.0):
        c = 65 + cnt(in_) * P["gat"] * cyc if in_[0] == "ind" else max(64, cnt(out)) * cyc
        return add("s", lambda g, T, r: g.scalar.activation(ap(T, out, r), ap(T, in_, r), func, bias=ap(T, bias, r), scale=scale),
                   [in_, bias], [out], c)

    def mm(terms, start=True, stop=True, after=()):
        def fn(g, T, r):
            last = None
            for i, (o, lhs, rhs) in enumerate(terms):
                last = g.tensor.matmul(ap(T, o, r), ap(T, lhs, r), ap(T, rhs, r),
                                       start and i == 0, stop and o[4:] not in [x[0][4:] for x in terms[i + 1:]])
            return last
        c, rd = 30, []
        for o, lhs, rhs in terms:
            c += max(min(64, cnt(lhs)), cnt(rhs)) * (4 if rhs[0] == "af" else 1) * pec
            rd += [lhs, rhs]
        tok = ("open" + terms[0][0][0], 0, 1, 1)
        return add("pe", fn, rd + ([] if start else [tok]), [o for o, _, _ in terms] + ([] if stop else [tok]), c,
                   start=start, stop=stop, bank=terms[0][0][0], after=after)

    def iota(out, pattern, base, cm):
        def fn(g, T, r):
            if out[0] == "ai":
                return g.iota(ap(T, out, r), pattern, base, cm)
            return g.iota(ap(T, out, r), pattern, base, cm, allow_small_or_imprecise_dtypes=True)
        return add("g", fn, [], [out], 130 + 2 * cnt(out) * cyc)

    def dma(q, out, in_, rd, wr, lat, after=()):
        sems.append("d%d" % len(sems))
        eng = {"y": lambda g: g.sync, "s": lambda g: g.scalar}[q]
        return add(q, lambda g, T, r: eng(g).dma_start(out(T, r), in_(T, r)), rd, wr, 60, sem=sems[-1], lat=lat, after=after)

    def load(q, dst, name, lat):
        return dma(q, lambda T, r: ap(T, dst, r), lambda T, r: T[name][:], [], [dst], lat)

    def store(q, name, a, b, src):
        return dma(q, lambda T, r: T[name][:, a:b], lambda T, r: ap(T, src, r), [src], [], P["dma"])

    def send(items, rd, wr, nbytes):
        sems.append("r%d" % len(sems))
        return add("g", None, rd, wr, P["issue"], sem=sems[-1], items=items, lat=P["fly"] + nbytes / P["rate"])

    bf, fh, f32, i32, u16 = "bfloat16", "float16", "float32", "int32", "uint16"
    tabs = [(n, 16, 16 + W, 1) for n in ("tb", "t2")]
    wins = [(n, 0, 16 + W, 1) for n in ("tb", "t2")]
    hi, gi, zi, thi, qi = new(i32, LN), new(i32, LN), new(i32, LN), new(i32, 1), new(i32, 4 * LN)
    first = load("s", tabs[0], "xt", P["dma"] + 3500)
    load("y", hi, "hn", P["dma"]); load("y", gi, "gt", P["dma"]); load("y", zi, "zs", P["dma"])
    load("y", qi, "qs", P["dma"] + 300); load("y", thi, "th", P["dma"])
    cur[0] = 2
    for k in range(1, NR):
        sx, lx, slot = ("sx", k, k + 1, 1), ("lx", k, k + 1, 1), NR - k
        dma("y", lambda T, r, k=k: T.sx[k - 1], lambda T, r, k=k: T.xt[BLK * ((r + k) % NR):BLK * ((r + k) % NR + 1), :],
            [], [sx], P["dma"] + 1000 * k, after=[first])
        send([(lambda T, k=k: T.sx[k - 1], lambda T, k=k: T.lx[k - 1], k)], [sx], [lx], BLK * W * k // 2)
        dma("y", lambda T, r, s=slot: T.t2[BLK * s:BLK * (s + 1), 16:16 + W], lambda T, r, k=k: T.lx[k - 1],
            [lx], [part(slot)], P["dma"] + 1500)
    dma("y", lambda T, r: T.t2[0:BLK, 16:16 + W], lambda T, r: T.xt[BLK * r:BLK * (r + 1), :], [], [part(0)],
        P["dma"] + 4000, after=[first])
    cur[0] = 0
    row128, rowg, rowp = new(bf, 128), new(bf, 128), new(bf, 128)
    ci, cj, cip, cjp = new(i32, 16), new(i32, 3), new(i32, 16), new(i32, 3)
    iota(ci, [[-1, 16]], 16, 1); iota(row128, [[1, 128]], 0, 0); iota(cj, [[BLK, 3]], 128 - BLK, 1)
    iota(rowg, [[16, 8], [0, 16]], 0, 0); iota(rowp, [[1, 16], [16, 8]], 0, 0)
    iota(cip, [[-8, 16]], 128, 1); iota(cjp, [[BLK, 3]], 128 - BLK, 16)
    SP = max(n for _, n in P["fp"])
    reset = new(bf, 16 * SP)
    iota(reset, [[0, SP], [256, 16]], 0, 0)
    wpi, WP = new(bf, 640), new(bf, 640)
    iota(wpi, [[-BLK, 5], [-1024, 4], [-1, BLK]], BLK, 1)
    ci2, cj2, c16 = new(i32, 16), new(i32, 3), new(f32, 3)
    ts(ci2, ci, 15, A.bitwise_and); ts(cj2, cj, 112, A.bitwise_and); cp(c16, cj2)
    cip2, cjp2, c16p = new(i32, 16), new(i32, 3), new(f32, 3)
    ts(cip2, cip, 3, A.arith_shift_right, 15, A.bitwise_and); ts(cjp2, cjp, 112, A.bitwise_and); cp(c16p, cjp2)
    g16 = {(sh, p): sub((c16, c16p)[p], sh + 1, sh + 2) for sh in (-1, 0, 1) for p in (0, 1)}
    col = {key: new(f32, 16) for key in g16}
    c24 = new(f32, 1)
    ts(col[0, 0], ci2, g16[0, 0], A.add); ts(c24, g16[0, 0], 1.0 / 16, A.mult, 24.0, A.add)
    made = {}

    def cmp_mat(src, c, op, scale, dt=bf):
        m, keep = new(dt, cnt(src)), cur[1:]
        cur[1:] = [-2, len(ops)]
        ts(m, src, c, op, scale, A.mult)
        cur[1:] = keep
        return m

    def rot(r, scale=1.0, sh=0, dt=bf, pin=0, pout=0):
        key = ("rot", r % 16, scale, sh, dt, pin, pout)
        if key not in made:
            made[key] = cmp_mat(rowp if pout else row128, sub(col[sh, pin], r % 16, r % 16 + 1), A.is_equal, scale, dt)
        return made[key]

    def grp(scale, sh=0, pin=0):
        key = ("grp", scale, sh, pin)
        if key not in made:
            made[key] = cmp_mat(rowg, g16[sh, pin], A.is_equal, scale)
        return made[key]

    def mrot(r, scale, sh=0, pout=0):
        return rot(r, scale, sh, bf, 1, pout)

    I1, I2080, I3232 = rot(0), rot(0, 2080.0), rot(0, 3232.0)
    k0, k1, khalf, k3072 = new(bf, L), new(bf, L), new(bf, L), new(bf, L)
    fill(k1, 1.0); fill(k0, 0.0)
    IW = 168
    IB, SB = new(fh, 4 * IW), new(fh, 4 * IW)
    fill(sub(IB, 5 * LN, 4 * IW), 0.0)
    names = [sub(b, 4 * LN, 5 * LN) for b in (IB, SB)]
    thc = [sub(b, 5 * LN, 5 * LN + 1) for b in (IB, SB)]
    st = []
    for c in range(NCH):
        st.append(dict(
            x=new(bf, 16 * L), d=[new(bf, 16 * L) for _ in range(NS)], a=[new(bf, 16 * L) for _ in range(NS)],
            fin=new(bf, 16 * L), sc=new(bf, 16 * L), s=new(i32, 3 * L), sx=new(i32, 2 * L),
            ix=new(i32, L), ux=new(u16, L), idx=new(i32, 3 * L), uy=[new(u16, L) for _ in range(NS)],
            rf=new(fh, 4 * L), m=new(bf, 3 * L), sel=new(fh, 2 * L), eq=new(bf, 4 * L), ef=new(bf, 3 * L),
            pb=[new(bf, 6 * L) for _ in range(2)], rb=[new(fh, 6 * L) for _ in range(NS)], fb=new(f32, 3 * L),
            F=[new(fh, L) for _ in range(NS)],
            e3=new(f32, 3 * L), s3=new(i32, 3 * L), g2=new(i32, L), fp=new(f32, 3 * L), uf=new(u16, L), fs=new(fh, 4 * L),
            hi=new(bf, 2 * L), tmp=new(fh, 4 * L), zf=new(bf, L), gb=new(fh, 2 * L),
            q=sub(IB, 4 * L * c, 4 * L * (c + 1)), z=new(bf, L), cn=k0, par=None, shut=[]))
    ts(names[0], hi, 2048.0, A.subtract)
    for c, S in enumerate(st):
        fill(S["gb"], 0.0)
        ts(sub(S["gb"], 1, 2 * L, 2), sub(gi, L * c, L * c + L), 2048.0, A.subtract)
        cp(S["z"], sub(zi, L * c, L * c + L))
        for b in range(2):
            ts(sub(S["q"], 2 * L * b, 2 * L * (b + 1)), sub(qi, 2 * (LN * b + L * c), 2 * (LN * b + L * c + L)),
               2048.0, A.subtract)
    ts(thc[0], thi, 2048.0, A.subtract)
    NI, BI, NB, ONE, NONE = rot(0, -1.0), rot(0, BIG), rot(0, -BIG), grp(1.0), grp(-1.0)
    fill(khalf, -0.5); fill(k3072, 3072.0)
    kn = new(bf, L)
    fill(kn, -2080.0)
    for S in st:
        for b in S["pb"]:
            fill(b, 0.0); fill(sub(b, 5, 6 * L, 6), 3232.0)
        for b in S["rb"]:
            fill(b, 0.0)
        fill(S["ef"], 0.0); fill(sub(S["ef"], 2, 3 * L, 3), 3232.0)
    B1 = cmp_mat(sub(row128, 0, 56), c24, A.is_equal, 1.0)
    LTa = cmp_mat(row128, sub(col[0, 0], 0, 1), A.is_lt, -2 * BIG)
    LTb = cmp_mat(row128, g16[0, 0], A.is_lt, 2 * BIG)
    ts(col[0, 1], cip2, g16[0, 1], A.add)
    for n in ("tb", "t2"):
        fill((n, 0, 16, 1), 0.0)
    for S in st:
        fill(S["eq"], 0.0); fill(S["e3"], 0.0)
    k1536, k1024, kq, k3q = new(bf, L), new(bf, L), new(bf, L), new(bf, L)
    fill(k1536, 1536.0); fill(k1024, 1024.0); fill(kq, 0.25); fill(k3q, 0.75)
    bias = new(f32, 5)
    BIAS = {v: sub(bias, i, i + 1) for i, v in enumerate((32.0, 2048.0, -2048.0, -2080.0, 16.0 - 2 * BIG))}
    for v in BIAS:
        fill(BIAS[v], v)
    for key in col:
        if key[0]:
            ts(col[key], (ci2, cip2)[key[1]], g16[key], A.add)
    MB, MN, MN2 = mrot(0, BIG), mrot(0, -BIG), mrot(0, -2 * BIG)
    ts(WP, wpi, 0.0, A.is_equal)
    IF, NB2 = rot(0, 1.0, 0, f32), rot(0, -2 * BIG)
    Q = [rot(-t) for t in range(NV)]
    QP = [rot(-t, pout=1) for t in range(NV)]
    thb = thv = new(f32, NV)
    H, TR = [names[0]] + [None] * (NV - 1), [None] * NV

    def move(src, dst):
        return (WP[0], WP[1], WP[2], 1, lambda r: 128 + 128 * src(r) - BLK * dst(r))

    def thresholds(bank, ts_):
        r = ps(bank, 504 + ts_[0], 505 + ts_[-1])
        mm([(ps(bank, 504 + t, 505 + t), QP[t], thc[t > 0]) for t in ts_])
        if P["on"].get("m", "s") == "v":
            ts(sub(thv, ts_[0], ts_[-1] + 1), r, 2048.0, A.add)
        else:
            ts(sub(thb, ts_[0], ts_[-1] + 1), r, 256.0, A.mult, 256.0 * 2048 - 128, A.add)

    def make_tr(t, bank):
        TR[t] = new(bf, 128)
        r, wtmp = ps(bank, 384, 512), new(bf, 128)
        mm([(r, LTa, Q[t]), (r, LTb, Q[t]), (r, BI, Q[t])])
        act(wtmp, r, AF.Copy)
        mm([(r, QP[t], wtmp)])
        act(TR[t], r, AF.Copy)

    def make_names(t, bank):
        H[t] = new(fh, LN)
        r = ps(bank, 384, 512)
        mm([(r, rot(-1, 1.0, 1), names[1] if t == 1 else H[t - 1])])
        act(H[t], r, AF.Copy)

    def ship(src, w, pack, from_blk, to_blk, copy):
        out, land = new(fh, 3 * w), new(fh, 3 * w)
        for k in range(1, NR):
            o = sub(pack, (k - 1) * w, k * w)
            mm([(o, move(lambda r, k=k: from_blk(r, k), lambda r, a=a: a), sub(src, a * w, (a + 1) * w)) for a in range(4)])
        copy(out, sub(pack, 0, 3 * w))
        send([(lambda T, k=k: ap(T, sub(out, (k - 1) * w, k * w), 0), lambda T, k=k: ap(T, sub(land, (k - 1) * w, k * w), 0), k)
              for k in range(1, NR)], [out], [land], 128 * w * 2 * 2)

        def unpack(reg, quarters, ahead=True):
            own, came = [], []
            for n, a in enumerate(quarters):
                o = sub(reg, n * w, (n + 1) * w)
                own.append((o, move(lambda r: from_blk(r, 0), lambda r, a=a: to_blk(r, 0, a)), sub(src, a * w, (a + 1) * w)))
                came += [(o, move(lambda r, a=a: a, lambda r, a=a, k=k: to_blk(r, k, a)), sub(land, (k - 1) * w, k * w))
                         for k in range(1, NR)]
            if ahead:
                mm(own, stop=False); mm(came, start=False)
            else:
                mm(own + came)
        return unpack

    def scopy(out, in_):
        act(out, in_, AF.Copy)

    def shift(name, out, in_, add_=0.0):
        if P["on"].get(name, "s") == "v":
            return ts(out, in_, add_, A.add)
        return act(out, in_, AF.Identity, bias=BIAS[add_]) if add_ else act(out, in_, AF.Copy)

    thresholds(7, [0])
    for t in range(NV):
        make_tr(t, 3 + 4 * (t % 2))
    cur[0] = 2
    dealt = ship(IB, IW, ps(4, 0, 3 * IW), lambda r, k: (r + k) % NR, lambda r, k, a: -k % NR, scopy)

    def pieces(sz):
        out, a = [], 0
        for n in sz:
            out.append((a, a + n)); a += n
        return out

    def gather(eng, out, win, off):
        if eng == "s":
            act(out, ("ind", win, off), AF.Copy)
        else:
            cp(out, ("ind", win, off))

    def names_tails(rf):
        return sub(rf, 1, 2 * L, 2), sub(rf, 2 * L + 1, 4 * L, 2)

    def visit(c, t):
        S = st[c]
        b0, b1, b2, b3 = 4 * c, 4 * c + 1, 4 * c + 2, 4 * c + 3
        lay = dict(d=(b0, 0), cn=(b0, 1), zf=(b0, 2), z=(b0, 3), hi=(b3, 4), T01=(b0, 4), fm=(b0, 1), w=(b0, 5), diff=(b0, 6),
                   sel=(b1, 0), T23=(b1, 2), lx=(b1, 2), dg=(b1, 4), ly=(b1, 5), dif1=(b1, 6),
                   dr=(b2, 0), par=(b2, 0), g3=(b2, 5),
                   D=(b3, 0), fid=(b3, 7), A=(b3, 0), qd=(b3, 0))

        def pr(name, a=0, b=1, o=0, st=1):
            bank, u = lay[name]
            return ("ps%d" % bank, int((u + a) * L) + o, int((u + b) * L), st)
        last = t == NV - 1
        table, win0 = tabs[t > 0], wins[t > 0]
        nr, ns = (NV - 1, 0) if last else (-1, int(t > 0))
        if c == 1 and 0 < t < NV - 1:
            make_names(t + 1, b3)
        Ht, G, z, x, m, q = sub(H[t], L * c, L * c + L), sub(S["gb"], 1, 2 * L, 2), S["z"], S["x"], S["m"], S["q"]
        mm([(pr("lx", 0, 2, 0, 2), I1, Ht), (pr("lx", 0, 2, 0, 2), I3232, k1), (pr("lx", 0, 2, 1, 2), I2080, Ht)])
        fma(S["sx"], S["gb"], pr("lx", 0, 2))
        ts(S["ix"], sub(S["sx"], 1, 2 * L, 2), 5, A.arith_shift_right, W - 1, A.bitwise_and)
        shift("ux", S["ux"], S["ix"])
        xp = P["xp" if t else "xp0"]
        for (e, _), (a, b) in zip(xp, pieces([n for _, n in xp])):
            gather(e, sub(x, 16 * a, 16 * b), table, sub(S["ux"], a, b))
        qv = [[sub(q, 2 * L * b + i, 2 * L * (b + 1), 2) for b in range(2)] for i in range(2)]

        def two(name, i):
            return pr(name, 0, 2, i, 2)

        def three(name, i):
            return pr(name, 2, 5, i, 3)

        def consts(name):
            return [(three(name, 1), I2080, k1), (three(name, 2), I3232, kn)]

        def renamed(s, name, er, ef):
            fma(S["fb"], ef, pr(name, 2, 5))
            fma(sub(S["rb"][s], 1, 6 * L, 3), er, pr(name, 0, 2))
            fma(S["s"], sub(S["rb"][s], 0, 6 * L, 2), S["fb"])
            shift("F", S["F"][s], sub(S["fb"], 1, 3 * L, 3), -2080.0)
        mm(consts("qd") + [x_ for f, v in zip((two, three), qv)
                           for x_ in ((f("qd", 0), I1, v[0]), (f("qd", 0), NI, v[1]), (f("qd", 1), I1, v[0]))])
        po, pb = pr("par"), S["pb"][t % 2]
        mm([(po, I1, khalf)], stop=False)
        mm([(po, ONE, z), (po, BI, k3072), (po, NB, k3072), (po, NONE, z)], start=False)
        par_before, S["par"] = S["par"], sub(pb, 3, 6 * L, 6)
        shift("par", S["par"], po)
        renamed(0, "qd", sub(pb, 0, 6 * L, 3), sub(pb, 1, 6 * L, 2))
        msg = new(fh, 6 * L if last else 4 * L) if t == 0 or last else None
        if t == 0:
            scopy(sub(msg, 3 * L, 4 * L), po)
        mm([(pr("w"), grp(1.0, ns), z)])
        shift("w", sub(S["e3"], 2, 3 * L, 3), pr("w"), 32.0)
        ms = [sub(m, s * L, (s + 1) * L) for s in range(NS)]
        fs = S["fs"]
        fq = [sub(fs, i * L, (i + 1) * L) for i in range(4)]
        for s in range(NS):
            idx = sub(S["idx"], NS - 1 - s, NS * L, NS)
            end = s == NS - 1
            R, F = sub(S["rb"][s], 4, 6 * L, 6), S["F"][s]
            ts(idx, sub(S["s"], 2, 3 * L, 3), 5, A.arith_shift_right, W - 1, A.bitwise_and)
            shift("uy", S["uy"][s], idx)
            early = []
            if end:
                early.append(mm([(pr("T01", i, i + 1), lhs, rhs) for i in range(2)
                                 for lhs, rhs in ((rot(5 * i - 10), F), (MB, ms[i]))]))
                ts(sub(fs, 0, 2 * L), pr("T01", 0, 2), BIG, A.subtract, -2048.0, A.max)
                fm = [pr("fm", 0, 3, i, 3) for i in range(3)]
                early.append(mm([(fm[0], NB2, k1), (fm[1], BI, k1), (fm[1], MN2, ms[1]), (fm[2], MB, ms[1]), (fm[2], MN2, ms[0])]))
                scan(S["fp"], pr("fm", 0, 3), S["idx"], A.add, A.max)
            d, a_, uy, nd = S["d"][s], S["a"][s], S["uy"][s], P["nd"][s]
            nv = L - nd
            ya, pD = sub(d, 16 * nv, 16 * L), pr("D", 0, 16.0 * nd / L)
            if nd:
                act(ya, ("ind", table, sub(uy, nv, L)), AF.Copy)
                mm([(pD, NI, sub(x, 16 * nv, 16 * L))], stop=False)
                mm([(pD, I1, ya)], start=False)
                act(sub(a_, 16 * nv, 16 * L), pD, AF.Abs)
            for a, b in pieces(P["vp"][nv]):
                tt(sub(d, 16 * a, 16 * b), ("ind", table, sub(uy, a, b)), sub(x, 16 * a, 16 * b), A.subtract)
                act(sub(a_, 16 * a, 16 * b), sub(d, 16 * a, 16 * b), AF.Abs)
            pre = [(rot(0, -1.0, pout=1), S["cn"])]
            pre += [(mrot(r, BIG, 0, 1), ms[s0]) for s0 in range(s) for r in (0, 5 * (s - s0))]
            if pre:
                mm([(pr("d"), lhs, rhs) for lhs, rhs in pre], stop=False, after=early + S["shut"])
            for h in range(2):
                mm([(pr("d", h / 2, (h + 1) / 2) + (32 * (k // 4), 32 * (k // 4 + 1)), sub(B1, 24 - 8 * (k % 4), 56 - 8 * (k % 4)),
                     sub(a_, 8 * L * h + k, 8 * L * (h + 1), 16)) for k in range(16)], start=not pre and not h, stop=h == 1)
            if P["on"].get("m", "s") == "v":
                matched = ts(ms[s], pr("d"), sub(thv, t, t + 1), A.is_lt)
            else:
                matched = act(ms[s], pr("d"), AF.Sigmoid, bias=sub(thb, t, t + 1), scale=-256.0)
            rename = not end or t > 0
            xs = -1 if end else 0
            RT = rot(6, 1.0, -1) if end and rename else rot(5)
            if end:
                mm([(pr("fid"), IF, sub(S["fp"], 2, 3 * L, 3)), (pr("fid"), mrot(0, 2 * BIG), ms[0]), (pr("fid"), MB, ms[1])],
                   stop=False)
                mm([(pr("fid"), MB, ms[2])], start=False)
                shift("uf", S["uf"], pr("fid"), 16.0 - 2 * BIG)
                for (e, _), (a, b) in zip(P["fp"], pieces([n for _, n in P["fp"]])):
                    gather(e, sub(S["fin"], 16 * a, 16 * b), win0, sub(S["uf"], a, b))
                    scan(sub(S["sc"], 16 * a, 16 * b), sub(reset, 0, 16 * (b - a)), sub(S["fin"], 16 * a, 16 * b), A.min, A.max)
            sR, sH = sub(S["sel"], 0, L), sub(S["sel"], L, 2 * L)
            T2, T3 = pr("T23", 0, 1), pr("T23", 1, 2)
            mm([(pr("sel", 0, 1), I1, R), (pr("sel", 1, 2), I1, Ht)]
               + ([(T2, I1, F), (T3, I1, G), (T3, BI, k1), (T3, MN, ms[0]), (T3, MN, ms[1])] if end else []),
               stop=False)
            mm([(pr("sel", 0, 1), TR[t], ms[s]), (pr("sel", 1, 2), TR[t], ms[s])]
               + ([(T2, MB, ms[s]), (T3, MN, ms[s])] if end else []), start=False)
            ts(S["sel"], pr("sel", 0, 2), BIG, A.subtract, -2048.0, A.max)
            if end:
                ts(sub(fs, 2 * L, 4 * L), pr("T23", 0, 2), BIG, A.subtract, -2048.0, A.max)
            g3 = [pr("g3", 0, 3, i, 3) for i in range(3)]
            f1 = rot(nr, 1.0, ns) if end else None
            pre, post = [], []
            if rename:
                dr = [[two("dr", i), pr("dr", 2, 4, i, 2) if end else three("dr", i)] for i in range(2)]
                pre += [(dr[1][i], RT, (R, F)[i]) for i in range(2)] + ([] if end else consts("dr"))
                post += [(dr[0][i], lhs, rhs) for i in range(2)
                         for lhs, rhs in ((grp(1.0, xs), sH), (grp(-1.0, xs), sR))]
            if end:
                pre += [(g3[1], NB, khalf), (g3[1], f1, fq[0]), (g3[1], f1, fq[1]),
                        (g3[2], grp(2048.0, ns), z), (g3[2], NB, k1024)]
            mm(pre, stop=False)
            if rename and not P["dpre"]:
                mm([(pr("dif1", i, i + 1), lhs, rhs) for i in range(2)
                    for lhs, rhs in ((RT, (R, F)[i]), (grp(-1.0, xs), sR))])
            elif rename:
                mm([(pr("diff", i, i + 1), RT, (R, F)[i]) for i in range(2)], stop=False, after=[matched])
                S["shut"] = [mm([(pr("diff", i, i + 1), grp(-1.0, xs), sR) for i in range(2)], start=False)]
            if end:
                mm([(pr("dg"), mrot(nr, -BIG, ns), ms[i]) for i in range(NS)] + [(pr("dg"), f1, fq[i]) for i in range(NS)]
                   + [(pr("dg"), grp(-1.0, ns), sR)])
                post += [(g3[0], grp(1.0, ns), sH), (g3[0], grp(-1.0, ns), sR), (g3[1], f1, fq[2]),
                         (g3[2], rot(nr, 32.0, ns), fq[3])]
            mm(post, start=False)
            if end:
                ts(sub(S["e3"], 1, 3 * L, 3), pr("dg"), 13 * 2048.0 - BIG, A.is_equal)
                fma(S["s3"], S["e3"], pr("g3", 0, 3))
                ts(S["g2"], sub(S["s3"], 2, 3 * L, 3), 5, A.arith_shift_right, W - 1, A.bitwise_and)
                shift("g", sub(msg, 4 * L, 5 * L) if last else sub(msg, 0, L) if t == 0 else G, S["g2"], -2048.0)
            df = "diff" if P["dpre"] else "dif1"
            if not end:
                ts(sub(S["ef"], 1, 3 * L, 3), pr(df, 1, 2), 15 * 2048.0, A.is_equal)
                ts(sub(S["eq"], 1, 2 * L, 2), pr(df, 0, 1), 15 * 2048.0, A.is_equal)
                renamed(s + 1, "dr", sub(S["eq"], 0, 2 * L), S["ef"])
            elif rename:
                ts(sub(S["eq"], 1, 4 * L, 2), pr(df, 0, 2), 15 * 2048.0, A.is_equal)
                fma(S["rf"], S["eq"], pr("dr", 0, 4))
        mm([(pr("zf"), I1, z)] + [(pr("zf"), grp(-BIG, 0, 1), ms[i]) for i in range(NS)])
        if P["on"].get("zf", "s") == "v":
            ts(S["zf"], pr("zf"), 0.0, A.max)
        else:
            act(S["zf"], pr("zf"), AF.Relu)
        early = []
        if not last:
            S["cn"] = sub(msg, 2 * L, 3 * L) if t == 0 else new(bf, L)
            early.append(mm([(pr("cn"), grp(1.0, ns, 1), ms[i]) for i in range(NS)]))
            shift("cn", S["cn"], pr("cn"))
        if t:
            early.append(mm([(pr("hi", b, b + 1), mrot(-5 * i, BIG, -1), ms[i]) for b in range(2) for i in range(NS)]
                            + [(pr("hi", 0, 1), NB, par_before), (pr("hi", 1, 2), BI, par_before),
                               (pr("hi", 0, 1), NB, kq), (pr("hi", 1, 2), BI, k3q)]))
            shift("hi", S["hi"], pr("hi", 0, 2), 2048.0)
            for i in range(2):
                tt(sub(S["tmp"], i, 4 * L, 2), sub(q, i, 4 * L, 2), pr("hi", 0, 2), A.min)
        IH = rot(0, 0.5, ns)
        mm([(pr("z"), IH, khalf), (pr("z"), IH, z), (pr("z"), IH, S["zf"])], stop=False, after=early + S["shut"])
        mm([(pr("z"), IH, sub(S["sc"], 15, 16 * L, 16)), (pr("z"), BI, k1536), (pr("z"), NB, k1536)], start=False)
        if last:
            shift("z", sub(msg, 5 * L, 6 * L), pr("z"), -2048.0)
        else:
            S["z"] = sub(msg, L, 2 * L) if t == 0 else new(bf, L)
            shift("z", S["z"], pr("z"))
        if t:
            R, F = names_tails(S["rf"])
            mm([(pr("A", 0, 4, i, 2), NI, S["hi"]) for i in range(2)]
               + [(pr("A", 2 * b, 2 * b + 2, i, 2), I1, (R, F)[i]) for b in range(2) for i in range(2)])
            S["q"] = sub(msg, 0, 4 * L) if last else new(fh, 4 * L)
            tt(S["q"], S["tmp"], pr("A", 0, 4), A.max)
        if t == 0:
            un = ps(b3, 4 * L, 8 * L)
            if c == 0:
                for i, b in enumerate((b1, b2)):
                    dealt(ps(b, 0, 2 * IW), (2 * i, 2 * i + 1), False)
                    scopy(sub(SB, 2 * IW * i, 2 * IW * (i + 1)), ps(b, 0, 2 * IW))
                make_names(1, b2)
                thresholds(b1, [1, 2, 3, 4])
            ship(msg, L, ps(b3, 0, 3 * L), lambda r, k: (r + k) % NR,
                 lambda r, k, a: (int(a < 3) - k) % NR, cp)(un, (0, 1, 2, 3))
            rest = new(bf, 3 * L)
            scopy(rest, sub(un, L, 4 * L)); cp(G, sub(un, 0, L))
            S["z"], S["cn"], S["par"] = [sub(rest, i * L, (i + 1) * L) for i in range(3)]
            S["q"] = sub(SB, 4 * L * c, 4 * L * (c + 1))
        if last:
            w = 6 * L // 4
            unpack = ship(msg, w, ps(b3, 0, 3 * w), lambda r, k: k, lambda r, k, a: (r - k) % NR, cp)
            unpack(ps(b1, 0, 2 * w), (0, 1)); unpack(ps(b2, 0, 2 * w), (2, 3))
            o = new(f32, 6 * L)
            shift("out", sub(o, 0, 2 * w), ps(b1, 0, 2 * w), 2048.0)
            ts(sub(o, 2 * w, 4 * w), ps(b2, 0, 2 * w), 2048.0, A.add)
            for b in range(2):
                store("ys"[b], "yq", 2 * (LN * b + L * c), 2 * (LN * b + L * c + L), sub(o, 2 * L * b, 2 * L * (b + 1)))
            store("y", "yg", L * c, L * c + L, sub(o, 4 * L, 5 * L)); store("s", "yz", L * c, L * c + L, sub(o, 5 * L, 6 * L))

    for t in range(NV):
        for c in range(NCH):
            cur[:] = [c, c + NCH * (0 if t == 0 else 2 if t == NV - 1 else 1), 0]
            visit(c, t)

    return ops, sems, top


def link(ops):
    hist = {}
    for i, o in enumerate(ops):
        dep = set(o.get("after", ()))
        acc = [(False, v) for v in o["rd"]] + [(True, v) for v in o["wr"]]
        for isw, v in acc:
            for (j, w, a, b) in hist.get(v[0], ()):
                if (w or isw) and a < v[2] and v[1] < b:
                    dep.add(j)
        for isw, v in acc:
            h = hist.setdefault(v[0], [])
            if isw and v[3] == 1:
                h[:] = [e for e in h if not (v[1] <= e[2] and e[3] <= v[2])]
            h.append((i, isw, v[1], v[2]))
        dep.discard(i)
        o["dep"] = dep
        o["banks"] = sorted({v[0] for v in o["rd"] + o["wr"] if v[0].startswith("ps")})
    anc, opened, starts = [], {}, {}
    for i, o in enumerate(ops):
        a = 0
        for j in o["dep"]:
            a |= anc[j] | 1 << j
        anc.append(a)
        if o["eng"] == "pe" and o["start"]:
            starts.setdefault(o["bank"], []).append(i)
        if o["eng"] == "pe" and o["start"] and not o["stop"]:
            opened[o["bank"]] = i
        elif o["eng"] == "pe" and o["stop"] and not o["start"]:
            k = opened.pop(o["bank"])
            ops[k]["dep"] |= {j for j in starts[o["bank"]] if j != k and a >> j & 1 and not anc[k] >> j & 1}
    for o in ops:
        o["dep"] = sorted(o["dep"])


def schedule(ops, P, seed, given=None):
    n = len(ops)
    succ = [[] for _ in range(n)]
    for i, o in enumerate(ops):
        for j in o["dep"]:
            succ[j].append(i)
    lam = P["lam"]
    left = [len(o["dep"]) for o in ops]
    topo_order = [i for i in range(n) if not left[i]]
    cnt = list(left)
    for i in topo_order:
        for j in succ[i]:
            cnt[j] -= 1
            if not cnt[j]:
                topo_order.append(j)
    rank = [0.0] * n
    for i in reversed(topo_order):
        rank[i] = ops[i]["cost"] + ops[i].get("lat", 0) + lam + max([rank[j] for j in succ[i]], default=0)
    pri = []
    for i, o in enumerate(ops):
        seed = (seed * 1103515245 + 12345) % 2 ** 31
        pri.append(rank[i] + (P["bias"] + (0,))[o["ch"]] + P.get("jit", 0) * seed / 2 ** 31 + P.get("prio", {}).get(o["key"], 0))
    if given:
        pri = [p - r + x for p, r, x in zip(pri, rank, given)]
    ready, fin = [o.get("pre", 0.0) for o in ops], [0.0] * n
    pool = {e: [] for e in ("v", "s", "pe", "g", "y")}
    for i in range(n):
        if not left[i]:
            pool[ops[i]["eng"]].append(i)
    free = {e: 0.0 for e in pool}
    order = {e: [] for e in pool}
    seq, deps, touch, shut = [], [None] * n, {}, set()

    def when(i):
        o = ops[i]
        if o.get("start") and o["bank"] in shut:
            return None
        t = ready[i]
        for b in o["banks"]:
            for e, j in touch.get(b, {}).items():
                if e != o["eng"] and fin[j] + lam > t:
                    t = fin[j] + lam
        return t
    while len(seq) < n:
        best = None
        for e, q in pool.items():
            cand = [(t, i) for t, i in ((when(i), i) for i in q) if t is not None]
            if cand:
                t0 = max(free[e], min(cand)[0])
                if best is None or t0 < best[0]:
                    best = (t0, e, cand)
        t0, e, cand = best
        t1, i = max(((t, i) for t, i in cand if t <= t0 + P["look"]), key=lambda x: pri[x[1]] - P["gam"] * max(0, x[0] - t0))
        if t1 > t0:
            fit = [j for t, j in cand if t <= t0 and ops[j]["cost"] <= t1 - t0 + P["fit"]]
            if fit:
                i = max(fit, key=lambda j: pri[j])
            else:
                t0 = t1
        o = ops[i]
        deps[i] = set(o["dep"])
        for b in o["banks"]:
            deps[i] |= {j for e2, j in touch.get(b, {}).items() if e2 != e}
            touch.setdefault(b, {})[e] = i
        if e == "pe":
            if not o["stop"]:
                shut.add(o["bank"])
            elif not o["start"]:
                shut.discard(o["bank"])
        pool[e].remove(i); order[e].append(i); seq.append(i)
        free[e] = t0 + o["cost"]
        fin[i] = free[e] + o.get("lat", 0)
        for j in succ[i]:
            ready[j] = max(ready[j], fin[i] + ops[j].get("pre", 0) + (0 if e == "pe" and ops[j]["eng"] == "pe" else lam))
            left[j] -= 1
            if not left[j]:
                pool[ops[j]["eng"]].append(j)
    return max(fin), order, seq, deps, fin


def replay(ops, lam, seq, deps):
    fin, free = {}, {}
    for i in seq:
        o = ops[i]
        t = max([free.get(o["eng"], 0)] + [fin[j] + (0 if o["eng"] == ops[j]["eng"] == "pe" else lam) for j in deps[i]])
        free[o["eng"]] = t + o["cost"]
        fin[i] = t + o["cost"] + o.get("lat", 0)
    return max(fin.values())


def mirror(ops, deps):
    back = [dict(o, dep=[], lat=0, pre=o.get("lat", 0), start=o.get("stop"), stop=o.get("start")) for o in ops]
    for i in range(len(ops)):
        for j in deps[i]:
            back[j]["dep"].append(i)
    return back


def plan(P):
    ops, sems, top = build(P)
    link(ops)
    back = mirror(ops, [o["dep"] for o in ops])
    others = [(build(dict(P, **m))[0], m["lam"]) for m in P["also"]]

    def worth(x):
        return x[0] + sum(replay(o, lam, x[2], x[3]) for o, lam in others)
    best = last = schedule(ops, P, 1)
    mark = worth(best)
    Q = dict(P, bias=(0, 0), jit=P["jit_"])
    for seed in range(P["tries"]):
        if seed % P["again"] == 0:
            last = best
        last = schedule(ops, Q, seed + P["seed"], schedule(back, Q, seed + P["seed"], last[4])[4])
        if last[0] < best[0] * 1.01 and worth(last) < mark:
            best, mark = last, worth(last)
    return (ops, sems, top) + best


OPS, DSEMS, TOP, SPAN, ORDER, SEQ, DEPS, FIN = plan(P)
SCRATCH = {ARENA[k]: ("sbuf", [128, TOP[k]], k) for k in ARENA}
SCRATCH["tb"] = ("sbuf", [128, W + 16], "bfloat16")
SCRATCH["t2"] = ("sbuf", [128, W + 16], "bfloat16")
SCRATCH["sx"] = ("dram", [NR - 1, 128, W // NR], "bfloat16")
SCRATCH["lx"] = ("dram", [NR - 1, 128, W // NR], "bfloat16")
for _b in range(8):
    SCRATCH["ps%d" % _b] = ("psum", [128, 512], "float32")
SEMAPHORES = ["cv", "cs", "cpe", "cg", "sent"] + DSEMS


def rank_program(g, core, T, topo):
    rank = T.rank_of(core)
    if rank is None:
        return
    queue = {"v": g.vector, "s": g.scalar, "pe": g.tensor, "g": g, "y": g.sync}
    peer = lambda step: T.cores[(rank + step) % NR]

    def split(src, dst, k):
        eng = topo.engines(src, dst)
        per = 1
        while 2 * per * k <= len(eng):
            per *= 2
        return [eng[i * per:(i + 1) * per] for i in range(k)]

    mark, total = {}, {}
    for e, lst in ORDER.items():
        for i in lst:
            o = OPS[i]
            if "items" in o:
                its = o["items"]
                mark[i] = (o["sem"], sum(len(split(peer(-s), core, len(its))[k]) for k, (_, _, s) in enumerate(its)))
            elif "sem" in o:
                mark[i] = (o["sem"], 16)
            else:
                total["c" + e] = total.get("c" + e, 0) + 1
                mark[i] = ("c" + e, total["c" + e])
    pos = {i: n for n, i in enumerate(SEQ)}
    waits, known, seen = {}, {}, {e: {} for e in ORDER}
    for i in SEQ:
        o, sn = OPS[i], seen[OPS[i]["eng"]]
        waits[i] = []
        for j in sorted(DEPS[i], key=lambda j: -pos[j]):
            s, v = mark[j]
            if (o["eng"] == "pe" and OPS[j]["eng"] == "pe") or sn.get(s, 0) >= v:
                continue
            waits[i].append((s, v)); sn[s] = v
            for s2, v2 in known[j].items():
                sn[s2] = max(sn.get(s2, 0), v2)
        known[i] = {} if "items" in o else dict(sn)
    sent, waited = 0, set()
    for e, lst in ORDER.items():
        q = queue[e]
        for i in lst:
            o = OPS[i]
            for s, v in waits[i]:
                q.wait_ge(T.sem[s], v); waited.add((s, v))
            if "items" in o:
                its, tr = o["items"], []
                for k, (src, dst, step) in enumerate(its):
                    d = peer(step)
                    rid, pid = topo.addr(d, core)
                    eng = split(core, d, len(its))[k]
                    tr.append(RemoteDMATransfer(dst_ids=[DstId(rid=rid, pnc=pid)], dma_engine_mask=sum(1 << x for x in eng),
                                                remote_sem=T.sem[o["sem"]], src=src(T), dst=dst(T)))
                    sent += len(eng)
                g.remote_dma_fused(tr, local_sem=T.sem.sent)
            else:
                o["fn"](g, T, rank).then_inc(T.sem[mark[i][0]], 16 if "sem" in o else 1)
    g.wait_ge(T.sem.sent, sent)
    for s, v in list(total.items()) + [m for i, m in mark.items() if "sem" in OPS[i]]:
        if (s, v) not in waited:
            g.wait_ge(T.sem[s], v)
